import numpy as np
import ml_dtypes


def mxq(x, axis, fmt="e4m3"):
    dtype, down = {"e4m3": (ml_dtypes.float8_e4m3fn, 7), "e5m2": (ml_dtypes.float8_e5m2, 14)}[fmt]
    v = np.moveaxis(np.asarray(x, np.float32).astype(ml_dtypes.bfloat16).astype(np.float64), axis, -1)
    blocks = v.reshape(v.shape[:-1] + (-1, 32))
    amax = np.abs(blocks).max(-1, keepdims=True)
    byte = np.maximum(np.where(amax > 0, np.frexp(amax)[1] - 1 + 127, 0) - down, 1)
    scale = np.exp2(byte - 127.0)
    codes = (blocks / scale).astype(np.float32).astype(dtype).astype(np.float64)
    return np.moveaxis((codes * scale).reshape(v.shape), -1, axis)


WIDE = False


def mx_kscale(k):
    if not WIDE:
        return np.ones(k)
    levels = np.array([10, -10, 5, -5, 0])
    if k % 512:
        return np.exp2(np.random.permutation(np.resize(levels, k // 32))).repeat(32)
    a = np.empty((k // 512, 16))
    for p in range(k // 512):
        a[p, :8] = np.random.permutation(np.resize(levels, 8))
        for g in range(8):
            far = levels[np.abs(levels - a[p, g]) >= 10]
            a[p, g + 8] = far[np.random.randint(len(far))]
    return np.exp2(a.ravel()).repeat(32)


def f64(x):
    return np.asarray(x).astype(np.float64)


def striped(idx):
    return np.tile(idx.reshape(-1, 16).T, (8, 1)).astype(np.uint16)


def unstriped(offs):
    return offs[:16].T.reshape(-1).astype(np.int64)


def pack_weight(w):
    k, n = w.shape
    w = f64(np.asarray(w, np.float32).astype(ml_dtypes.bfloat16)).reshape(k // 32, 32, n)
    amax = np.abs(w).max(1)
    byte = np.clip(np.where(amax > 0, np.frexp(amax)[1] - 1 + 127 - 7, 1), 1, 254)
    scaled = (w * np.exp2(127.0 - byte)[:, None, :]).reshape(k, n).astype(np.float32)
    words = np.ascontiguousarray(scaled.reshape(k // 512, 128, 4, n).transpose(0, 1, 3, 2)).astype(ml_dtypes.float8_e4m3fn).view(np.uint8)
    return words, np.ascontiguousarray(byte.astype(np.uint8).reshape(k // 512, 16, n))


def unpack_weight(words, scales):
    g, p, n, _ = words.shape
    vals = np.ascontiguousarray(words).view(ml_dtypes.float8_e4m3fn).astype(np.float64) * np.repeat(np.exp2(scales.astype(np.float64) - 127.0), 8, axis=1)[..., None]
    return vals.transpose(0, 1, 3, 2).reshape(g * 512, n)


def relu(v):
    return np.maximum(v, 0.0)


K, T, S, D, H, N = 512, 2048, 512, 8, 512, 128


def setup_inputs():
    n = np.random.standard_normal
    s = mx_kscale(K)[:, None]
    u = mx_kscale(H)
    packed_xT = pack_weight(n((K, T)) * s)
    return {
        "x_words": packed_xT[0],
        "x_scales": packed_xT[1],
        "wc": (n((K, H)) / np.sqrt(K) / s).astype(np.float32),
        "ws": (n((K, H)) / np.sqrt(K) / s).astype(np.float32),
        "unit": (np.random.uniform(0.5, 1.0, (H, 1)) * u[:, None]).astype(np.float32),
        "vc": (n((H, N)) / np.sqrt(2 * H) / u[:, None]).astype(np.float32),
        "vs": (n((H, N)) / np.sqrt(2 * H) / u[:, None]).astype(np.float32),
        "offs": striped(np.random.permutation(T)[:S]),
    }


def reference(x_words, x_scales, wc, ws, unit, vc, vs, offs):
    xq = unpack_weight(x_words, x_scales)[:, unstriped(offs)]
    re = mxq(f64(wc), 0, "e4m3").T @ xq
    im = mxq(f64(ws), 0, "e4m3").T @ xq
    pw = (re) ** 2 + (im) ** 2
    nf = 1.5 * (pw.reshape(len(pw), -1, D).min(axis=2))
    gain = np.sqrt(relu(-1.0 * (np.repeat(nf, D, axis=1) / (pw + 0.05)) + 1.0) + 0.02)
    zvc = f64(unit) * (gain * re)
    zvs = f64(unit) * (gain * im)
    return mxq(f64(vc), 0, "e4m3").T @ mxq(zvc, 0, "e4m3") + mxq(f64(vs), 0, "e4m3").T @ mxq(zvs, 0, "e4m3")

@@ -1,0 +1,189 @@
+from contextlib import ExitStack
+
+import concourse.mybir as mybir
+
+F32 = mybir.dt.float32
+BF16 = mybir.dt.bfloat16
+I32 = mybir.dt.int32
+U32 = mybir.dt.uint32
+U16 = mybir.dt.uint16
+U8 = mybir.dt.uint8
+FP8X4 = mybir.dt.float8_e4m3fn_x4
+ALU = mybir.AluOpType
+ACT = mybir.ActivationFunctionType
+AX = mybir.AxisListType
+
+P = 128
+PACK = 4
+K, T, S, D, H, N = 512, 2048, 512, 8, 512, 128
+CHUNK = 128
+CHUNKS = S // CHUNK
+HALF = 2 * CHUNK
+WCOLS = H // 2
+FLOPS = 2 * (2 * K * H * S + 2 * H * N * S)
+
+
+def tile_picked_ysubtr_sub_p_kernel(tc, x_words, x_scales, wc, ws, unit, vc, vs, offs, out):
+    nc = tc.nc
+    with ExitStack() as ctx:
+        keep = ctx.enter_context(tc.tile_pool(name="keep", bufs=1))
+        psum = ctx.enter_context(tc.psum_pool(name="psum", bufs=1))
+
+        def sb(name, shape, dtype):
+            return keep.tile(shape, dtype, name=name, align_bytes=64)
+
+        offsets = keep.tile([P, S // 16], U16, name="offsets")
+        nc.sync.dma_start(offsets[:], offs)
+        wc_raw = keep.tile([P, PACK, H], F32, name="wc_raw", tag="raw", align_bytes=64)
+        nc.sync.dma_start(out=wc_raw[:], in_=wc.rearrange("(p j) c -> p j c", j=PACK))
+        bytes_all = sb("bytes_all", [P, T], U8)
+        nc.vector.memset(bytes_all[:].bitcast(I32), 0)
+        for quad in range(4):
+            nc.scalar.dma_start(out=bytes_all[32 * quad:32 * quad + 4, :].bitcast(I32), in_=x_scales[0, 4 * quad:4 * quad + 4, :].bitcast(I32))
+        words = sb("words", [P, T], I32)
+        nc.sync.dma_start(out=words[:], in_=x_words[0].rearrange("p n t -> p (n t)").bitcast(I32))
+        ws_raw = []
+        for h in range(2):
+            raw = sb("ws_raw%d" % h, [P, PACK, WCOLS], F32)
+            nc.sync.dma_start(out=raw[:], in_=ws.rearrange("(p j) c -> p j c", j=PACK)[:, :, h * WCOLS:(h + 1) * WCOLS])
+            ws_raw.append(raw)
+        u = sb("u", [P, PACK], F32)
+        nc.scalar.dma_start(out=u[:], in_=unit.rearrange("(p t) o -> p (t o)", t=PACK))
+
+        one = sb("one", [P, 1], F32)
+        nc.vector.memset(one[:], 1.0)
+        warm = sb("warm", [P, 1], F32)
+        nc.scalar.activation(warm[:], one[:], ACT.Abs_reciprocal_sqrt)
+
+        def cast_w(raw, grouped):
+            nc.vector.tensor_copy(out=grouped.rearrange("p t m j -> p m j t"), in_=raw[:].rearrange("p j (m t) -> p m j t", t=PACK))
+
+        wc_bf = sb("wc_bf", [P, PACK, P, PACK], BF16)
+        x_bytes = sb("x_bytes", [P, S], U8)
+        nc.vector.tensor_copy(x_bytes[:], bytes_all[:].indirect(offsets[:]))
+        cast_w(wc_raw, wc_bf[:])
+        v_raw = keep.tile([P, 2, PACK, N], F32, name="v_raw", tag="raw", align_bytes=64)
+        for a, v in enumerate((vc, vs)):
+            nc.sync.dma_start(out=v_raw[:, a, :, :], in_=v.rearrange("(p j) m -> p j m", j=PACK))
+        wc_codes = sb("wc_codes", [P, H], U32)
+        wc_scales = sb("wc_scales", [P, H], U8)
+        nc.vector.quantize_mx(out=wc_codes[:].bitcast(FP8X4), scales=wc_scales[:], in_=wc_bf[:].rearrange("p t m j -> p (t m j)"))
+
+        x_codes = []
+        for h in range(2):
+            g = sb("x_codes%d" % h, [P, HALF], U32)
+            nc.vector.tensor_copy(g[:], words[:].bitcast(U32).indirect(offsets[:, h * HALF // 16:(h + 1) * HALF // 16]))
+            x_codes.append(g)
+
+        def first_product(tag, codes, scales, c):
+            bank = psum.tile([P, PACK, CHUNK], F32, name="%s%d" % (tag, c), tag="%s%d" % (tag, c))
+            cols = slice((c % 2) * CHUNK, (c % 2 + 1) * CHUNK)
+            for t in range(PACK):
+                nc.tensor.matmul_mx(out=bank[:, t, :], lhsT=codes[:, t * P:(t + 1) * P].bitcast(FP8X4), lhsT_scale=scales[:, t * P:(t + 1) * P],
+                                    rhs=x_codes[c // 2][:, cols].bitcast(FP8X4), rhs_scale=x_bytes[:, c * CHUNK:(c + 1) * CHUNK], start=True, stop=True)
+            return bank
+
+        re = [first_product("re", wc_codes, wc_scales, c) for c in range(CHUNKS)]
+        re_sq = []
+        for c in range(CHUNKS):
+            sq = sb("re_sq%d" % c, [P, PACK, CHUNK], F32)
+            nc.scalar.activation(sq[:], re[c][:], ACT.Square)
+            re_sq.append(sq)
+
+        ws_codes = sb("ws_codes", [P, H], U32)
+        ws_scales = sb("ws_scales", [P, H], U8)
+        for h in range(2):
+            ws_bf = sb("ws_bf%d" % h, [P, PACK, 64, PACK], BF16)
+            cast_w(ws_raw[h], ws_bf[:])
+            for t in range(PACK):
+                cols = slice(t * P + 64 * h, t * P + 64 * h + 64)
+                nc.vector.quantize_mx(out=ws_codes[:, cols].bitcast(FP8X4), scales=ws_scales[:, cols], in_=ws_bf[:, t, :, :].rearrange("p m j -> p (m j)"))
+
+        u_sign = sb("u_sign", [P, PACK], F32)
+        nc.scalar.activation(u_sign[:], u[:], ACT.Sign)
+        u2 = sb("u2", [P, PACK], F32)
+        nc.vector.tensor_tensor(u2[:], u[:], u[:], ALU.mult)
+        u2_noise = sb("u2_noise", [P, PACK], F32)
+        nc.vector.tensor_scalar(u2_noise[:], u2[:], 1.5, None, ALU.mult)
+        u2_top = sb("u2_top", [P, PACK], F32)
+        nc.vector.tensor_scalar(u2_top[:], u2[:], 1.02, None, ALU.mult)
+
+        im = [first_product("im", ws_codes, ws_scales, c) for c in range(CHUNKS)]
+
+        den = []
+        for c in range(CHUNKS):
+            sq = sb("im_sq%d" % c, [P, PACK, CHUNK], F32)
+            nc.scalar.activation(sq[:], im[c][:], ACT.Square)
+            d = sb("den%d" % c, [P, PACK, CHUNK], F32)
+            nc.vector.scalar_tensor_tensor(d[:], re_sq[c][:], 0.05, sq[:], ALU.add, ALU.add)
+            den.append(d)
+
+        groups = CHUNK // D
+        inv, least = [], []
+        for c in range(CHUNKS):
+            rs = sb("rs%d" % c, [P, PACK, CHUNK], F32)
+            nc.scalar.activation(rs[:], den[c][:], ACT.Abs_reciprocal_sqrt)
+            r = sb("inv%d" % c, [P, PACK, CHUNK], F32)
+            nc.scalar.activation(r[:], rs[:], ACT.Square)
+            inv.append(r)
+            m = sb("least%d" % c, [P, PACK, groups], F32)
+            nc.vector.tensor_reduce(m[:], den[c][:].rearrange("p t (v d) -> p t v d", d=D), AX.X, ALU.min)
+            least.append(m)
+
+        noise = []
+        for c in range(CHUNKS):
+            nf = sb("noise%d" % c, [P, PACK, groups], F32)
+            nc.vector.scalar_tensor_tensor(nf[:], least[c][:], -0.05, u2_noise[:].unsqueeze(2).to_broadcast([P, PACK, groups]), ALU.add, ALU.mult)
+            noise.append(nf)
+
+        neg_gain2 = []
+        for h in range(2):
+            q = sb("ratio%d" % h, [P, PACK, HALF], F32)
+            for c in (2 * h, 2 * h + 1):
+                cols = slice((c % 2) * CHUNK, (c % 2 + 1) * CHUNK)
+                nc.vector.tensor_tensor(q[:, :, cols].rearrange("p t (v d) -> p t v d", d=D), inv[c][:].rearrange("p t (v d) -> p t v d", d=D),
+                                        noise[c][:].unsqueeze(3).to_broadcast([P, PACK, groups, D]), ALU.mult)
+            y = sb("neg_gain2_%d" % h, [P, PACK, HALF], F32)
+            for t in range(PACK):
+                nc.vector.tensor_scalar(y[:, t, :], q[:, t, :], u2[:, t:t + 1], u2_top[:, t:t + 1], ALU.min, ALU.subtract)
+            neg_gain2.append(y)
+
+        v_bf = sb("v_bf", [P, 2, N, PACK], BF16)
+        for a in range(2):
+            nc.vector.tensor_tensor(v_bf[:, a, :, :], v_raw[:, a, :, :].rearrange("p j m -> p m j"), u_sign[:].unsqueeze(1).to_broadcast([P, N, PACK]), ALU.mult)
+        v_codes = sb("v_codes", [P, 2 * N], U32)
+        v_scales = sb("v_scales", [P, 2 * N], U8)
+        nc.vector.quantize_mx(out=v_codes[:].bitcast(FP8X4), scales=v_scales[:], in_=v_bf[:].rearrange("p a m j -> p (a m j)"))
+
+        gain = []
+        for c in range(CHUNKS):
+            cols = slice((c % 2) * CHUNK, (c % 2 + 1) * CHUNK)
+            g = sb("gain%d" % c, [P, CHUNK, PACK], F32)
+            nc.scalar.activation(g[:], neg_gain2[c // 2][:, :, cols].rearrange("p t n -> p n t"), ACT.Sqrt, scale=-1.0)
+            gain.append(g)
+
+        z = [sb("z%d" % c, [P, 2, CHUNK, PACK], BF16) for c in range(CHUNKS)]
+
+        def weigh(c, a):
+            bank = (re, im)[a][c]
+            nc.vector.tensor_tensor(z[c][:, a, :, :], bank[:].rearrange("p t n -> p n t"), gain[c][:], ALU.mult)
+
+        def second_product(c):
+            z_codes = sb("z_codes%d" % c, [P, 2 * CHUNK], U32)
+            z_scales = sb("z_scales%d" % c, [P, 2 * CHUNK], U8)
+            nc.vector.quantize_mx(out=z_codes[:].bitcast(FP8X4), scales=z_scales[:], in_=z[c][:].rearrange("p a n t -> p (a n t)"))
+            acc = psum.tile([P, CHUNK], F32, name="acc%d" % c, tag="re%d" % c)
+            for a in range(2):
+                nc.tensor.matmul_mx(out=acc[:], lhsT=v_codes[:, a * N:(a + 1) * N].bitcast(FP8X4), lhsT_scale=v_scales[:, a * N:(a + 1) * N],
+                                    rhs=z_codes[:, a * CHUNK:(a + 1) * CHUNK].bitcast(FP8X4), rhs_scale=z_scales[:, a * CHUNK:(a + 1) * CHUNK],
+                                    start=(a == 0), stop=(a == 1))
+            result = sb("result%d" % c, [P, CHUNK], F32)
+            nc.scalar.copy(result[:], acc[:])
+            nc.sync.dma_start(out=out[:, c * CHUNK:(c + 1) * CHUNK], in_=result[:])
+
+        for c in range(CHUNKS):
+            weigh(c, 0)
+            if c > 0:
+                second_product(c - 1)
+            weigh(c, 1)
+        second_product(CHUNKS - 1)

@@ -33,39 +33,54 @@ def tile_picked_ysubtr_sub_p_kernel(tc, x_words, x_scales, wc, ws, unit, vc, vs,
             return keep.tile(shape, dtype, name=name, align_bytes=64)
 
         offsets = keep.tile([P, S // 16], U16, name="offsets")
-        nc.sync.dma_start(offsets[:], offs)
-        wc_raw = keep.tile([P, PACK, H], F32, name="wc_raw", tag="raw", align_bytes=64)
+
+        def load_half(name, w, h):
+            raw = sb("%s_raw%d" % (name, h), [P, PACK, WCOLS], F32)
+            nc.sync.dma_start(out=raw[:], in_=w.rearrange("(p j) c -> p j c", j=PACK)[:, :, h * WCOLS:(h + 1) * WCOLS])
+            return raw
+
+        wc_raw = sb("wc_raw", [P, PACK, H], F32)
         nc.sync.dma_start(out=wc_raw[:], in_=wc.rearrange("(p j) c -> p j c", j=PACK))
-        bytes_all = sb("bytes_all", [P, T], U8)
+        nc.sync.dma_start(offsets[:], offs)
+        bytes_all = keep.tile([P, T], U8, name="bytes_all", tag="bytes_all", align_bytes=64)
         nc.vector.memset(bytes_all[:].bitcast(I32), 0)
         for quad in range(4):
-            nc.scalar.dma_start(out=bytes_all[32 * quad:32 * quad + 4, :].bitcast(I32), in_=x_scales[0, 4 * quad:4 * quad + 4, :].bitcast(I32))
+            nc.sync.dma_start(out=bytes_all[32 * quad:32 * quad + 4, :].bitcast(I32), in_=x_scales[0, 4 * quad:4 * quad + 4, :].bitcast(I32))
         words = sb("words", [P, T], I32)
         nc.sync.dma_start(out=words[:], in_=x_words[0].rearrange("p n t -> p (n t)").bitcast(I32))
-        ws_raw = []
-        for h in range(2):
-            raw = sb("ws_raw%d" % h, [P, PACK, WCOLS], F32)
-            nc.sync.dma_start(out=raw[:], in_=ws.rearrange("(p j) c -> p j c", j=PACK)[:, :, h * WCOLS:(h + 1) * WCOLS])
-            ws_raw.append(raw)
-        u = sb("u", [P, PACK], F32)
-        nc.scalar.dma_start(out=u[:], in_=unit.rearrange("(p t) o -> p (t o)", t=PACK))
+        u_rows = sb("u_rows", [P, 8], F32)
+        for e in range(2):
+            nc.sync.dma_start(out=u_rows[e:P:2, 0:7], in_=unit.rearrange("(a r) o -> a (r o)", r=8)[:, e:e + 7])
+        u = u_rows[:, 0:8:2]
+        ws_raw = [load_half("ws", ws, h) for h in range(2)]
+        v_raw = sb("v_raw", [P, 2, PACK, N], F32)
+        for a, v in enumerate((vc, vs)):
+            for e in range(2):
+                nc.sync.dma_start(out=v_raw[e:P:2, a, :, :], in_=v.rearrange("(a t e) m -> e a t m", t=PACK, e=2)[e])
 
         one = sb("one", [P, 1], F32)
         nc.vector.memset(one[:], 1.0)
         warm = sb("warm", [P, 1], F32)
         nc.scalar.activation(warm[:], one[:], ACT.Abs_reciprocal_sqrt)
 
-        def cast_w(raw, grouped):
-            nc.vector.tensor_copy(out=grouped.rearrange("p t m j -> p m j t"), in_=raw[:].rearrange("p j (m t) -> p m j t", t=PACK))
+        u_sign = sb("u_sign", [P, PACK], F32)
+        nc.scalar.activation(u_sign[:], u, ACT.Sign)
+        u2 = sb("u2", [P, PACK], F32)
+        nc.scalar.activation(u2[:], u, ACT.Square)
+        u2_noise = sb("u2_noise", [P, PACK], F32)
+        nc.scalar.activation(u2_noise[:], u2[:], ACT.Copy, scale=1.5)
+        u2_top = sb("u2_top", [P, PACK], F32)
+        nc.scalar.activation(u2_top[:], u2[:], ACT.Copy, scale=1.02)
+
+        def cast_w(copy, raw, grouped):
+            copy(grouped.rearrange("p t (a e) j -> p t a j e", e=2), raw.rearrange("p j (a t e) -> p t a j e", t=PACK, e=2))
 
         wc_bf = sb("wc_bf", [P, PACK, P, PACK], BF16)
+        cast_w(nc.scalar.copy, wc_raw[:, :, 0:320], wc_bf[:, :, 0:80, :])
         x_bytes = sb("x_bytes", [P, S], U8)
         nc.vector.tensor_copy(x_bytes[:], bytes_all[:].indirect(offsets[:]))
-        cast_w(wc_raw, wc_bf[:])
-        v_raw = keep.tile([P, 2, PACK, N], F32, name="v_raw", tag="raw", align_bytes=64)
-        for a, v in enumerate((vc, vs)):
-            nc.sync.dma_start(out=v_raw[:, a, :, :], in_=v.rearrange("(p j) m -> p j m", j=PACK))
-        wc_codes = sb("wc_codes", [P, H], U32)
+        cast_w(nc.vector.tensor_copy, wc_raw[:, :, 320:H], wc_bf[:, :, 80:128, :])
+        wc_codes = keep.tile([P, H], U32, name="wc_codes", tag="bytes_all", align_bytes=64)
         wc_scales = sb("wc_scales", [P, H], U8)
         nc.vector.quantize_mx(out=wc_codes[:].bitcast(FP8X4), scales=wc_scales[:], in_=wc_bf[:].rearrange("p t m j -> p (t m j)"))
 
@@ -94,96 +109,89 @@ def tile_picked_ysubtr_sub_p_kernel(tc, x_words, x_scales, wc, ws, unit, vc, vs,
         ws_scales = sb("ws_scales", [P, H], U8)
         for h in range(2):
             ws_bf = sb("ws_bf%d" % h, [P, PACK, 64, PACK], BF16)
-            cast_w(ws_raw[h], ws_bf[:])
+            cast_w(nc.vector.tensor_copy, ws_raw[h][:], ws_bf[:])
             for t in range(PACK):
                 cols = slice(t * P + 64 * h, t * P + 64 * h + 64)
                 nc.vector.quantize_mx(out=ws_codes[:, cols].bitcast(FP8X4), scales=ws_scales[:, cols], in_=ws_bf[:, t, :, :].rearrange("p m j -> p (m j)"))
 
-        u_sign = sb("u_sign", [P, PACK], F32)
-        nc.scalar.activation(u_sign[:], u[:], ACT.Sign)
-        u2 = sb("u2", [P, PACK], F32)
-        nc.vector.tensor_tensor(u2[:], u[:], u[:], ALU.mult)
-        u2_noise = sb("u2_noise", [P, PACK], F32)
-        nc.vector.tensor_scalar(u2_noise[:], u2[:], 1.5, None, ALU.mult)
-        u2_top = sb("u2_top", [P, PACK], F32)
-        nc.vector.tensor_scalar(u2_top[:], u2[:], 1.02, None, ALU.mult)
-
         im = [first_product("im", ws_codes, ws_scales, c) for c in range(CHUNKS)]
 
-        den = []
+        den = [sb("den%d" % h, [P, PACK, HALF], F32) for h in range(2)]
         for c in range(CHUNKS):
             sq = sb("im_sq%d" % c, [P, PACK, CHUNK], F32)
             nc.scalar.activation(sq[:], im[c][:], ACT.Square)
-            d = sb("den%d" % c, [P, PACK, CHUNK], F32)
-            nc.vector.scalar_tensor_tensor(d[:], re_sq[c][:], 0.05, sq[:], ALU.add, ALU.add)
-            den.append(d)
+            cols = slice((c % 2) * CHUNK, (c % 2 + 1) * CHUNK)
+            nc.vector.scalar_tensor_tensor(den[c // 2][:, :, cols], re_sq[c][:], 0.05, sq[:], ALU.add, ALU.add)
 
-        groups = CHUNK // D
-        inv, least = [], []
-        for c in range(CHUNKS):
-            rs = sb("rs%d" % c, [P, PACK, CHUNK], F32)
-            nc.scalar.activation(rs[:], den[c][:], ACT.Abs_reciprocal_sqrt)
-            r = sb("inv%d" % c, [P, PACK, CHUNK], F32)
+        groups = HALF // D
+        inv, noise = [], []
+        for h in range(2):
+            rs = sb("rs%d" % h, [P, PACK, HALF], F32)
+            nc.scalar.activation(rs[:], den[h][:], ACT.Abs_reciprocal_sqrt)
+            r = sb("inv%d" % h, [P, PACK, HALF], F32)
             nc.scalar.activation(r[:], rs[:], ACT.Square)
             inv.append(r)
-            m = sb("least%d" % c, [P, PACK, groups], F32)
-            nc.vector.tensor_reduce(m[:], den[c][:].rearrange("p t (v d) -> p t v d", d=D), AX.X, ALU.min)
+        least = []
+        for h in range(2):
+            m = sb("least%d" % h, [P, PACK, groups], F32)
+            nc.vector.tensor_reduce(m[:], den[h][:].rearrange("p t (v d) -> p t v d", d=D), AX.X, ALU.min)
             least.append(m)
-
-        noise = []
-        for c in range(CHUNKS):
-            nf = sb("noise%d" % c, [P, PACK, groups], F32)
-            nc.vector.scalar_tensor_tensor(nf[:], least[c][:], -0.05, u2_noise[:].unsqueeze(2).to_broadcast([P, PACK, groups]), ALU.add, ALU.mult)
+        for h in range(2):
+            nf = sb("noise%d" % h, [P, PACK, groups], F32)
+            nc.vector.scalar_tensor_tensor(nf[:], least[h][:], -0.05, u2_noise[:].unsqueeze(2).to_broadcast([P, PACK, groups]), ALU.add, ALU.mult)
             noise.append(nf)
 
         neg_gain2 = []
         for h in range(2):
-            q = sb("ratio%d" % h, [P, PACK, HALF], F32)
-            for c in (2 * h, 2 * h + 1):
-                cols = slice((c % 2) * CHUNK, (c % 2 + 1) * CHUNK)
-                nc.vector.tensor_tensor(q[:, :, cols].rearrange("p t (v d) -> p t v d", d=D), inv[c][:].rearrange("p t (v d) -> p t v d", d=D),
-                                        noise[c][:].unsqueeze(3).to_broadcast([P, PACK, groups, D]), ALU.mult)
+            q = keep.tile([P, PACK, HALF], F32, name="ratio%d" % h, tag="ratio%d" % h, align_bytes=64)
+            for t in (0, 2):
+                nc.vector.tensor_tensor(q[:, t:t + 2, :].rearrange("p t (v d) -> p t v d", d=D), inv[h][:, t:t + 2, :].rearrange("p t (v d) -> p t v d", d=D),
+                                        noise[h][:, t:t + 2, :].unsqueeze(3).to_broadcast([P, 2, groups, D]), ALU.mult)
             y = sb("neg_gain2_%d" % h, [P, PACK, HALF], F32)
             for t in range(PACK):
                 nc.vector.tensor_scalar(y[:, t, :], q[:, t, :], u2[:, t:t + 1], u2_top[:, t:t + 1], ALU.min, ALU.subtract)
             neg_gain2.append(y)
 
-        v_bf = sb("v_bf", [P, 2, N, PACK], BF16)
+        v_bf = keep.tile([P, 2, N, PACK], BF16, name="v_bf", tag="ratio1", align_bytes=64)
         for a in range(2):
-            nc.vector.tensor_tensor(v_bf[:, a, :, :], v_raw[:, a, :, :].rearrange("p j m -> p m j"), u_sign[:].unsqueeze(1).to_broadcast([P, N, PACK]), ALU.mult)
-        v_codes = sb("v_codes", [P, 2 * N], U32)
-        v_scales = sb("v_scales", [P, 2 * N], U8)
-        nc.vector.quantize_mx(out=v_codes[:].bitcast(FP8X4), scales=v_scales[:], in_=v_bf[:].rearrange("p a m j -> p (a m j)"))
+            nc.gpsimd.tensor_tensor(v_bf[:, a, :, :], v_raw[:, a, :, :].rearrange("p j m -> p m j"), u_sign[:].unsqueeze(1).to_broadcast([P, N, PACK]), ALU.mult)
 
         gain = []
         for c in range(CHUNKS):
             cols = slice((c % 2) * CHUNK, (c % 2 + 1) * CHUNK)
-            g = sb("gain%d" % c, [P, CHUNK, PACK], F32)
+            g = keep.tile([P, CHUNK, PACK], F32, name="gain%d" % c, tag="gain%d" % c, align_bytes=64)
             nc.scalar.activation(g[:], neg_gain2[c // 2][:, :, cols].rearrange("p t n -> p n t"), ACT.Sqrt, scale=-1.0)
             gain.append(g)
 
-        z = [sb("z%d" % c, [P, 2, CHUNK, PACK], BF16) for c in range(CHUNKS)]
+        z = sb("z", [P, 2 * CHUNKS, CHUNK, PACK], BF16)
+        z_codes = sb("z_codes", [P, 2 * S], U32)
+        z_scales = sb("z_scales", [P, 2 * S], U8)
 
-        def weigh(c, a):
-            bank = (re, im)[a][c]
-            nc.vector.tensor_tensor(z[c][:, a, :, :], bank[:].rearrange("p t n -> p n t"), gain[c][:], ALU.mult)
+        def weigh(c):
+            for a, bank in enumerate((re[c], im[c])):
+                nc.vector.tensor_tensor(z[:, 2 * c + a, :, :], bank[:].rearrange("p t n -> p n t"), gain[c][:], ALU.mult)
 
-        def second_product(c):
-            z_codes = sb("z_codes%d" % c, [P, 2 * CHUNK], U32)
-            z_scales = sb("z_scales%d" % c, [P, 2 * CHUNK], U8)
-            nc.vector.quantize_mx(out=z_codes[:].bitcast(FP8X4), scales=z_scales[:], in_=z[c][:].rearrange("p a n t -> p (a n t)"))
+        def quantize_z(first, last):
+            cols = slice(first * CHUNK, last * CHUNK)
+            nc.vector.quantize_mx(out=z_codes[:, cols].bitcast(FP8X4), scales=z_scales[:, cols], in_=z[:, first:last, :, :].rearrange("p s n t -> p (s n t)"))
+
+        for c in range(CHUNKS - 1):
+            weigh(c)
+        quantize_z(0, 4)
+        quantize_z(4, 6)
+        v_codes = keep.tile([P, 2 * N], U32, name="v_codes", tag="gain2", align_bytes=64)
+        v_scales = sb("v_scales", [P, 2 * N], U8)
+        nc.vector.quantize_mx(out=v_codes[:].bitcast(FP8X4), scales=v_scales[:], in_=v_bf[:].rearrange("p a m j -> p (a m j)"))
+        weigh(CHUNKS - 1)
+        quantize_z(6, 7)
+        quantize_z(7, 8)
+
+        for c in range(CHUNKS):
             acc = psum.tile([P, CHUNK], F32, name="acc%d" % c, tag="re%d" % c)
             for a in range(2):
+                cols = slice((2 * c + a) * CHUNK, (2 * c + a + 1) * CHUNK)
                 nc.tensor.matmul_mx(out=acc[:], lhsT=v_codes[:, a * N:(a + 1) * N].bitcast(FP8X4), lhsT_scale=v_scales[:, a * N:(a + 1) * N],
-                                    rhs=z_codes[:, a * CHUNK:(a + 1) * CHUNK].bitcast(FP8X4), rhs_scale=z_scales[:, a * CHUNK:(a + 1) * CHUNK],
-                                    start=(a == 0), stop=(a == 1))
+                                    rhs=z_codes[:, cols].bitcast(FP8X4), rhs_scale=z_scales[:, cols], start=(a == 0), stop=(a == 1))
             result = sb("result%d" % c, [P, CHUNK], F32)
             nc.scalar.copy(result[:], acc[:])
             nc.sync.dma_start(out=out[:, c * CHUNK:(c + 1) * CHUNK], in_=result[:])
-
-        for c in range(CHUNKS):
-            weigh(c, 0)
-            if c > 0:
-                second_product(c - 1)
-            weigh(c, 1)
-        second_product(CHUNKS - 1)

@@ -44,8 +44,8 @@ def tile_picked_ysubtr_sub_p_kernel(tc, x_words, x_scales, wc, ws, unit, vc, vs,
         nc.sync.dma_start(offsets[:], offs)
         bytes_all = keep.tile([P, T], U8, name="bytes_all", tag="bytes_all", align_bytes=64)
         nc.vector.memset(bytes_all[:].bitcast(I32), 0)
-        for quad in range(4):
-            nc.sync.dma_start(out=bytes_all[32 * quad:32 * quad + 4, :].bitcast(I32), in_=x_scales[0, 4 * quad:4 * quad + 4, :].bitcast(I32))
+        for r in range(4):
+            nc.sync.dma_start(out=bytes_all[r:P:32, :].bitcast(I32), in_=x_scales[0, r:16:4, :].bitcast(I32))
         words = sb("words", [P, T], I32)
         nc.sync.dma_start(out=words[:], in_=x_words[0].rearrange("p n t -> p (n t)").bitcast(I32))
         u_rows = sb("u_rows", [P, 8], F32)
@@ -69,6 +69,8 @@ def tile_picked_ysubtr_sub_p_kernel(tc, x_words, x_scales, wc, ws, unit, vc, vs,
         nc.scalar.activation(u2[:], u, ACT.Square)
         u2_noise = sb("u2_noise", [P, PACK], F32)
         nc.scalar.activation(u2_noise[:], u2[:], ACT.Copy, scale=1.5)
+        u2_floor = sb("u2_floor", [P, PACK], F32)
+        nc.scalar.activation(u2_floor[:], u2[:], ACT.Copy, scale=0.02)
         u2_top = sb("u2_top", [P, PACK], F32)
         nc.scalar.activation(u2_top[:], u2[:], ACT.Copy, scale=1.02)
 
@@ -116,52 +118,74 @@ def tile_picked_ysubtr_sub_p_kernel(tc, x_words, x_scales, wc, ws, unit, vc, vs,
 
         im = [first_product("im", ws_codes, ws_scales, c) for c in range(CHUNKS)]
 
-        den = [sb("den%d" % h, [P, PACK, HALF], F32) for h in range(2)]
+        power = [sb("power%d" % h, [P, PACK, HALF], F32) for h in range(2)]
         for c in range(CHUNKS):
             sq = sb("im_sq%d" % c, [P, PACK, CHUNK], F32)
             nc.scalar.activation(sq[:], im[c][:], ACT.Square)
             cols = slice((c % 2) * CHUNK, (c % 2 + 1) * CHUNK)
-            nc.vector.scalar_tensor_tensor(den[c // 2][:, :, cols], re_sq[c][:], 0.05, sq[:], ALU.add, ALU.add)
+            nc.vector.tensor_tensor(power[c // 2][:, :, cols], re_sq[c][:], sq[:], ALU.add)
 
         groups = HALF // D
-        inv, noise = [], []
-        for h in range(2):
-            rs = sb("rs%d" % h, [P, PACK, HALF], F32)
-            nc.scalar.activation(rs[:], den[h][:], ACT.Abs_reciprocal_sqrt)
-            r = sb("inv%d" % h, [P, PACK, HALF], F32)
-            nc.scalar.activation(r[:], rs[:], ACT.Square)
-            inv.append(r)
-        least = []
-        for h in range(2):
-            m = sb("least%d" % h, [P, PACK, groups], F32)
-            nc.vector.tensor_reduce(m[:], den[h][:].rearrange("p t (v d) -> p t v d", d=D), AX.X, ALU.min)
-            least.append(m)
-        for h in range(2):
-            nf = sb("noise%d" % h, [P, PACK, groups], F32)
-            nc.vector.scalar_tensor_tensor(nf[:], least[h][:], -0.05, u2_noise[:].unsqueeze(2).to_broadcast([P, PACK, groups]), ALU.add, ALU.mult)
-            noise.append(nf)
+        rs = [keep.tile([P, PACK, HALF], F32, name="rs%d" % h, tag="rs%d" % h, align_bytes=64) for h in range(2)]
+        least = [sb("least%d" % h, [P, PACK, groups], F32) for h in range(2)]
 
-        neg_gain2 = []
-        for h in range(2):
-            q = keep.tile([P, PACK, HALF], F32, name="ratio%d" % h, tag="ratio%d" % h, align_bytes=64)
-            for t in (0, 2):
-                nc.vector.tensor_tensor(q[:, t:t + 2, :].rearrange("p t (v d) -> p t v d", d=D), inv[h][:, t:t + 2, :].rearrange("p t (v d) -> p t v d", d=D),
-                                        noise[h][:, t:t + 2, :].unsqueeze(3).to_broadcast([P, 2, groups, D]), ALU.mult)
-            y = sb("neg_gain2_%d" % h, [P, PACK, HALF], F32)
-            for t in range(PACK):
-                nc.vector.tensor_scalar(y[:, t, :], q[:, t, :], u2[:, t:t + 1], u2_top[:, t:t + 1], ALU.min, ALU.subtract)
-            neg_gain2.append(y)
+        def least_power(h):
+            nc.vector.tensor_reduce(least[h][:], power[h][:].rearrange("p t (v d) -> p t v d", d=D), AX.X, ALU.min)
 
-        v_bf = keep.tile([P, 2, N, PACK], BF16, name="v_bf", tag="ratio1", align_bytes=64)
+        nc.scalar.activation(rs[0][:], power[0][:], ACT.Abs_reciprocal_sqrt, bias=0.05)
+        inv = sb("inv", [P, PACK, HALF], F32)
+        nc.scalar.activation(inv[:], rs[0][:], ACT.Square)
+        nc.scalar.activation(rs[1][:], power[1][:], ACT.Abs_reciprocal_sqrt, bias=0.05)
+        least_power(0)
+        noise = sb("noise", [P, PACK, groups], F32)
+        nc.vector.tensor_tensor(noise[:], least[0][:], u2_noise[:].unsqueeze(2).to_broadcast([P, PACK, groups]), ALU.mult)
+        least_power(1)
+        noise_rs = sb("noise_rs", [P, PACK, groups], F32)
+        nc.scalar.activation(noise_rs[:], least[1][:], ACT.Abs_reciprocal_sqrt, scale=1.5, bias=1e-30)
+
+        ratio = sb("ratio", [P, PACK, HALF], F32)
+        for t in (0, 2):
+            nc.vector.tensor_tensor(ratio[:, t:t + 2, :].rearrange("p t (v d) -> p t v d", d=D), inv[:, t:t + 2, :].rearrange("p t (v d) -> p t v d", d=D),
+                                    noise[:, t:t + 2, :].unsqueeze(3).to_broadcast([P, 2, groups, D]), ALU.mult)
+        noise_root = sb("noise_root", [P, PACK, groups], F32)
+        nc.vector.scalar_tensor_tensor(noise_root[:], least[1][:], 1.5, noise_rs[:], ALU.mult, ALU.mult)
+        neg_gain2 = sb("neg_gain2", [P, PACK, HALF], F32)
+        for t in range(PACK):
+            nc.vector.tensor_scalar(neg_gain2[:, t, :], ratio[:, t, :], u2[:, t:t + 1], u2_top[:, t:t + 1], ALU.min, ALU.subtract)
+
+        root_ratio = []
+        for c in range(2):
+            w = sb("root_ratio%d" % c, [P, PACK, CHUNK], F32)
+            nc.vector.tensor_tensor(w[:].rearrange("p t (v d) -> p t v d", d=D), rs[1][:, :, c * CHUNK:(c + 1) * CHUNK].rearrange("p t (v d) -> p t v d", d=D),
+                                    noise_root[:, :, c * groups // 2:(c + 1) * groups // 2].unsqueeze(3).to_broadcast([P, PACK, groups // 2, D]), ALU.mult)
+            root_ratio.append(w)
+
+        v_bf = keep.tile([P, 2, N, PACK], BF16, name="v_bf", tag="rs1", align_bytes=64)
         for a in range(2):
             nc.gpsimd.tensor_tensor(v_bf[:, a, :, :], v_raw[:, a, :, :].rearrange("p j m -> p m j"), u_sign[:].unsqueeze(1).to_broadcast([P, N, PACK]), ALU.mult)
 
-        gain = []
-        for c in range(CHUNKS):
-            cols = slice((c % 2) * CHUNK, (c % 2 + 1) * CHUNK)
-            g = keep.tile([P, CHUNK, PACK], F32, name="gain%d" % c, tag="gain%d" % c, align_bytes=64)
-            nc.scalar.activation(g[:], neg_gain2[c // 2][:, :, cols].rearrange("p t n -> p n t"), ACT.Sqrt, scale=-1.0)
-            gain.append(g)
+        gain = [keep.tile([P, PACK * CHUNK], F32, name="gain%d" % c, tag="gain%d" % c, align_bytes=64) for c in range(CHUNKS)]
+        late_ratio = [sb("late_ratio%d" % c, [P, PACK, CHUNK], F32) for c in range(2)]
+
+        def early_gain(c):
+            nc.scalar.activation(gain[c][:].rearrange("p (b e t) -> p b t e", e=2, t=PACK),
+                                 neg_gain2[:, :, c * CHUNK:(c + 1) * CHUNK].rearrange("p t (b e) -> p b t e", e=2), ACT.Sqrt, scale=-1.0)
+
+        def square_ratio(c):
+            nc.scalar.activation(late_ratio[c][:], root_ratio[c][:], ACT.Square)
+
+        def late_gain(c):
+            kept = sb("kept%d" % c, [P, PACK, CHUNK], F32)
+            nc.scalar.activation(kept[:], late_ratio[c][:], ACT.Relu, scale=-1.0, bias=1.0)
+            for t in range(PACK):
+                nc.scalar.activation(gain[2 + c][:, t * CHUNK:(t + 1) * CHUNK], kept[:, t, :], ACT.Sqrt, scale=u2[:, t:t + 1], bias=u2_floor[:, t:t + 1])
+
+        early_gain(0)
+        square_ratio(0)
+        early_gain(1)
+        late_gain(0)
+        square_ratio(1)
+        late_gain(1)
 
         z = sb("z", [P, 2 * CHUNKS, CHUNK, PACK], BF16)
         z_codes = sb("z_codes", [P, 2 * S], U32)
@@ -169,7 +193,11 @@ def tile_picked_ysubtr_sub_p_kernel(tc, x_words, x_scales, wc, ws, unit, vc, vs,
 
         def weigh(c):
             for a, bank in enumerate((re[c], im[c])):
-                nc.vector.tensor_tensor(z[:, 2 * c + a, :, :], bank[:].rearrange("p t n -> p n t"), gain[c][:], ALU.mult)
+                if c < 2:
+                    nc.vector.tensor_tensor(z[:, 2 * c + a, :, :], bank[:].rearrange("p t n -> p n t"), gain[c][:].rearrange("p (n t) -> p n t", t=PACK), ALU.mult)
+                else:
+                    nc.vector.tensor_tensor(z[:, 2 * c + a, :, :].rearrange("p (b e) t -> p b t e", e=2), bank[:].rearrange("p t (b e) -> p b t e", e=2),
+                                            gain[c][:].rearrange("p (t b e) -> p b t e", t=PACK, e=2), ALU.mult)
 
         def quantize_z(first, last):
             cols = slice(first * CHUNK, last * CHUNK)

@@ -13,14 +13,23 @@ ALU = mybir.AluOpType
 ACT = mybir.ActivationFunctionType
 AX = mybir.AxisListType
 
+K, T, S, D, H, N = 512, 2048, 512, 8, 512, 128
+FLOPS = 2 * (2 * K * H * S + 2 * H * N * S)
+
 P = 128
 PACK = 4
-K, T, S, D, H, N = 512, 2048, 512, 8, 512, 128
+PAIR = 2
+QUADRANT = 32
 CHUNK = 128
 CHUNKS = S // CHUNK
-HALF = 2 * CHUNK
-WCOLS = H // 2
-FLOPS = 2 * (2 * K * H * S + 2 * H * N * S)
+HALF = S // 2
+PER_HALF = HALF // CHUNK
+GROUPS = HALF // D
+WS_COLS = H // 2
+WS_ROWS = P // 2
+SCALAR_ROWS = 80
+
+POWER_OFFSET, NOISE_FACTOR, GAIN_FLOOR = 0.05, 1.5, 0.02
 
 
 def tile_picked_ysubtr_sub_p_kernel(tc, x_words, x_scales, wc, ws, unit, vc, vs, offs, out):
@@ -29,75 +38,70 @@ def tile_picked_ysubtr_sub_p_kernel(tc, x_words, x_scales, wc, ws, unit, vc, vs,
         keep = ctx.enter_context(tc.tile_pool(name="keep", bufs=1))
         psum = ctx.enter_context(tc.psum_pool(name="psum", bufs=1))
 
-        def sb(name, shape, dtype):
-            return keep.tile(shape, dtype, name=name, align_bytes=64)
+        def sb(name, shape, dtype, tag=None):
+            return keep.tile(shape, dtype, name=name, tag=tag or name, align_bytes=64)
+
+        def in_half(c):
+            return slice((c % PER_HALF) * CHUNK, (c % PER_HALF + 1) * CHUNK)
+
+        def by_runs(ap):
+            return ap.rearrange("p t (v d) -> p t v d", d=D)
 
         offsets = keep.tile([P, S // 16], U16, name="offsets")
-
-        def load_half(name, w, h):
-            raw = sb("%s_raw%d" % (name, h), [P, PACK, WCOLS], F32)
-            nc.sync.dma_start(out=raw[:], in_=w.rearrange("(p j) c -> p j c", j=PACK)[:, :, h * WCOLS:(h + 1) * WCOLS])
-            return raw
-
         wc_raw = sb("wc_raw", [P, PACK, H], F32)
         nc.sync.dma_start(out=wc_raw[:], in_=wc.rearrange("(p j) c -> p j c", j=PACK))
         nc.sync.dma_start(offsets[:], offs)
-        bytes_all = keep.tile([P, T], U8, name="bytes_all", tag="bytes_all", align_bytes=64)
+        bytes_all = sb("bytes_all", [P, T], U8)
         nc.vector.memset(bytes_all[:].bitcast(I32), 0)
-        for r in range(4):
-            nc.sync.dma_start(out=bytes_all[r:P:32, :].bitcast(I32), in_=x_scales[0, r:16:4, :].bitcast(I32))
-        words = sb("words", [P, T], I32)
-        nc.sync.dma_start(out=words[:], in_=x_words[0].rearrange("p n t -> p (n t)").bitcast(I32))
-        u_rows = sb("u_rows", [P, 8], F32)
-        for e in range(2):
-            nc.sync.dma_start(out=u_rows[e:P:2, 0:7], in_=unit.rearrange("(a r) o -> a (r o)", r=8)[:, e:e + 7])
-        u = u_rows[:, 0:8:2]
-        ws_raw = [load_half("ws", ws, h) for h in range(2)]
+        for r in range(PACK):
+            nc.sync.dma_start(out=bytes_all[r:P:QUADRANT, :].bitcast(I32), in_=x_scales[0, r:K // 32:PACK, :].bitcast(I32))
+        words_all = sb("words_all", [P, T], I32)
+        nc.sync.dma_start(out=words_all[:], in_=x_words[0].rearrange("p n t -> p (n t)").bitcast(I32))
+        ws_raw = []
+        for h in range(2):
+            raw = sb("ws_raw%d" % h, [P, PACK, WS_COLS], F32)
+            nc.sync.dma_start(out=raw[:], in_=ws.rearrange("(p j) c -> p j c", j=PACK)[:, :, h * WS_COLS:(h + 1) * WS_COLS])
+            ws_raw.append(raw)
+        run = PAIR * PACK
+        unit_runs = sb("unit_runs", [P, run], F32)
+        for e in range(PAIR):
+            nc.sync.dma_start(out=unit_runs[e:P:PAIR, 0:run - 1], in_=unit.rearrange("(a r) o -> a (r o)", r=run)[:, e:e + run - 1])
+        u = unit_runs[:, 0:run:PAIR]
         v_raw = sb("v_raw", [P, 2, PACK, N], F32)
-        for a, v in enumerate((vc, vs)):
-            for e in range(2):
-                nc.sync.dma_start(out=v_raw[e:P:2, a, :, :], in_=v.rearrange("(a t e) m -> e a t m", t=PACK, e=2)[e])
+        for part, v in enumerate((vc, vs)):
+            for e in range(PAIR):
+                nc.sync.dma_start(out=v_raw[e:P:PAIR, part, :, :], in_=v.rearrange("(a t e) m -> e a t m", t=PACK, e=PAIR)[e])
 
-        one = sb("one", [P, 1], F32)
-        nc.vector.memset(one[:], 1.0)
-        warm = sb("warm", [P, 1], F32)
-        nc.scalar.activation(warm[:], one[:], ACT.Abs_reciprocal_sqrt)
+        huge = sb("huge", [P, 1], F32)
+        nc.vector.memset(huge[:], 2.0 ** 96)
+        guard = sb("guard", [P, 1], F32)
+        nc.scalar.activation(guard[:], huge[:], ACT.Abs_reciprocal_sqrt)
 
-        u_sign = sb("u_sign", [P, PACK], F32)
-        nc.scalar.activation(u_sign[:], u, ACT.Sign)
-        u2 = sb("u2", [P, PACK], F32)
-        nc.scalar.activation(u2[:], u, ACT.Square)
-        u2_noise = sb("u2_noise", [P, PACK], F32)
-        nc.scalar.activation(u2_noise[:], u2[:], ACT.Copy, scale=1.5)
-        u2_floor = sb("u2_floor", [P, PACK], F32)
-        nc.scalar.activation(u2_floor[:], u2[:], ACT.Copy, scale=0.02)
-        u2_top = sb("u2_top", [P, PACK], F32)
-        nc.scalar.activation(u2_top[:], u2[:], ACT.Copy, scale=1.02)
-
-        def cast_w(copy, raw, grouped):
-            copy(grouped.rearrange("p t (a e) j -> p t a j e", e=2), raw.rearrange("p j (a t e) -> p t a j e", t=PACK, e=2))
+        def round_and_deal(copy, raw, grouped):
+            copy(grouped.rearrange("p t (a e) j -> p t a j e", e=PAIR), raw.rearrange("p j (a t e) -> p t a j e", t=PACK, e=PAIR))
 
         wc_bf = sb("wc_bf", [P, PACK, P, PACK], BF16)
-        cast_w(nc.scalar.copy, wc_raw[:, :, 0:320], wc_bf[:, :, 0:80, :])
+        round_and_deal(nc.scalar.copy, wc_raw[:, :, 0:PACK * SCALAR_ROWS], wc_bf[:, :, 0:SCALAR_ROWS, :])
         x_bytes = sb("x_bytes", [P, S], U8)
         nc.vector.tensor_copy(x_bytes[:], bytes_all[:].indirect(offsets[:]))
-        cast_w(nc.vector.tensor_copy, wc_raw[:, :, 320:H], wc_bf[:, :, 80:128, :])
-        wc_codes = keep.tile([P, H], U32, name="wc_codes", tag="bytes_all", align_bytes=64)
+        round_and_deal(nc.vector.tensor_copy, wc_raw[:, :, PACK * SCALAR_ROWS:H], wc_bf[:, :, SCALAR_ROWS:P, :])
+        wc_codes = sb("wc_codes", [P, H], U32, tag="bytes_all")
         wc_scales = sb("wc_scales", [P, H], U8)
         nc.vector.quantize_mx(out=wc_codes[:].bitcast(FP8X4), scales=wc_scales[:], in_=wc_bf[:].rearrange("p t m j -> p (t m j)"))
 
         x_codes = []
         for h in range(2):
-            g = sb("x_codes%d" % h, [P, HALF], U32)
-            nc.vector.tensor_copy(g[:], words[:].bitcast(U32).indirect(offsets[:, h * HALF // 16:(h + 1) * HALF // 16]))
-            x_codes.append(g)
+            picked = sb("x_codes%d" % h, [P, HALF], U32)
+            nc.vector.tensor_copy(picked[:], words_all[:].bitcast(U32).indirect(offsets[:, h * HALF // 16:(h + 1) * HALF // 16]))
+            x_codes.append(picked)
 
-        def first_product(tag, codes, scales, c):
-            bank = psum.tile([P, PACK, CHUNK], F32, name="%s%d" % (tag, c), tag="%s%d" % (tag, c))
-            cols = slice((c % 2) * CHUNK, (c % 2 + 1) * CHUNK)
+        def first_product(name, codes, scales, c):
+            bank = psum.tile([P, PACK, CHUNK], F32, name="%s%d" % (name, c), tag="%s%d" % (name, c))
             for t in range(PACK):
-                nc.tensor.matmul_mx(out=bank[:, t, :], lhsT=codes[:, t * P:(t + 1) * P].bitcast(FP8X4), lhsT_scale=scales[:, t * P:(t + 1) * P],
-                                    rhs=x_codes[c // 2][:, cols].bitcast(FP8X4), rhs_scale=x_bytes[:, c * CHUNK:(c + 1) * CHUNK], start=True, stop=True)
+                plane = slice(t * P, (t + 1) * P)
+                nc.tensor.matmul_mx(out=bank[:, t, :], lhsT=codes[:, plane].bitcast(FP8X4), lhsT_scale=scales[:, plane],
+                                    rhs=x_codes[c // PER_HALF][:, in_half(c)].bitcast(FP8X4), rhs_scale=x_bytes[:, c * CHUNK:(c + 1) * CHUNK],
+                                    start=True, stop=True)
             return bank
 
         re = [first_product("re", wc_codes, wc_scales, c) for c in range(CHUNKS)]
@@ -110,11 +114,24 @@ def tile_picked_ysubtr_sub_p_kernel(tc, x_words, x_scales, wc, ws, unit, vc, vs,
         ws_codes = sb("ws_codes", [P, H], U32)
         ws_scales = sb("ws_scales", [P, H], U8)
         for h in range(2):
-            ws_bf = sb("ws_bf%d" % h, [P, PACK, 64, PACK], BF16)
-            cast_w(nc.vector.tensor_copy, ws_raw[h][:], ws_bf[:])
+            ws_bf = sb("ws_bf%d" % h, [P, PACK, WS_ROWS, PACK], BF16)
+            round_and_deal(nc.vector.tensor_copy, ws_raw[h][:], ws_bf[:])
             for t in range(PACK):
-                cols = slice(t * P + 64 * h, t * P + 64 * h + 64)
+                cols = slice(t * P + WS_ROWS * h, t * P + WS_ROWS * (h + 1))
                 nc.vector.quantize_mx(out=ws_codes[:, cols].bitcast(FP8X4), scales=ws_scales[:, cols], in_=ws_bf[:, t, :, :].rearrange("p m j -> p (m j)"))
+
+        u2 = sb("u2", [P, PACK], F32)
+        nc.vector.tensor_tensor(u2[:], u, u, ALU.mult)
+        u_step = sb("u_step", [P, PACK], F32)
+        nc.vector.tensor_scalar(u_step[:], u, 0.0, 2.0, ALU.is_ge, ALU.mult)
+        u2_noise = sb("u2_noise", [P, PACK], F32)
+        nc.vector.tensor_scalar(u2_noise[:], u2[:], NOISE_FACTOR, None, ALU.mult)
+        u2_top = sb("u2_top", [P, PACK], F32)
+        nc.vector.tensor_scalar(u2_top[:], u2[:], 1.02, None, ALU.mult)
+        u2_floor = sb("u2_floor", [P, PACK], F32)
+        nc.vector.tensor_scalar(u2_floor[:], u2[:], GAIN_FLOOR, None, ALU.mult)
+        u_sign = sb("u_sign", [P, PACK], F32)
+        nc.vector.tensor_scalar(u_sign[:], u_step[:], -1.0, None, ALU.add)
 
         im = [first_product("im", ws_codes, ws_scales, c) for c in range(CHUNKS)]
 
@@ -122,54 +139,54 @@ def tile_picked_ysubtr_sub_p_kernel(tc, x_words, x_scales, wc, ws, unit, vc, vs,
         for c in range(CHUNKS):
             sq = sb("im_sq%d" % c, [P, PACK, CHUNK], F32)
             nc.scalar.activation(sq[:], im[c][:], ACT.Square)
-            cols = slice((c % 2) * CHUNK, (c % 2 + 1) * CHUNK)
-            nc.vector.tensor_tensor(power[c // 2][:, :, cols], re_sq[c][:], sq[:], ALU.add)
+            nc.vector.tensor_tensor(power[c // PER_HALF][:, :, in_half(c)], re_sq[c][:], sq[:], ALU.add)
 
-        groups = HALF // D
-        rs = [keep.tile([P, PACK, HALF], F32, name="rs%d" % h, tag="rs%d" % h, align_bytes=64) for h in range(2)]
-        least = [sb("least%d" % h, [P, PACK, groups], F32) for h in range(2)]
+        inv_root = [sb("inv_root%d" % h, [P, PACK, HALF], F32) for h in range(2)]
+        least = [sb("least%d" % h, [P, PACK, GROUPS], F32) for h in range(2)]
 
         def least_power(h):
-            nc.vector.tensor_reduce(least[h][:], power[h][:].rearrange("p t (v d) -> p t v d", d=D), AX.X, ALU.min)
+            nc.vector.tensor_reduce(least[h][:], by_runs(power[h][:]), AX.X, ALU.min)
 
-        nc.scalar.activation(rs[0][:], power[0][:], ACT.Abs_reciprocal_sqrt, bias=0.05)
-        inv = sb("inv", [P, PACK, HALF], F32)
-        nc.scalar.activation(inv[:], rs[0][:], ACT.Square)
-        nc.scalar.activation(rs[1][:], power[1][:], ACT.Abs_reciprocal_sqrt, bias=0.05)
+        nc.scalar.activation(inv_root[0][:], power[0][:], ACT.Abs_reciprocal_sqrt, bias=POWER_OFFSET)
+        inv_power = sb("inv_power", [P, PACK, HALF], F32)
+        nc.scalar.activation(inv_power[:], inv_root[0][:], ACT.Square)
+        nc.scalar.activation(inv_root[1][:], power[1][:], ACT.Abs_reciprocal_sqrt, bias=POWER_OFFSET)
         least_power(0)
-        noise = sb("noise", [P, PACK, groups], F32)
-        nc.vector.tensor_tensor(noise[:], least[0][:], u2_noise[:].unsqueeze(2).to_broadcast([P, PACK, groups]), ALU.mult)
+        noise_u2 = sb("noise_u2", [P, PACK, GROUPS], F32)
+        nc.vector.tensor_tensor(noise_u2[:], least[0][:], u2_noise[:].unsqueeze(2).to_broadcast([P, PACK, GROUPS]), ALU.mult)
         least_power(1)
-        noise_rs = sb("noise_rs", [P, PACK, groups], F32)
-        nc.scalar.activation(noise_rs[:], least[1][:], ACT.Abs_reciprocal_sqrt, scale=1.5, bias=1e-30)
+        noise_inv_root = sb("noise_inv_root", [P, PACK, GROUPS], F32)
+        nc.scalar.activation(noise_inv_root[:], least[1][:], ACT.Abs_reciprocal_sqrt, scale=NOISE_FACTOR, bias=guard[:])
 
-        ratio = sb("ratio", [P, PACK, HALF], F32)
-        for t in (0, 2):
-            nc.vector.tensor_tensor(ratio[:, t:t + 2, :].rearrange("p t (v d) -> p t v d", d=D), inv[:, t:t + 2, :].rearrange("p t (v d) -> p t v d", d=D),
-                                    noise[:, t:t + 2, :].unsqueeze(3).to_broadcast([P, 2, groups, D]), ALU.mult)
-        noise_root = sb("noise_root", [P, PACK, groups], F32)
-        nc.vector.scalar_tensor_tensor(noise_root[:], least[1][:], 1.5, noise_rs[:], ALU.mult, ALU.mult)
+        ratio_u2 = sb("ratio_u2", [P, PACK, HALF], F32)
+        for t in range(0, PACK, 2):
+            nc.vector.tensor_tensor(by_runs(ratio_u2[:, t:t + 2, :]), by_runs(inv_power[:, t:t + 2, :]),
+                                    noise_u2[:, t:t + 2, :].unsqueeze(3).to_broadcast([P, 2, GROUPS, D]), ALU.mult)
+        noise_root = sb("noise_root", [P, PACK, GROUPS], F32)
+        nc.vector.scalar_tensor_tensor(noise_root[:], least[1][:], NOISE_FACTOR, noise_inv_root[:], ALU.mult, ALU.mult)
         neg_gain2 = sb("neg_gain2", [P, PACK, HALF], F32)
         for t in range(PACK):
-            nc.vector.tensor_scalar(neg_gain2[:, t, :], ratio[:, t, :], u2[:, t:t + 1], u2_top[:, t:t + 1], ALU.min, ALU.subtract)
+            nc.vector.tensor_scalar(neg_gain2[:, t, :], ratio_u2[:, t, :], u2[:, t:t + 1], u2_top[:, t:t + 1], ALU.min, ALU.subtract)
 
         root_ratio = []
-        for c in range(2):
+        runs = CHUNK // D
+        for c in range(PER_HALF):
             w = sb("root_ratio%d" % c, [P, PACK, CHUNK], F32)
-            nc.vector.tensor_tensor(w[:].rearrange("p t (v d) -> p t v d", d=D), rs[1][:, :, c * CHUNK:(c + 1) * CHUNK].rearrange("p t (v d) -> p t v d", d=D),
-                                    noise_root[:, :, c * groups // 2:(c + 1) * groups // 2].unsqueeze(3).to_broadcast([P, PACK, groups // 2, D]), ALU.mult)
+            nc.vector.tensor_tensor(by_runs(w[:]), by_runs(inv_root[1][:, :, in_half(c)]),
+                                    noise_root[:, :, c * runs:(c + 1) * runs].unsqueeze(3).to_broadcast([P, PACK, runs, D]), ALU.mult)
             root_ratio.append(w)
 
-        v_bf = keep.tile([P, 2, N, PACK], BF16, name="v_bf", tag="rs1", align_bytes=64)
-        for a in range(2):
-            nc.gpsimd.tensor_tensor(v_bf[:, a, :, :], v_raw[:, a, :, :].rearrange("p j m -> p m j"), u_sign[:].unsqueeze(1).to_broadcast([P, N, PACK]), ALU.mult)
+        v_bf = sb("v_bf", [P, 2, N, PACK], BF16, tag="inv_root1")
+        for part in range(2):
+            nc.gpsimd.tensor_tensor(v_bf[:, part, :, :], v_raw[:, part, :, :].rearrange("p t m -> p m t"),
+                                    u_sign[:].unsqueeze(1).to_broadcast([P, N, PACK]), ALU.mult)
 
-        gain = [keep.tile([P, PACK * CHUNK], F32, name="gain%d" % c, tag="gain%d" % c, align_bytes=64) for c in range(CHUNKS)]
-        late_ratio = [sb("late_ratio%d" % c, [P, PACK, CHUNK], F32) for c in range(2)]
+        gain = [sb("gain%d" % c, [P, PACK * CHUNK], F32) for c in range(CHUNKS)]
+        late_ratio = [sb("late_ratio%d" % c, [P, PACK, CHUNK], F32) for c in range(PER_HALF)]
 
         def early_gain(c):
-            nc.scalar.activation(gain[c][:].rearrange("p (b e t) -> p b t e", e=2, t=PACK),
-                                 neg_gain2[:, :, c * CHUNK:(c + 1) * CHUNK].rearrange("p t (b e) -> p b t e", e=2), ACT.Sqrt, scale=-1.0)
+            nc.scalar.activation(gain[c][:].rearrange("p (b e t) -> p b t e", e=PAIR, t=PACK),
+                                 neg_gain2[:, :, in_half(c)].rearrange("p t (b e) -> p b t e", e=PAIR), ACT.Sqrt, scale=-1.0)
 
         def square_ratio(c):
             nc.scalar.activation(late_ratio[c][:], root_ratio[c][:], ACT.Square)
@@ -178,7 +195,8 @@ def tile_picked_ysubtr_sub_p_kernel(tc, x_words, x_scales, wc, ws, unit, vc, vs,
             kept = sb("kept%d" % c, [P, PACK, CHUNK], F32)
             nc.scalar.activation(kept[:], late_ratio[c][:], ACT.Relu, scale=-1.0, bias=1.0)
             for t in range(PACK):
-                nc.scalar.activation(gain[2 + c][:, t * CHUNK:(t + 1) * CHUNK], kept[:, t, :], ACT.Sqrt, scale=u2[:, t:t + 1], bias=u2_floor[:, t:t + 1])
+                nc.scalar.activation(gain[PER_HALF + c][:, t * CHUNK:(t + 1) * CHUNK], kept[:, t, :], ACT.Sqrt,
+                                     scale=u2[:, t:t + 1], bias=u2_floor[:, t:t + 1])
 
         early_gain(0)
         square_ratio(0)
@@ -192,34 +210,37 @@ def tile_picked_ysubtr_sub_p_kernel(tc, x_words, x_scales, wc, ws, unit, vc, vs,
         z_scales = sb("z_scales", [P, 2 * S], U8)
 
         def weigh(c):
-            for a, bank in enumerate((re[c], im[c])):
-                if c < 2:
-                    nc.vector.tensor_tensor(z[:, 2 * c + a, :, :], bank[:].rearrange("p t n -> p n t"), gain[c][:].rearrange("p (n t) -> p n t", t=PACK), ALU.mult)
+            for part, bank in enumerate((re[c], im[c])):
+                strip = z[:, 2 * c + part, :, :]
+                if c < PER_HALF:
+                    nc.vector.tensor_tensor(strip, bank[:].rearrange("p t n -> p n t"), gain[c][:].rearrange("p (n t) -> p n t", t=PACK), ALU.mult)
                 else:
-                    nc.vector.tensor_tensor(z[:, 2 * c + a, :, :].rearrange("p (b e) t -> p b t e", e=2), bank[:].rearrange("p t (b e) -> p b t e", e=2),
-                                            gain[c][:].rearrange("p (t b e) -> p b t e", t=PACK, e=2), ALU.mult)
+                    nc.vector.tensor_tensor(strip.rearrange("p (b e) t -> p b t e", e=PAIR), bank[:].rearrange("p t (b e) -> p b t e", e=PAIR),
+                                            gain[c][:].rearrange("p (t b e) -> p b t e", t=PACK, e=PAIR), ALU.mult)
 
-        def quantize_z(first, last):
+        def quantize_strips(first, last):
             cols = slice(first * CHUNK, last * CHUNK)
             nc.vector.quantize_mx(out=z_codes[:, cols].bitcast(FP8X4), scales=z_scales[:, cols], in_=z[:, first:last, :, :].rearrange("p s n t -> p (s n t)"))
 
-        for c in range(CHUNKS - 1):
+        last = CHUNKS - 1
+        for c in range(last):
             weigh(c)
-        quantize_z(0, 4)
-        quantize_z(4, 6)
-        v_codes = keep.tile([P, 2 * N], U32, name="v_codes", tag="gain2", align_bytes=64)
+        quantize_strips(0, 2 * PER_HALF)
+        quantize_strips(2 * PER_HALF, 2 * last)
+        v_codes = sb("v_codes", [P, 2 * N], U32, tag="gain%d" % (last - 1))
         v_scales = sb("v_scales", [P, 2 * N], U8)
-        nc.vector.quantize_mx(out=v_codes[:].bitcast(FP8X4), scales=v_scales[:], in_=v_bf[:].rearrange("p a m j -> p (a m j)"))
-        weigh(CHUNKS - 1)
-        quantize_z(6, 7)
-        quantize_z(7, 8)
+        nc.vector.quantize_mx(out=v_codes[:].bitcast(FP8X4), scales=v_scales[:], in_=v_bf[:].rearrange("p a m t -> p (a m t)"))
+        weigh(last)
+        quantize_strips(2 * last, 2 * last + 1)
+        quantize_strips(2 * last + 1, 2 * last + 2)
 
         for c in range(CHUNKS):
             acc = psum.tile([P, CHUNK], F32, name="acc%d" % c, tag="re%d" % c)
-            for a in range(2):
-                cols = slice((2 * c + a) * CHUNK, (2 * c + a + 1) * CHUNK)
-                nc.tensor.matmul_mx(out=acc[:], lhsT=v_codes[:, a * N:(a + 1) * N].bitcast(FP8X4), lhsT_scale=v_scales[:, a * N:(a + 1) * N],
-                                    rhs=z_codes[:, cols].bitcast(FP8X4), rhs_scale=z_scales[:, cols], start=(a == 0), stop=(a == 1))
+            for part in range(2):
+                cols = slice((2 * c + part) * CHUNK, (2 * c + part + 1) * CHUNK)
+                rows = slice(part * N, (part + 1) * N)
+                nc.tensor.matmul_mx(out=acc[:], lhsT=v_codes[:, rows].bitcast(FP8X4), lhsT_scale=v_scales[:, rows],
+                                    rhs=z_codes[:, cols].bitcast(FP8X4), rhs_scale=z_scales[:, cols], start=(part == 0), stop=(part == 1))
             result = sb("result%d" % c, [P, CHUNK], F32)
             nc.scalar.copy(result[:], acc[:])
             nc.sync.dma_start(out=out[:, c * CHUNK:(c + 1) * CHUNK], in_=result[:])

@@ -27,7 +27,7 @@ PER_HALF = HALF // CHUNK
 GROUPS = HALF // D
 WS_COLS = H // 2
 WS_ROWS = P // 2
-SCALAR_ROWS = 80
+SCALAR_ROWS = 96
 
 POWER_OFFSET, NOISE_FACTOR, GAIN_FLOOR = 0.05, 1.5, 0.02
 
@@ -48,6 +48,9 @@ def tile_picked_ysubtr_sub_p_kernel(tc, x_words, x_scales, wc, ws, unit, vc, vs,
             return ap.rearrange("p t (v d) -> p t v d", d=D)
 
         offsets = keep.tile([P, S // 16], U16, name="offsets")
+        unit_planes = sb("unit_planes", [P, PACK], F32)
+        nc.sync.dma_start(out=unit_planes[:], in_=unit.rearrange("(p t) o -> p (t o)", t=PACK))
+        u = unit_planes[:]
         wc_raw = sb("wc_raw", [P, PACK, H], F32)
         nc.sync.dma_start(out=wc_raw[:], in_=wc.rearrange("(p j) c -> p j c", j=PACK))
         nc.sync.dma_start(offsets[:], offs)
@@ -62,23 +65,26 @@ def tile_picked_ysubtr_sub_p_kernel(tc, x_words, x_scales, wc, ws, unit, vc, vs,
             raw = sb("ws_raw%d" % h, [P, PACK, WS_COLS], F32)
             nc.sync.dma_start(out=raw[:], in_=ws.rearrange("(p j) c -> p j c", j=PACK)[:, :, h * WS_COLS:(h + 1) * WS_COLS])
             ws_raw.append(raw)
-        run = PAIR * PACK
-        unit_runs = sb("unit_runs", [P, run], F32)
-        for e in range(PAIR):
-            nc.sync.dma_start(out=unit_runs[e:P:PAIR, 0:run - 1], in_=unit.rearrange("(a r) o -> a (r o)", r=run)[:, e:e + run - 1])
-        u = unit_runs[:, 0:run:PAIR]
         v_raw = sb("v_raw", [P, 2, PACK, N], F32)
         for part, v in enumerate((vc, vs)):
-            for e in range(PAIR):
-                nc.sync.dma_start(out=v_raw[e:P:PAIR, part, :, :], in_=v.rearrange("(a t e) m -> e a t m", t=PACK, e=PAIR)[e])
+            nc.sync.dma_start(out=v_raw[:, part, :, :], in_=v.rearrange("(p t) m -> p t m", t=PACK))
 
         huge = sb("huge", [P, 1], F32)
         nc.vector.memset(huge[:], 2.0 ** 96)
         guard = sb("guard", [P, 1], F32)
         nc.scalar.activation(guard[:], huge[:], ACT.Abs_reciprocal_sqrt)
 
+        u_step = sb("u_step", [P, PACK], F32)
+        nc.vector.tensor_scalar(u_step[:], u, 0.0, 2.0, ALU.is_ge, ALU.mult)
+        u2_neg = sb("u2_neg", [P, PACK], F32)
+        nc.vector.scalar_tensor_tensor(u2_neg[:], u, -1.0, u, ALU.mult, ALU.mult)
+        u2_top = sb("u2_top", [P, PACK], F32)
+        nc.vector.scalar_tensor_tensor(u2_top[:], u, 1.02, u, ALU.mult, ALU.mult)
+        u_sign = sb("u_sign", [P, PACK], F32)
+        nc.vector.tensor_scalar(u_sign[:], u_step[:], -1.0, None, ALU.add)
+
         def round_and_deal(copy, raw, grouped):
-            copy(grouped.rearrange("p t (a e) j -> p t a j e", e=PAIR), raw.rearrange("p j (a t e) -> p t a j e", t=PACK, e=PAIR))
+            copy(grouped.rearrange("p t m j -> p m j t"), raw.rearrange("p j (m t) -> p m j t", t=PACK))
 
         wc_bf = sb("wc_bf", [P, PACK, P, PACK], BF16)
         round_and_deal(nc.scalar.copy, wc_raw[:, :, 0:PACK * SCALAR_ROWS], wc_bf[:, :, 0:SCALAR_ROWS, :])
@@ -113,33 +119,29 @@ def tile_picked_ysubtr_sub_p_kernel(tc, x_words, x_scales, wc, ws, unit, vc, vs,
 
         ws_codes = sb("ws_codes", [P, H], U32)
         ws_scales = sb("ws_scales", [P, H], U8)
+        ws_bf = sb("ws_bf", [P, PACK, P, PACK], BF16)
         for h in range(2):
-            ws_bf = sb("ws_bf%d" % h, [P, PACK, WS_ROWS, PACK], BF16)
-            round_and_deal(nc.vector.tensor_copy, ws_raw[h][:], ws_bf[:])
-            for t in range(PACK):
-                cols = slice(t * P + WS_ROWS * h, t * P + WS_ROWS * (h + 1))
-                nc.vector.quantize_mx(out=ws_codes[:, cols].bitcast(FP8X4), scales=ws_scales[:, cols], in_=ws_bf[:, t, :, :].rearrange("p m j -> p (m j)"))
-
-        u2 = sb("u2", [P, PACK], F32)
-        nc.vector.tensor_tensor(u2[:], u, u, ALU.mult)
-        u_step = sb("u_step", [P, PACK], F32)
-        nc.vector.tensor_scalar(u_step[:], u, 0.0, 2.0, ALU.is_ge, ALU.mult)
-        u2_noise = sb("u2_noise", [P, PACK], F32)
-        nc.vector.tensor_scalar(u2_noise[:], u2[:], NOISE_FACTOR, None, ALU.mult)
-        u2_top = sb("u2_top", [P, PACK], F32)
-        nc.vector.tensor_scalar(u2_top[:], u2[:], 1.02, None, ALU.mult)
-        u2_floor = sb("u2_floor", [P, PACK], F32)
-        nc.vector.tensor_scalar(u2_floor[:], u2[:], GAIN_FLOOR, None, ALU.mult)
-        u_sign = sb("u_sign", [P, PACK], F32)
-        nc.vector.tensor_scalar(u_sign[:], u_step[:], -1.0, None, ALU.add)
+            round_and_deal(nc.vector.tensor_copy, ws_raw[h][:], ws_bf[:, :, h * WS_ROWS:(h + 1) * WS_ROWS, :])
+        for t in range(0, PACK, 2):
+            cols = slice(t * P, (t + 2) * P)
+            nc.vector.quantize_mx(out=ws_codes[:, cols].bitcast(FP8X4), scales=ws_scales[:, cols], in_=ws_bf[:, t:t + 2, :, :].rearrange("p t m j -> p (t m j)"))
 
         im = [first_product("im", ws_codes, ws_scales, c) for c in range(CHUNKS)]
+
+        v_bf = sb("v_bf", [P, 2, N, PACK], BF16)
+        for part in range(2):
+            nc.vector.tensor_tensor(v_bf[:, part, :, :].rearrange("p (b i) t -> p b t i", i=PACK), v_raw[:, part, :, :].rearrange("p t (b i) -> p b t i", i=PACK),
+                                    u_sign[:].unsqueeze(1).unsqueeze(3).to_broadcast([P, N // PACK, PACK, PACK]), ALU.mult)
+        v_codes = sb("v_codes", [P, 2 * N], U32)
+        v_scales = sb("v_scales", [P, 2 * N], U8)
 
         power = [sb("power%d" % h, [P, PACK, HALF], F32) for h in range(2)]
         for c in range(CHUNKS):
             sq = sb("im_sq%d" % c, [P, PACK, CHUNK], F32)
             nc.scalar.activation(sq[:], im[c][:], ACT.Square)
             nc.vector.tensor_tensor(power[c // PER_HALF][:, :, in_half(c)], re_sq[c][:], sq[:], ALU.add)
+            if c == 0:
+                nc.vector.quantize_mx(out=v_codes[:].bitcast(FP8X4), scales=v_scales[:], in_=v_bf[:].rearrange("p a m t -> p (a m t)"))
 
         inv_root = [sb("inv_root%d" % h, [P, PACK, HALF], F32) for h in range(2)]
         least = [sb("least%d" % h, [P, PACK, GROUPS], F32) for h in range(2)]
@@ -153,7 +155,7 @@ def tile_picked_ysubtr_sub_p_kernel(tc, x_words, x_scales, wc, ws, unit, vc, vs,
         nc.scalar.activation(inv_root[1][:], power[1][:], ACT.Abs_reciprocal_sqrt, bias=POWER_OFFSET)
         least_power(0)
         noise_u2 = sb("noise_u2", [P, PACK, GROUPS], F32)
-        nc.vector.tensor_tensor(noise_u2[:], least[0][:], u2_noise[:].unsqueeze(2).to_broadcast([P, PACK, GROUPS]), ALU.mult)
+        nc.vector.scalar_tensor_tensor(noise_u2[:], least[0][:], NOISE_FACTOR, u2_neg[:].unsqueeze(2).to_broadcast([P, PACK, GROUPS]), ALU.mult, ALU.mult)
         least_power(1)
         noise_inv_root = sb("noise_inv_root", [P, PACK, GROUPS], F32)
         nc.scalar.activation(noise_inv_root[:], least[1][:], ACT.Abs_reciprocal_sqrt, scale=NOISE_FACTOR, bias=guard[:])
@@ -164,46 +166,44 @@ def tile_picked_ysubtr_sub_p_kernel(tc, x_words, x_scales, wc, ws, unit, vc, vs,
                                     noise_u2[:, t:t + 2, :].unsqueeze(3).to_broadcast([P, 2, GROUPS, D]), ALU.mult)
         noise_root = sb("noise_root", [P, PACK, GROUPS], F32)
         nc.vector.scalar_tensor_tensor(noise_root[:], least[1][:], NOISE_FACTOR, noise_inv_root[:], ALU.mult, ALU.mult)
+        runs = CHUNK // D
+
+        def root_ratio(engine, w, c):
+            engine.tensor_tensor(by_runs(w), by_runs(inv_root[1][:, :, in_half(c)]),
+                                 noise_root[:, :, c * runs:(c + 1) * runs].unsqueeze(3).to_broadcast([P, PACK, runs, D]), ALU.mult)
+
+        def clip(dst, w):
+            nc.gpsimd.tensor_scalar(dst, w, 1.0, 0.0, ALU.min, ALU.max)
+
         neg_gain2 = sb("neg_gain2", [P, PACK, HALF], F32)
         for t in range(PACK):
-            nc.vector.tensor_scalar(neg_gain2[:, t, :], ratio_u2[:, t, :], u2[:, t:t + 1], u2_top[:, t:t + 1], ALU.min, ALU.subtract)
+            nc.vector.tensor_scalar(neg_gain2[:, t, :], ratio_u2[:, t, :], u2_neg[:, t:t + 1], u2_top[:, t:t + 1], ALU.max, ALU.add)
 
-        root_ratio = []
-        runs = CHUNK // D
-        for c in range(PER_HALF):
-            w = sb("root_ratio%d" % c, [P, PACK, CHUNK], F32)
-            nc.vector.tensor_tensor(by_runs(w[:]), by_runs(inv_root[1][:, :, in_half(c)]),
-                                    noise_root[:, :, c * runs:(c + 1) * runs].unsqueeze(3).to_broadcast([P, PACK, runs, D]), ALU.mult)
-            root_ratio.append(w)
-
-        v_bf = sb("v_bf", [P, 2, N, PACK], BF16, tag="inv_root1")
-        for part in range(2):
-            nc.gpsimd.tensor_tensor(v_bf[:, part, :, :], v_raw[:, part, :, :].rearrange("p t m -> p m t"),
-                                    u_sign[:].unsqueeze(1).to_broadcast([P, N, PACK]), ALU.mult)
+        third = sb("third", [P, PACK, CHUNK], F32)
+        root_ratio(nc.vector, third[:], 0)
+        clipped = [sb("clipped%d" % c, [P, PACK, CHUNK], F32) for c in range(PER_HALF)]
+        clip(clipped[0][:], third[:])
+        fourth = sb("fourth", [P, PACK, CHUNK], F32, tag="third")
+        root_ratio(nc.gpsimd, fourth[:], 1)
+        clip(clipped[1][:], fourth[:])
 
         gain = [sb("gain%d" % c, [P, PACK * CHUNK], F32) for c in range(CHUNKS)]
-        late_ratio = [sb("late_ratio%d" % c, [P, PACK, CHUNK], F32) for c in range(PER_HALF)]
 
         def early_gain(c):
             nc.scalar.activation(gain[c][:].rearrange("p (b e t) -> p b t e", e=PAIR, t=PACK),
-                                 neg_gain2[:, :, in_half(c)].rearrange("p t (b e) -> p b t e", e=PAIR), ACT.Sqrt, scale=-1.0)
-
-        def square_ratio(c):
-            nc.scalar.activation(late_ratio[c][:], root_ratio[c][:], ACT.Square)
+                                 neg_gain2[:, :, in_half(c)].rearrange("p t (b e) -> p b t e", e=PAIR), ACT.Sqrt)
 
         def late_gain(c):
-            kept = sb("kept%d" % c, [P, PACK, CHUNK], F32)
-            nc.scalar.activation(kept[:], late_ratio[c][:], ACT.Relu, scale=-1.0, bias=1.0)
+            late_ratio = sb("late_ratio%d" % c, [P, PACK, CHUNK], F32, tag="late_ratio")
+            nc.scalar.activation(late_ratio[:], clipped[c][:], ACT.Square)
             for t in range(PACK):
-                nc.scalar.activation(gain[PER_HALF + c][:, t * CHUNK:(t + 1) * CHUNK], kept[:, t, :], ACT.Sqrt,
-                                     scale=u2[:, t:t + 1], bias=u2_floor[:, t:t + 1])
+                nc.scalar.activation(gain[PER_HALF + c][:, t * CHUNK:(t + 1) * CHUNK], late_ratio[:, t, :], ACT.Sqrt,
+                                     scale=u2_neg[:, t:t + 1], bias=u2_top[:, t:t + 1])
 
-        early_gain(0)
-        square_ratio(0)
-        early_gain(1)
-        late_gain(0)
-        square_ratio(1)
-        late_gain(1)
+        for c in range(PER_HALF):
+            early_gain(c)
+        for c in range(PER_HALF):
+            late_gain(c)
 
         z = sb("z", [P, 2 * CHUNKS, CHUNK, PACK], BF16)
         z_codes = sb("z_codes", [P, 2 * S], U32)
@@ -227,13 +227,11 @@ def tile_picked_ysubtr_sub_p_kernel(tc, x_words, x_scales, wc, ws, unit, vc, vs,
             weigh(c)
         quantize_strips(0, 2 * PER_HALF)
         quantize_strips(2 * PER_HALF, 2 * last)
-        v_codes = sb("v_codes", [P, 2 * N], U32, tag="gain%d" % (last - 1))
-        v_scales = sb("v_scales", [P, 2 * N], U8)
-        nc.vector.quantize_mx(out=v_codes[:].bitcast(FP8X4), scales=v_scales[:], in_=v_bf[:].rearrange("p a m t -> p (a m t)"))
         weigh(last)
         quantize_strips(2 * last, 2 * last + 1)
         quantize_strips(2 * last + 1, 2 * last + 2)
 
+        result = sb("result", [P, CHUNKS, CHUNK], F32, tag="late_ratio")
         for c in range(CHUNKS):
             acc = psum.tile([P, CHUNK], F32, name="acc%d" % c, tag="re%d" % c)
             for part in range(2):
@@ -241,6 +239,5 @@ def tile_picked_ysubtr_sub_p_kernel(tc, x_words, x_scales, wc, ws, unit, vc, vs,
                 rows = slice(part * N, (part + 1) * N)
                 nc.tensor.matmul_mx(out=acc[:], lhsT=v_codes[:, rows].bitcast(FP8X4), lhsT_scale=v_scales[:, rows],
                                     rhs=z_codes[:, cols].bitcast(FP8X4), rhs_scale=z_scales[:, cols], start=(part == 0), stop=(part == 1))
-            result = sb("result%d" % c, [P, CHUNK], F32)
-            nc.scalar.copy(result[:], acc[:])
-            nc.sync.dma_start(out=out[:, c * CHUNK:(c + 1) * CHUNK], in_=result[:])
+            nc.scalar.copy(result[:, c, :], acc[:])
+            nc.sync.dma_start(out=out[:, c * CHUNK:(c + 1) * CHUNK], in_=result[:, c, :])

@@ -48,9 +48,6 @@ def tile_picked_ysubtr_sub_p_kernel(tc, x_words, x_scales, wc, ws, unit, vc, vs,
             return ap.rearrange("p t (v d) -> p t v d", d=D)
 
         offsets = keep.tile([P, S // 16], U16, name="offsets")
-        unit_planes = sb("unit_planes", [P, PACK], F32)
-        nc.sync.dma_start(out=unit_planes[:], in_=unit.rearrange("(p t) o -> p (t o)", t=PACK))
-        u = unit_planes[:]
         wc_raw = sb("wc_raw", [P, PACK, H], F32)
         nc.sync.dma_start(out=wc_raw[:], in_=wc.rearrange("(p j) c -> p j c", j=PACK))
         nc.sync.dma_start(offsets[:], offs)
@@ -60,6 +57,9 @@ def tile_picked_ysubtr_sub_p_kernel(tc, x_words, x_scales, wc, ws, unit, vc, vs,
             nc.sync.dma_start(out=bytes_all[r:P:QUADRANT, :].bitcast(I32), in_=x_scales[0, r:K // 32:PACK, :].bitcast(I32))
         words_all = sb("words_all", [P, T], I32)
         nc.sync.dma_start(out=words_all[:], in_=x_words[0].rearrange("p n t -> p (n t)").bitcast(I32))
+        unit_planes = sb("unit_planes", [P, PACK], F32)
+        nc.sync.dma_start(out=unit_planes[:], in_=unit.rearrange("(p t) o -> p (t o)", t=PACK))
+        u = unit_planes[:]
         ws_raw = []
         for h in range(2):
             raw = sb("ws_raw%d" % h, [P, PACK, WS_COLS], F32)
@@ -74,15 +74,6 @@ def tile_picked_ysubtr_sub_p_kernel(tc, x_words, x_scales, wc, ws, unit, vc, vs,
         guard = sb("guard", [P, 1], F32)
         nc.scalar.activation(guard[:], huge[:], ACT.Abs_reciprocal_sqrt)
 
-        u_step = sb("u_step", [P, PACK], F32)
-        nc.vector.tensor_scalar(u_step[:], u, 0.0, 2.0, ALU.is_ge, ALU.mult)
-        u2_neg = sb("u2_neg", [P, PACK], F32)
-        nc.vector.scalar_tensor_tensor(u2_neg[:], u, -1.0, u, ALU.mult, ALU.mult)
-        u2_top = sb("u2_top", [P, PACK], F32)
-        nc.vector.scalar_tensor_tensor(u2_top[:], u, 1.02, u, ALU.mult, ALU.mult)
-        u_sign = sb("u_sign", [P, PACK], F32)
-        nc.vector.tensor_scalar(u_sign[:], u_step[:], -1.0, None, ALU.add)
-
         def round_and_deal(copy, raw, grouped):
             copy(grouped.rearrange("p t m j -> p m j t"), raw.rearrange("p j (m t) -> p m j t", t=PACK))
 
@@ -94,6 +85,15 @@ def tile_picked_ysubtr_sub_p_kernel(tc, x_words, x_scales, wc, ws, unit, vc, vs,
         wc_codes = sb("wc_codes", [P, H], U32, tag="bytes_all")
         wc_scales = sb("wc_scales", [P, H], U8)
         nc.vector.quantize_mx(out=wc_codes[:].bitcast(FP8X4), scales=wc_scales[:], in_=wc_bf[:].rearrange("p t m j -> p (t m j)"))
+
+        u2 = sb("u2", [P, PACK], F32)
+        nc.scalar.activation(u2[:], u, ACT.Square)
+        u_sign = sb("u_sign", [P, PACK], F32)
+        nc.scalar.activation(u_sign[:], u, ACT.Sign)
+        u2_top = sb("u2_top", [P, PACK], F32)
+        nc.scalar.activation(u2_top[:], u2[:], ACT.Copy, scale=1.02)
+        u2_floor = sb("u2_floor", [P, PACK], F32)
+        nc.scalar.activation(u2_floor[:], u2[:], ACT.Copy, scale=GAIN_FLOOR)
 
         x_codes = []
         for h in range(2):
@@ -128,20 +128,11 @@ def tile_picked_ysubtr_sub_p_kernel(tc, x_words, x_scales, wc, ws, unit, vc, vs,
 
         im = [first_product("im", ws_codes, ws_scales, c) for c in range(CHUNKS)]
 
-        v_bf = sb("v_bf", [P, 2, N, PACK], BF16)
-        for part in range(2):
-            nc.vector.tensor_tensor(v_bf[:, part, :, :].rearrange("p (b i) t -> p b t i", i=PACK), v_raw[:, part, :, :].rearrange("p t (b i) -> p b t i", i=PACK),
-                                    u_sign[:].unsqueeze(1).unsqueeze(3).to_broadcast([P, N // PACK, PACK, PACK]), ALU.mult)
-        v_codes = sb("v_codes", [P, 2 * N], U32)
-        v_scales = sb("v_scales", [P, 2 * N], U8)
-
         power = [sb("power%d" % h, [P, PACK, HALF], F32) for h in range(2)]
         for c in range(CHUNKS):
             sq = sb("im_sq%d" % c, [P, PACK, CHUNK], F32)
             nc.scalar.activation(sq[:], im[c][:], ACT.Square)
             nc.vector.tensor_tensor(power[c // PER_HALF][:, :, in_half(c)], re_sq[c][:], sq[:], ALU.add)
-            if c == 0:
-                nc.vector.quantize_mx(out=v_codes[:].bitcast(FP8X4), scales=v_scales[:], in_=v_bf[:].rearrange("p a m t -> p (a m t)"))
 
         inv_root = [sb("inv_root%d" % h, [P, PACK, HALF], F32) for h in range(2)]
         least = [sb("least%d" % h, [P, PACK, GROUPS], F32) for h in range(2)]
@@ -155,7 +146,7 @@ def tile_picked_ysubtr_sub_p_kernel(tc, x_words, x_scales, wc, ws, unit, vc, vs,
         nc.scalar.activation(inv_root[1][:], power[1][:], ACT.Abs_reciprocal_sqrt, bias=POWER_OFFSET)
         least_power(0)
         noise_u2 = sb("noise_u2", [P, PACK, GROUPS], F32)
-        nc.vector.scalar_tensor_tensor(noise_u2[:], least[0][:], NOISE_FACTOR, u2_neg[:].unsqueeze(2).to_broadcast([P, PACK, GROUPS]), ALU.mult, ALU.mult)
+        nc.vector.scalar_tensor_tensor(noise_u2[:], least[0][:], NOISE_FACTOR, u2[:].unsqueeze(2).to_broadcast([P, PACK, GROUPS]), ALU.mult, ALU.mult)
         least_power(1)
         noise_inv_root = sb("noise_inv_root", [P, PACK, GROUPS], F32)
         nc.scalar.activation(noise_inv_root[:], least[1][:], ACT.Abs_reciprocal_sqrt, scale=NOISE_FACTOR, bias=guard[:])
@@ -166,44 +157,46 @@ def tile_picked_ysubtr_sub_p_kernel(tc, x_words, x_scales, wc, ws, unit, vc, vs,
                                     noise_u2[:, t:t + 2, :].unsqueeze(3).to_broadcast([P, 2, GROUPS, D]), ALU.mult)
         noise_root = sb("noise_root", [P, PACK, GROUPS], F32)
         nc.vector.scalar_tensor_tensor(noise_root[:], least[1][:], NOISE_FACTOR, noise_inv_root[:], ALU.mult, ALU.mult)
-        runs = CHUNK // D
-
-        def root_ratio(engine, w, c):
-            engine.tensor_tensor(by_runs(w), by_runs(inv_root[1][:, :, in_half(c)]),
-                                 noise_root[:, :, c * runs:(c + 1) * runs].unsqueeze(3).to_broadcast([P, PACK, runs, D]), ALU.mult)
-
-        def clip(dst, w):
-            nc.gpsimd.tensor_scalar(dst, w, 1.0, 0.0, ALU.min, ALU.max)
-
         neg_gain2 = sb("neg_gain2", [P, PACK, HALF], F32)
         for t in range(PACK):
-            nc.vector.tensor_scalar(neg_gain2[:, t, :], ratio_u2[:, t, :], u2_neg[:, t:t + 1], u2_top[:, t:t + 1], ALU.max, ALU.add)
+            nc.vector.tensor_scalar(neg_gain2[:, t, :], ratio_u2[:, t, :], u2[:, t:t + 1], u2_top[:, t:t + 1], ALU.min, ALU.subtract)
 
-        third = sb("third", [P, PACK, CHUNK], F32)
-        root_ratio(nc.vector, third[:], 0)
-        clipped = [sb("clipped%d" % c, [P, PACK, CHUNK], F32) for c in range(PER_HALF)]
-        clip(clipped[0][:], third[:])
-        fourth = sb("fourth", [P, PACK, CHUNK], F32, tag="third")
-        root_ratio(nc.gpsimd, fourth[:], 1)
-        clip(clipped[1][:], fourth[:])
+        root_ratio = []
+        runs = CHUNK // D
+        for c in range(PER_HALF):
+            w = sb("root_ratio%d" % c, [P, PACK, CHUNK], F32)
+            nc.vector.tensor_tensor(by_runs(w[:]), by_runs(inv_root[1][:, :, in_half(c)]),
+                                    noise_root[:, :, c * runs:(c + 1) * runs].unsqueeze(3).to_broadcast([P, PACK, runs, D]), ALU.mult)
+            root_ratio.append(w)
+
+        v_bf = sb("v_bf", [P, 2, N, PACK], BF16, tag="inv_root1")
+        for part in range(2):
+            nc.gpsimd.tensor_tensor(v_bf[:, part, :, :].rearrange("p (b i) t -> p b t i", i=PACK), v_raw[:, part, :, :].rearrange("p t (b i) -> p b t i", i=PACK),
+                                    u_sign[:].unsqueeze(1).unsqueeze(3).to_broadcast([P, N // PACK, PACK, PACK]), ALU.mult)
 
         gain = [sb("gain%d" % c, [P, PACK * CHUNK], F32) for c in range(CHUNKS)]
+        late_ratio = [sb("late_ratio%d" % c, [P, PACK, CHUNK], F32) for c in range(PER_HALF)]
 
         def early_gain(c):
             nc.scalar.activation(gain[c][:].rearrange("p (b e t) -> p b t e", e=PAIR, t=PACK),
-                                 neg_gain2[:, :, in_half(c)].rearrange("p t (b e) -> p b t e", e=PAIR), ACT.Sqrt)
+                                 neg_gain2[:, :, in_half(c)].rearrange("p t (b e) -> p b t e", e=PAIR), ACT.Sqrt, scale=-1.0)
+
+        def square_ratio(c):
+            nc.scalar.activation(late_ratio[c][:], root_ratio[c][:], ACT.Square)
 
         def late_gain(c):
-            late_ratio = sb("late_ratio%d" % c, [P, PACK, CHUNK], F32, tag="late_ratio")
-            nc.scalar.activation(late_ratio[:], clipped[c][:], ACT.Square)
+            kept = sb("kept%d" % c, [P, PACK, CHUNK], F32)
+            nc.scalar.activation(kept[:], late_ratio[c][:], ACT.Relu, scale=-1.0, bias=1.0)
             for t in range(PACK):
-                nc.scalar.activation(gain[PER_HALF + c][:, t * CHUNK:(t + 1) * CHUNK], late_ratio[:, t, :], ACT.Sqrt,
-                                     scale=u2_neg[:, t:t + 1], bias=u2_top[:, t:t + 1])
+                nc.scalar.activation(gain[PER_HALF + c][:, t * CHUNK:(t + 1) * CHUNK], kept[:, t, :], ACT.Sqrt,
+                                     scale=u2[:, t:t + 1], bias=u2_floor[:, t:t + 1])
 
-        for c in range(PER_HALF):
-            early_gain(c)
-        for c in range(PER_HALF):
-            late_gain(c)
+        early_gain(0)
+        square_ratio(0)
+        early_gain(1)
+        late_gain(0)
+        square_ratio(1)
+        late_gain(1)
 
         z = sb("z", [P, 2 * CHUNKS, CHUNK, PACK], BF16)
         z_codes = sb("z_codes", [P, 2 * S], U32)
@@ -227,11 +220,13 @@ def tile_picked_ysubtr_sub_p_kernel(tc, x_words, x_scales, wc, ws, unit, vc, vs,
             weigh(c)
         quantize_strips(0, 2 * PER_HALF)
         quantize_strips(2 * PER_HALF, 2 * last)
+        v_codes = sb("v_codes", [P, 2 * N], U32, tag="gain%d" % (last - 1))
+        v_scales = sb("v_scales", [P, 2 * N], U8)
+        nc.vector.quantize_mx(out=v_codes[:].bitcast(FP8X4), scales=v_scales[:], in_=v_bf[:].rearrange("p a m t -> p (a m t)"))
         weigh(last)
         quantize_strips(2 * last, 2 * last + 1)
         quantize_strips(2 * last + 1, 2 * last + 2)
 
-        result = sb("result", [P, CHUNKS, CHUNK], F32, tag="late_ratio")
         for c in range(CHUNKS):
             acc = psum.tile([P, CHUNK], F32, name="acc%d" % c, tag="re%d" % c)
             for part in range(2):
@@ -239,5 +234,6 @@ def tile_picked_ysubtr_sub_p_kernel(tc, x_words, x_scales, wc, ws, unit, vc, vs,
                 rows = slice(part * N, (part + 1) * N)
                 nc.tensor.matmul_mx(out=acc[:], lhsT=v_codes[:, rows].bitcast(FP8X4), lhsT_scale=v_scales[:, rows],
                                     rhs=z_codes[:, cols].bitcast(FP8X4), rhs_scale=z_scales[:, cols], start=(part == 0), stop=(part == 1))
-            nc.scalar.copy(result[:, c, :], acc[:])
-            nc.sync.dma_start(out=out[:, c * CHUNK:(c + 1) * CHUNK], in_=result[:, c, :])
+            result = sb("result%d" % c, [P, CHUNK], F32)
+            nc.scalar.copy(result[:], acc[:])
+            nc.sync.dma_start(out=out[:, c * CHUNK:(c + 1) * CHUNK], in_=result[:])

@@ -128,11 +128,28 @@ def tile_picked_ysubtr_sub_p_kernel(tc, x_words, x_scales, wc, ws, unit, vc, vs,
 
         im = [first_product("im", ws_codes, ws_scales, c) for c in range(CHUNKS)]
 
+        v_codes, v_scales = [], []
+
+        def sign_and_round(engine, part, tag):
+            v_bf = sb("v_bf%d" % part, [P, N, PACK], BF16, tag=tag)
+            engine.tensor_tensor(v_bf[:].rearrange("p (b i) t -> p b t i", i=PACK), v_raw[:, part, :, :].rearrange("p t (b i) -> p b t i", i=PACK),
+                                 u_sign[:].unsqueeze(1).unsqueeze(3).to_broadcast([P, N // PACK, PACK, PACK]), ALU.mult)
+            return v_bf
+
+        def quantize_v(part, v_bf, tag=None):
+            v_codes.append(sb("v_codes%d" % part, [P, N], U32, tag=tag))
+            v_scales.append(sb("v_scales%d" % part, [P, N], U8))
+            nc.vector.quantize_mx(out=v_codes[part][:].bitcast(FP8X4), scales=v_scales[part][:], in_=v_bf[:].rearrange("p m t -> p (m t)"))
+
+        vc_bf = sign_and_round(nc.vector, 0, tag="ws_bf")
+
         power = [sb("power%d" % h, [P, PACK, HALF], F32) for h in range(2)]
         for c in range(CHUNKS):
             sq = sb("im_sq%d" % c, [P, PACK, CHUNK], F32)
             nc.scalar.activation(sq[:], im[c][:], ACT.Square)
             nc.vector.tensor_tensor(power[c // PER_HALF][:, :, in_half(c)], re_sq[c][:], sq[:], ALU.add)
+            if c == 0:
+                quantize_v(0, vc_bf)
 
         inv_root = [sb("inv_root%d" % h, [P, PACK, HALF], F32) for h in range(2)]
         least = [sb("least%d" % h, [P, PACK, GROUPS], F32) for h in range(2)]
@@ -169,10 +186,7 @@ def tile_picked_ysubtr_sub_p_kernel(tc, x_words, x_scales, wc, ws, unit, vc, vs,
                                     noise_root[:, :, c * runs:(c + 1) * runs].unsqueeze(3).to_broadcast([P, PACK, runs, D]), ALU.mult)
             root_ratio.append(w)
 
-        v_bf = sb("v_bf", [P, 2, N, PACK], BF16, tag="inv_root1")
-        for part in range(2):
-            nc.gpsimd.tensor_tensor(v_bf[:, part, :, :].rearrange("p (b i) t -> p b t i", i=PACK), v_raw[:, part, :, :].rearrange("p t (b i) -> p b t i", i=PACK),
-                                    u_sign[:].unsqueeze(1).unsqueeze(3).to_broadcast([P, N // PACK, PACK, PACK]), ALU.mult)
+        vs_bf = sign_and_round(nc.gpsimd, 1, tag="inv_root1")
 
         gain = [sb("gain%d" % c, [P, PACK * CHUNK], F32) for c in range(CHUNKS)]
         late_ratio = [sb("late_ratio%d" % c, [P, PACK, CHUNK], F32) for c in range(PER_HALF)]
@@ -220,9 +234,7 @@ def tile_picked_ysubtr_sub_p_kernel(tc, x_words, x_scales, wc, ws, unit, vc, vs,
             weigh(c)
         quantize_strips(0, 2 * PER_HALF)
         quantize_strips(2 * PER_HALF, 2 * last)
-        v_codes = sb("v_codes", [P, 2 * N], U32, tag="gain%d" % (last - 1))
-        v_scales = sb("v_scales", [P, 2 * N], U8)
-        nc.vector.quantize_mx(out=v_codes[:].bitcast(FP8X4), scales=v_scales[:], in_=v_bf[:].rearrange("p a m t -> p (a m t)"))
+        quantize_v(1, vs_bf, tag="gain%d" % (last - 1))
         weigh(last)
         quantize_strips(2 * last, 2 * last + 1)
         quantize_strips(2 * last + 1, 2 * last + 2)
@@ -231,8 +243,7 @@ def tile_picked_ysubtr_sub_p_kernel(tc, x_words, x_scales, wc, ws, unit, vc, vs,
             acc = psum.tile([P, CHUNK], F32, name="acc%d" % c, tag="re%d" % c)
             for part in range(2):
                 cols = slice((2 * c + part) * CHUNK, (2 * c + part + 1) * CHUNK)
-                rows = slice(part * N, (part + 1) * N)
-                nc.tensor.matmul_mx(out=acc[:], lhsT=v_codes[:, rows].bitcast(FP8X4), lhsT_scale=v_scales[:, rows],
+                nc.tensor.matmul_mx(out=acc[:], lhsT=v_codes[part][:].bitcast(FP8X4), lhsT_scale=v_scales[part][:],
                                     rhs=z_codes[:, cols].bitcast(FP8X4), rhs_scale=z_scales[:, cols], start=(part == 0), stop=(part == 1))
             result = sb("result%d" % c, [P, CHUNK], F32)
             nc.scalar.copy(result[:], acc[:])

@@ -29,6 +29,8 @@ WS_COLS = H // 2
 WS_ROWS = P // 2
 SCALAR_ROWS = 96
 
+FIRST_FRAMES = 48
+
 POWER_OFFSET, NOISE_FACTOR, GAIN_FLOOR = 0.05, 1.5, 0.02
 
 
@@ -92,6 +94,8 @@ def tile_picked_ysubtr_sub_p_kernel(tc, x_words, x_scales, wc, ws, unit, vc, vs,
         nc.scalar.activation(u_sign[:], u, ACT.Sign)
         u2_top = sb("u2_top", [P, PACK], F32)
         nc.scalar.activation(u2_top[:], u2[:], ACT.Copy, scale=1.02)
+        u2_neg = sb("u2_neg", [P, PACK], F32)
+        nc.scalar.activation(u2_neg[:], u2[:], ACT.Copy, scale=-1.0)
         u2_floor = sb("u2_floor", [P, PACK], F32)
         nc.scalar.activation(u2_floor[:], u2[:], ACT.Copy, scale=GAIN_FLOOR)
 
@@ -157,9 +161,12 @@ def tile_picked_ysubtr_sub_p_kernel(tc, x_words, x_scales, wc, ws, unit, vc, vs,
         def least_power(h):
             nc.vector.tensor_reduce(least[h][:], by_runs(power[h][:]), AX.X, ALU.min)
 
-        nc.scalar.activation(inv_root[0][:], power[0][:], ACT.Abs_reciprocal_sqrt, bias=POWER_OFFSET)
         inv_power = sb("inv_power", [P, PACK, HALF], F32)
-        nc.scalar.activation(inv_power[:], inv_root[0][:], ACT.Square)
+        plane_pairs = (slice(0, PAIR), slice(PAIR, PACK))
+        for planes in plane_pairs:
+            nc.scalar.activation(inv_root[0][:, planes, :], power[0][:, planes, :], ACT.Abs_reciprocal_sqrt, bias=POWER_OFFSET)
+        for planes in plane_pairs:
+            nc.scalar.activation(inv_power[:, planes, :], inv_root[0][:, planes, :], ACT.Square)
         nc.scalar.activation(inv_root[1][:], power[1][:], ACT.Abs_reciprocal_sqrt, bias=POWER_OFFSET)
         least_power(0)
         noise_u2 = sb("noise_u2", [P, PACK, GROUPS], F32)
@@ -178,39 +185,44 @@ def tile_picked_ysubtr_sub_p_kernel(tc, x_words, x_scales, wc, ws, unit, vc, vs,
         for t in range(PACK):
             nc.vector.tensor_scalar(neg_gain2[:, t, :], ratio_u2[:, t, :], u2[:, t:t + 1], u2_top[:, t:t + 1], ALU.min, ALU.subtract)
 
-        root_ratio = []
         runs = CHUNK // D
-        for c in range(PER_HALF):
-            w = sb("root_ratio%d" % c, [P, PACK, CHUNK], F32)
-            nc.vector.tensor_tensor(by_runs(w[:]), by_runs(inv_root[1][:, :, in_half(c)]),
-                                    noise_root[:, :, c * runs:(c + 1) * runs].unsqueeze(3).to_broadcast([P, PACK, runs, D]), ALU.mult)
-            root_ratio.append(w)
 
+        def root_ratio(engine, w, c):
+            engine.tensor_tensor(by_runs(w[:]), by_runs(inv_root[1][:, :, in_half(c)]),
+                                 noise_root[:, :, c * runs:(c + 1) * runs].unsqueeze(3).to_broadcast([P, PACK, runs, D]), ALU.mult)
+
+        third = sb("third", [P, PACK, CHUNK], F32)
+        root_ratio(nc.vector, third, 0)
+        clipped = sb("clipped", [P, PACK, CHUNK], F32)
+        nc.gpsimd.tensor_scalar(clipped[:], third[:], 1.0, 0.0, ALU.min, ALU.max)
+        fourth = sb("fourth", [P, PACK, CHUNK], F32, tag="third")
+        root_ratio(nc.gpsimd, fourth, 1)
         vs_bf = sign_and_round(nc.gpsimd, 1, tag="inv_root1")
 
         gain = [sb("gain%d" % c, [P, PACK * CHUNK], F32) for c in range(CHUNKS)]
-        late_ratio = [sb("late_ratio%d" % c, [P, PACK, CHUNK], F32) for c in range(PER_HALF)]
 
-        def early_gain(c):
-            nc.scalar.activation(gain[c][:].rearrange("p (b e t) -> p b t e", e=PAIR, t=PACK),
-                                 neg_gain2[:, :, in_half(c)].rearrange("p t (b e) -> p b t e", e=PAIR), ACT.Sqrt, scale=-1.0)
+        def early_gain(c, first, count):
+            nc.scalar.activation(gain[c][:, PACK * first:PACK * (first + count)].rearrange("p (b e t) -> p b t e", e=PAIR, t=PACK),
+                                 neg_gain2[:, :, c * CHUNK + first:c * CHUNK + first + count].rearrange("p t (b e) -> p b t e", e=PAIR), ACT.Sqrt, scale=-1.0)
 
-        def square_ratio(c):
-            nc.scalar.activation(late_ratio[c][:], root_ratio[c][:], ACT.Square)
-
-        def late_gain(c):
-            kept = sb("kept%d" % c, [P, PACK, CHUNK], F32)
-            nc.scalar.activation(kept[:], late_ratio[c][:], ACT.Relu, scale=-1.0, bias=1.0)
+        def root_by_planes(c, source, scale, bias):
             for t in range(PACK):
-                nc.scalar.activation(gain[PER_HALF + c][:, t * CHUNK:(t + 1) * CHUNK], kept[:, t, :], ACT.Sqrt,
-                                     scale=u2[:, t:t + 1], bias=u2_floor[:, t:t + 1])
+                nc.scalar.activation(gain[c][:, t * CHUNK:(t + 1) * CHUNK], source[:, t, :], ACT.Sqrt, scale=scale[:, t:t + 1], bias=bias[:, t:t + 1])
 
-        early_gain(0)
-        square_ratio(0)
-        early_gain(1)
-        late_gain(0)
-        square_ratio(1)
-        late_gain(1)
+        early_gain(0, 0, FIRST_FRAMES)
+        early_gain(0, FIRST_FRAMES, CHUNK - FIRST_FRAMES)
+        early_gain(1, 0, CHUNK)
+        third_sq = sb("third_sq", [P, PACK, CHUNK], F32)
+        for planes in (slice(0, PAIR), slice(PAIR, PACK)):
+            nc.scalar.activation(third_sq[:, planes, :], clipped[:, planes, :], ACT.Square)
+        root_by_planes(2, third_sq, u2_neg, u2_top)
+        fourth_sq = sb("fourth_sq", [P, PACK, CHUNK], F32, tag="third_sq")
+        for planes in (slice(0, PAIR), slice(PAIR, PACK)):
+            nc.scalar.activation(fourth_sq[:, planes, :], fourth[:, planes, :], ACT.Square)
+        kept = sb("kept", [P, PACK, CHUNK], F32)
+        for planes in (slice(0, PAIR), slice(PAIR, PACK)):
+            nc.scalar.activation(kept[:, planes, :], fourth_sq[:, planes, :], ACT.Relu, scale=-1.0, bias=1.0)
+        root_by_planes(3, kept, u2, u2_floor)
 
         z = sb("z", [P, 2 * CHUNKS, CHUNK, PACK], BF16)
         z_codes = sb("z_codes", [P, 2 * S], U32)
@@ -220,7 +232,10 @@ def tile_picked_ysubtr_sub_p_kernel(tc, x_words, x_scales, wc, ws, unit, vc, vs,
             for part, bank in enumerate((re[c], im[c])):
                 strip = z[:, 2 * c + part, :, :]
                 if c < PER_HALF:
-                    nc.vector.tensor_tensor(strip, bank[:].rearrange("p t n -> p n t"), gain[c][:].rearrange("p (n t) -> p n t", t=PACK), ALU.mult)
+                    cuts = (0, FIRST_FRAMES, CHUNK) if (c, part) == (0, 0) else (0, CHUNK)
+                    for first, end in zip(cuts, cuts[1:]):
+                        nc.vector.tensor_tensor(strip[:, first:end, :], bank[:, :, first:end].rearrange("p t n -> p n t"),
+                                                gain[c][:, PACK * first:PACK * end].rearrange("p (n t) -> p n t", t=PACK), ALU.mult)
                 else:
                     nc.vector.tensor_tensor(strip.rearrange("p (b e) t -> p b t e", e=PAIR), bank[:].rearrange("p t (b e) -> p b t e", e=PAIR),
                                             gain[c][:].rearrange("p (t b e) -> p b t e", t=PACK, e=PAIR), ALU.mult)

@@ -124,8 +124,10 @@ def tile_picked_ysubtr_sub_p_kernel(tc, x_words, x_scales, wc, ws, unit, vc, vs,
         ws_codes = sb("ws_codes", [P, H], U32)
         ws_scales = sb("ws_scales", [P, H], U8)
         ws_bf = sb("ws_bf", [P, PACK, P, PACK], BF16)
-        for h in range(2):
-            round_and_deal(nc.vector.tensor_copy, ws_raw[h][:], ws_bf[:, :, h * WS_ROWS:(h + 1) * WS_ROWS, :])
+        round_and_deal(nc.vector.tensor_copy, ws_raw[0][:], ws_bf[:, :, 0:WS_ROWS, :])
+        for t in range(0, PACK, 2):
+            nc.vector.tensor_copy(ws_bf[:, t:t + 2, WS_ROWS:P, :].rearrange("p t m j -> p m j t"),
+                                  ws_raw[1][:].rearrange("p j (m t) -> p m j t", t=PACK)[:, :, :, t:t + 2])
         for t in range(0, PACK, 2):
             cols = slice(t * P, (t + 2) * P)
             nc.vector.quantize_mx(out=ws_codes[:, cols].bitcast(FP8X4), scales=ws_scales[:, cols], in_=ws_bf[:, t:t + 2, :, :].rearrange("p t m j -> p (t m j)"))
@@ -158,8 +160,8 @@ def tile_picked_ysubtr_sub_p_kernel(tc, x_words, x_scales, wc, ws, unit, vc, vs,
         inv_root = [sb("inv_root%d" % h, [P, PACK, HALF], F32) for h in range(2)]
         least = [sb("least%d" % h, [P, PACK, GROUPS], F32) for h in range(2)]
 
-        def least_power(h):
-            nc.vector.tensor_reduce(least[h][:], by_runs(power[h][:]), AX.X, ALU.min)
+        def least_power(h, first, count):
+            nc.vector.tensor_reduce(least[h][:, :, first // D:(first + count) // D], by_runs(power[h][:, :, first:first + count]), AX.X, ALU.min)
 
         inv_power = sb("inv_power", [P, PACK, HALF], F32)
         plane_pairs = (slice(0, PAIR), slice(PAIR, PACK))
@@ -168,10 +170,11 @@ def tile_picked_ysubtr_sub_p_kernel(tc, x_words, x_scales, wc, ws, unit, vc, vs,
         for planes in plane_pairs:
             nc.scalar.activation(inv_power[:, planes, :], inv_root[0][:, planes, :], ACT.Square)
         nc.scalar.activation(inv_root[1][:], power[1][:], ACT.Abs_reciprocal_sqrt, bias=POWER_OFFSET)
-        least_power(0)
+        least_power(0, 0, HALF)
         noise_u2 = sb("noise_u2", [P, PACK, GROUPS], F32)
         nc.vector.scalar_tensor_tensor(noise_u2[:], least[0][:], NOISE_FACTOR, u2[:].unsqueeze(2).to_broadcast([P, PACK, GROUPS]), ALU.mult, ALU.mult)
-        least_power(1)
+        for c in range(PER_HALF):
+            least_power(1, c * CHUNK, CHUNK)
         noise_inv_root = sb("noise_inv_root", [P, PACK, GROUPS], F32)
         nc.scalar.activation(noise_inv_root[:], least[1][:], ACT.Abs_reciprocal_sqrt, scale=NOISE_FACTOR, bias=guard[:])
 

@@ -148,6 +148,8 @@ def tile_picked_ysubtr_sub_p_kernel(tc, x_words, x_scales, wc, ws, unit, vc, vs,
             nc.vector.quantize_mx(out=v_codes[part][:].bitcast(FP8X4), scales=v_scales[part][:], in_=v_bf[:].rearrange("p m t -> p (m t)"))
 
         vc_bf = sign_and_round(nc.vector, 0, tag="ws_bf")
+        vs_bf = sign_and_round(nc.vector, 1, tag="ws_raw1")
+        quantize_v(0, vc_bf)
 
         power = [sb("power%d" % h, [P, PACK, HALF], F32) for h in range(2)]
         for c in range(CHUNKS):
@@ -155,7 +157,7 @@ def tile_picked_ysubtr_sub_p_kernel(tc, x_words, x_scales, wc, ws, unit, vc, vs,
             nc.scalar.activation(sq[:], im[c][:], ACT.Square)
             nc.vector.tensor_tensor(power[c // PER_HALF][:, :, in_half(c)], re_sq[c][:], sq[:], ALU.add)
             if c == 0:
-                quantize_v(0, vc_bf)
+                quantize_v(1, vs_bf)
 
         inv_root = [sb("inv_root%d" % h, [P, PACK, HALF], F32) for h in range(2)]
         least = [sb("least%d" % h, [P, PACK, GROUPS], F32) for h in range(2)]
@@ -200,7 +202,9 @@ def tile_picked_ysubtr_sub_p_kernel(tc, x_words, x_scales, wc, ws, unit, vc, vs,
         nc.gpsimd.tensor_scalar(clipped[:], third[:], 1.0, 0.0, ALU.min, ALU.max)
         fourth = sb("fourth", [P, PACK, CHUNK], F32, tag="third")
         root_ratio(nc.gpsimd, fourth, 1)
-        vs_bf = sign_and_round(nc.gpsimd, 1, tag="inv_root1")
+        by_gpsimd, by_scalar = plane_pairs
+        clipped_last = sb("clipped_last", [P, PAIR, CHUNK], F32)
+        nc.gpsimd.tensor_scalar(clipped_last[:], fourth[:, by_gpsimd, :], 1.0, 0.0, ALU.min, ALU.max)
 
         gain = [sb("gain%d" % c, [P, PACK * CHUNK], F32) for c in range(CHUNKS)]
 
@@ -208,8 +212,8 @@ def tile_picked_ysubtr_sub_p_kernel(tc, x_words, x_scales, wc, ws, unit, vc, vs,
             nc.scalar.activation(gain[c][:, PACK * first:PACK * (first + count)].rearrange("p (b e t) -> p b t e", e=PAIR, t=PACK),
                                  neg_gain2[:, :, c * CHUNK + first:c * CHUNK + first + count].rearrange("p t (b e) -> p b t e", e=PAIR), ACT.Sqrt, scale=-1.0)
 
-        def root_by_planes(c, source, scale, bias):
-            for t in range(PACK):
+        def root_by_planes(c, source, scale, bias, planes):
+            for t in range(planes.start, planes.stop):
                 nc.scalar.activation(gain[c][:, t * CHUNK:(t + 1) * CHUNK], source[:, t, :], ACT.Sqrt, scale=scale[:, t:t + 1], bias=bias[:, t:t + 1])
 
         early_gain(0, 0, FIRST_FRAMES)
@@ -218,14 +222,14 @@ def tile_picked_ysubtr_sub_p_kernel(tc, x_words, x_scales, wc, ws, unit, vc, vs,
         third_sq = sb("third_sq", [P, PACK, CHUNK], F32)
         for planes in (slice(0, PAIR), slice(PAIR, PACK)):
             nc.scalar.activation(third_sq[:, planes, :], clipped[:, planes, :], ACT.Square)
-        root_by_planes(2, third_sq, u2_neg, u2_top)
-        fourth_sq = sb("fourth_sq", [P, PACK, CHUNK], F32, tag="third_sq")
-        for planes in (slice(0, PAIR), slice(PAIR, PACK)):
-            nc.scalar.activation(fourth_sq[:, planes, :], fourth[:, planes, :], ACT.Square)
+        root_by_planes(2, third_sq, u2_neg, u2_top, slice(0, PACK))
+        fourth_sq = sb("fourth_sq", [P, PACK, CHUNK], F32)
         kept = sb("kept", [P, PACK, CHUNK], F32)
-        for planes in (slice(0, PAIR), slice(PAIR, PACK)):
-            nc.scalar.activation(kept[:, planes, :], fourth_sq[:, planes, :], ACT.Relu, scale=-1.0, bias=1.0)
-        root_by_planes(3, kept, u2, u2_floor)
+        nc.scalar.activation(fourth_sq[:, by_scalar, :], fourth[:, by_scalar, :], ACT.Square)
+        nc.scalar.activation(fourth_sq[:, by_gpsimd, :], clipped_last[:], ACT.Square)
+        nc.scalar.activation(kept[:, by_scalar, :], fourth_sq[:, by_scalar, :], ACT.Relu, scale=-1.0, bias=1.0)
+        root_by_planes(3, fourth_sq, u2_neg, u2_top, by_gpsimd)
+        root_by_planes(3, kept, u2, u2_floor, by_scalar)
 
         z = sb("z", [P, 2 * CHUNKS, CHUNK, PACK], BF16)
         z_codes = sb("z_codes", [P, 2 * S], U32)
@@ -252,17 +256,16 @@ def tile_picked_ysubtr_sub_p_kernel(tc, x_words, x_scales, wc, ws, unit, vc, vs,
             weigh(c)
         quantize_strips(0, 2 * PER_HALF)
         quantize_strips(2 * PER_HALF, 2 * last)
-        quantize_v(1, vs_bf, tag="gain%d" % (last - 1))
         weigh(last)
         quantize_strips(2 * last, 2 * last + 1)
         quantize_strips(2 * last + 1, 2 * last + 2)
 
+        result = sb("result", [P, CHUNKS, CHUNK], F32, tag="kept")
         for c in range(CHUNKS):
             acc = psum.tile([P, CHUNK], F32, name="acc%d" % c, tag="re%d" % c)
             for part in range(2):
                 cols = slice((2 * c + part) * CHUNK, (2 * c + part + 1) * CHUNK)
                 nc.tensor.matmul_mx(out=acc[:], lhsT=v_codes[part][:].bitcast(FP8X4), lhsT_scale=v_scales[part][:],
                                     rhs=z_codes[:, cols].bitcast(FP8X4), rhs_scale=z_scales[:, cols], start=(part == 0), stop=(part == 1))
-            result = sb("result%d" % c, [P, CHUNK], F32)
-            nc.scalar.copy(result[:], acc[:])
-            nc.sync.dma_start(out=out[:, c * CHUNK:(c + 1) * CHUNK], in_=result[:])
+            nc.scalar.copy(result[:, c, :], acc[:])
+            nc.sync.dma_start(out=out[:, c * CHUNK:(c + 1) * CHUNK], in_=result[:, c, :])

@@ -27,7 +27,7 @@ PER_HALF = HALF // CHUNK
 GROUPS = HALF // D
 WS_COLS = H // 2
 WS_ROWS = P // 2
-SCALAR_ROWS = 96
+SCALAR_ROWS = 80
 
 FIRST_FRAMES = 48
 

@@ -209,8 +209,8 @@ def tile_picked_ysubtr_sub_p_kernel(tc, x_words, x_scales, wc, ws, unit, vc, vs,
         gain = [sb("gain%d" % c, [P, PACK * CHUNK], F32) for c in range(CHUNKS)]
 
         def early_gain(c, first, count):
-            nc.scalar.activation(gain[c][:, PACK * first:PACK * (first + count)].rearrange("p (b e t) -> p b t e", e=PAIR, t=PACK),
-                                 neg_gain2[:, :, c * CHUNK + first:c * CHUNK + first + count].rearrange("p t (b e) -> p b t e", e=PAIR), ACT.Sqrt, scale=-1.0)
+            nc.scalar.activation(gain[c][:].rearrange("p (t n) -> p t n", t=PACK)[:, :, first:first + count],
+                                 neg_gain2[:, :, c * CHUNK + first:c * CHUNK + first + count], ACT.Sqrt, scale=-1.0)
 
         def root_by_planes(c, source, scale, bias, planes):
             for t in range(planes.start, planes.stop):
@@ -238,14 +238,11 @@ def tile_picked_ysubtr_sub_p_kernel(tc, x_words, x_scales, wc, ws, unit, vc, vs,
         def weigh(c):
             for part, bank in enumerate((re[c], im[c])):
                 strip = z[:, 2 * c + part, :, :]
-                if c < PER_HALF:
-                    cuts = (0, FIRST_FRAMES, CHUNK) if (c, part) == (0, 0) else (0, CHUNK)
-                    for first, end in zip(cuts, cuts[1:]):
-                        nc.vector.tensor_tensor(strip[:, first:end, :], bank[:, :, first:end].rearrange("p t n -> p n t"),
-                                                gain[c][:, PACK * first:PACK * end].rearrange("p (n t) -> p n t", t=PACK), ALU.mult)
-                else:
-                    nc.vector.tensor_tensor(strip.rearrange("p (b e) t -> p b t e", e=PAIR), bank[:].rearrange("p t (b e) -> p b t e", e=PAIR),
-                                            gain[c][:].rearrange("p (t b e) -> p b t e", t=PACK, e=PAIR), ALU.mult)
+                cuts = (0, FIRST_FRAMES, CHUNK) if (c, part) == (0, 0) else (0, CHUNK)
+                for first, end in zip(cuts, cuts[1:]):
+                    nc.vector.tensor_tensor(strip[:, first:end, :].rearrange("p (b e) t -> p b t e", e=PAIR),
+                                            bank[:, :, first:end].rearrange("p t (b e) -> p b t e", e=PAIR),
+                                            gain[c][:].rearrange("p (t n) -> p t n", t=PACK)[:, :, first:end].rearrange("p t (b e) -> p b t e", e=PAIR), ALU.mult)
 
         def quantize_strips(first, last):
             cols = slice(first * CHUNK, last * CHUNK)

@@ -1,6 +1,7 @@
 from contextlib import ExitStack
 
 import concourse.mybir as mybir
+from concourse.masks import make_identity
 
 F32 = mybir.dt.float32
 BF16 = mybir.dt.bfloat16
@@ -76,6 +77,9 @@ def tile_picked_ysubtr_sub_p_kernel(tc, x_words, x_scales, wc, ws, unit, vc, vs,
         guard = sb("guard", [P, 1], F32)
         nc.scalar.activation(guard[:], huge[:], ACT.Abs_reciprocal_sqrt)
 
+        identity = sb("identity", [P, P], F32)
+        make_identity(nc, identity[:])
+
         def round_and_deal(copy, raw, grouped):
             copy(grouped.rearrange("p t m j -> p m j t"), raw.rearrange("p j (m t) -> p m j t", t=PACK))
 
@@ -105,8 +109,14 @@ def tile_picked_ysubtr_sub_p_kernel(tc, x_words, x_scales, wc, ws, unit, vc, vs,
             nc.vector.tensor_copy(picked[:], words_all[:].bitcast(U32).indirect(offsets[:, h * HALF // 16:(h + 1) * HALF // 16]))
             x_codes.append(picked)
 
-        def first_product(name, codes, scales, c):
-            bank = psum.tile([P, PACK, CHUNK], F32, name="%s%d" % (name, c), tag="%s%d" % (name, c))
+        def turned_square(name, codes, scales, c):
+            bank = psum.tile([P, H], F32, name="%s_turned" % name, tag="%s%d" % (name, c))
+            nc.tensor.matmul_mx(out=bank[:], lhsT=x_codes[c // PER_HALF][:, in_half(c)].bitcast(FP8X4), lhsT_scale=x_bytes[:, c * CHUNK:(c + 1) * CHUNK],
+                                rhs=codes[:].bitcast(FP8X4), rhs_scale=scales[:], start=True, stop=True)
+            return bank
+
+        def first_product(name, codes, scales, c, tag=None):
+            bank = psum.tile([P, PACK, CHUNK], F32, name="%s%d" % (name, c), tag=tag or "%s%d" % (name, c))
             for t in range(PACK):
                 plane = slice(t * P, (t + 1) * P)
                 nc.tensor.matmul_mx(out=bank[:, t, :], lhsT=codes[:, plane].bitcast(FP8X4), lhsT_scale=scales[:, plane],
@@ -114,12 +124,16 @@ def tile_picked_ysubtr_sub_p_kernel(tc, x_words, x_scales, wc, ws, unit, vc, vs,
                                     start=True, stop=True)
             return bank
 
-        re = [first_product("re", wc_codes, wc_scales, c) for c in range(CHUNKS)]
+        last = CHUNKS - 1
+        re = [first_product("re", wc_codes, wc_scales, c) for c in range(last)]
+        re_turned = turned_square("re", wc_codes, wc_scales, last)
         re_sq = []
-        for c in range(CHUNKS):
+        for c in range(last):
             sq = sb("re_sq%d" % c, [P, PACK, CHUNK], F32)
             nc.scalar.activation(sq[:], re[c][:], ACT.Square)
             re_sq.append(sq)
+        turned_sq = [sb("turned_sq%d" % part, [P, H], F32) for part in range(2)]
+        nc.scalar.activation(turned_sq[0][:], re_turned[:], ACT.Square)
 
         ws_codes = sb("ws_codes", [P, H], U32)
         ws_scales = sb("ws_scales", [P, H], U8)
@@ -132,7 +146,9 @@ def tile_picked_ysubtr_sub_p_kernel(tc, x_words, x_scales, wc, ws, unit, vc, vs,
             cols = slice(t * P, (t + 2) * P)
             nc.vector.quantize_mx(out=ws_codes[:, cols].bitcast(FP8X4), scales=ws_scales[:, cols], in_=ws_bf[:, t:t + 2, :, :].rearrange("p t m j -> p (t m j)"))
 
-        im = [first_product("im", ws_codes, ws_scales, c) for c in range(CHUNKS)]
+        im = [first_product("im", ws_codes, ws_scales, c) for c in range(last)]
+        im_turned = turned_square("im", ws_codes, ws_scales, last)
+        im.append(first_product("im", ws_codes, ws_scales, last, tag="re%d" % last))
 
         v_codes, v_scales = [], []
 
@@ -151,19 +167,26 @@ def tile_picked_ysubtr_sub_p_kernel(tc, x_words, x_scales, wc, ws, unit, vc, vs,
         vs_bf = sign_and_round(nc.vector, 1, tag="ws_raw1")
         quantize_v(0, vc_bf)
 
-        power = [sb("power%d" % h, [P, PACK, HALF], F32) for h in range(2)]
-        for c in range(CHUNKS):
+        power = [sb("power0", [P, PACK, HALF], F32), sb("power1", [P, PACK, CHUNK], F32)]
+        for c in range(last):
             sq = sb("im_sq%d" % c, [P, PACK, CHUNK], F32)
             nc.scalar.activation(sq[:], im[c][:], ACT.Square)
             nc.vector.tensor_tensor(power[c // PER_HALF][:, :, in_half(c)], re_sq[c][:], sq[:], ALU.add)
             if c == 0:
                 quantize_v(1, vs_bf)
 
+        nc.scalar.activation(turned_sq[1][:], im_turned[:], ACT.Square)
+        last_power = psum.tile([P, PACK, CHUNK], F32, name="last_power", tag="im%d" % last)
+        for part in range(2):
+            for t in range(PACK):
+                nc.tensor.matmul(last_power[:, t, :], turned_sq[part][:, t * P:(t + 1) * P], identity[:], is_transpose=True,
+                                 start=(part, t) == (0, 0), stop=(part, t) == (1, PACK - 1))
+        late_power = (power[1], last_power)
+
         inv_root = [sb("inv_root%d" % h, [P, PACK, HALF], F32) for h in range(2)]
         least = [sb("least%d" % h, [P, PACK, GROUPS], F32) for h in range(2)]
 
-        def least_power(h, first, count):
-            nc.vector.tensor_reduce(least[h][:, :, first // D:(first + count) // D], by_runs(power[h][:, :, first:first + count]), AX.X, ALU.min)
+        runs = CHUNK // D
 
         inv_power = sb("inv_power", [P, PACK, HALF], F32)
         plane_pairs = (slice(0, PAIR), slice(PAIR, PACK))
@@ -171,12 +194,14 @@ def tile_picked_ysubtr_sub_p_kernel(tc, x_words, x_scales, wc, ws, unit, vc, vs,
             nc.scalar.activation(inv_root[0][:, planes, :], power[0][:, planes, :], ACT.Abs_reciprocal_sqrt, bias=POWER_OFFSET)
         for planes in plane_pairs:
             nc.scalar.activation(inv_power[:, planes, :], inv_root[0][:, planes, :], ACT.Square)
-        nc.scalar.activation(inv_root[1][:], power[1][:], ACT.Abs_reciprocal_sqrt, bias=POWER_OFFSET)
-        least_power(0, 0, HALF)
+        nc.vector.tensor_reduce(least[0][:], by_runs(power[0][:]), AX.X, ALU.min)
+        nc.vector.tensor_reduce(least[1][:, :, 0:runs], by_runs(late_power[0][:]), AX.X, ALU.min)
         noise_u2 = sb("noise_u2", [P, PACK, GROUPS], F32)
         nc.vector.scalar_tensor_tensor(noise_u2[:], least[0][:], NOISE_FACTOR, u2[:].unsqueeze(2).to_broadcast([P, PACK, GROUPS]), ALU.mult, ALU.mult)
+        nc.vector.tensor_reduce(least[1][:, :, runs:], by_runs(late_power[1][:]), AX.X, ALU.min)
         for c in range(PER_HALF):
-            least_power(1, c * CHUNK, CHUNK)
+            nc.scalar.activation(inv_root[1][:, :, in_half(c)], late_power[c][:], ACT.Abs_reciprocal_sqrt, bias=POWER_OFFSET)
+        re.append(first_product("re", wc_codes, wc_scales, last, tag="im%d" % last))
         noise_inv_root = sb("noise_inv_root", [P, PACK, GROUPS], F32)
         nc.scalar.activation(noise_inv_root[:], least[1][:], ACT.Abs_reciprocal_sqrt, scale=NOISE_FACTOR, bias=guard[:])
 
@@ -189,8 +214,6 @@ def tile_picked_ysubtr_sub_p_kernel(tc, x_words, x_scales, wc, ws, unit, vc, vs,
         neg_gain2 = sb("neg_gain2", [P, PACK, HALF], F32)
         for t in range(PACK):
             nc.vector.tensor_scalar(neg_gain2[:, t, :], ratio_u2[:, t, :], u2[:, t:t + 1], u2_top[:, t:t + 1], ALU.min, ALU.subtract)
-
-        runs = CHUNK // D
 
         def root_ratio(engine, w, c):
             engine.tensor_tensor(by_runs(w[:]), by_runs(inv_root[1][:, :, in_half(c)]),
@@ -248,7 +271,6 @@ def tile_picked_ysubtr_sub_p_kernel(tc, x_words, x_scales, wc, ws, unit, vc, vs,
             cols = slice(first * CHUNK, last * CHUNK)
             nc.vector.quantize_mx(out=z_codes[:, cols].bitcast(FP8X4), scales=z_scales[:, cols], in_=z[:, first:last, :, :].rearrange("p s n t -> p (s n t)"))
 
-        last = CHUNKS - 1
         for c in range(last):
             weigh(c)
         quantize_strips(0, 2 * PER_HALF)

@@ -23,16 +23,17 @@ PAIR = 2
 QUADRANT = 32
 CHUNK = 128
 CHUNKS = S // CHUNK
-HALF = S // 2
-PER_HALF = HALF // CHUNK
-GROUPS = HALF // D
+RUNS = CHUNK // D
+LIST_ROWS = 16
 WS_COLS = H // 2
 WS_ROWS = P // 2
 SCALAR_ROWS = 80
 
-FIRST_FRAMES = 48
-
 POWER_OFFSET, NOISE_FACTOR, GAIN_FLOOR = 0.05, 1.5, 0.02
+TOP = 1.02
+CEILING = 2.0 ** 90
+TURNED = 2
+TINY = 2.0 ** -80
 
 
 def tile_picked_ysubtr_sub_p_kernel(tc, x_words, x_scales, wc, ws, unit, vc, vs, offs, out):
@@ -44,13 +45,15 @@ def tile_picked_ysubtr_sub_p_kernel(tc, x_words, x_scales, wc, ws, unit, vc, vs,
         def sb(name, shape, dtype, tag=None):
             return keep.tile(shape, dtype, name=name, tag=tag or name, align_bytes=64)
 
-        def in_half(c):
-            return slice((c % PER_HALF) * CHUNK, (c % PER_HALF + 1) * CHUNK)
+        def planes_tile(name, tag=None):
+            return sb(name, [P, PACK, CHUNK], F32, tag=tag)
 
         def by_runs(ap):
-            return ap.rearrange("p t (v d) -> p t v d", d=D)
+            return ap.rearrange("p t (v d) -> p (t v) d", d=D)
 
-        offsets = keep.tile([P, S // 16], U16, name="offsets")
+        plane_pairs = (slice(0, PAIR), slice(PAIR, PACK))
+
+        offsets = keep.tile([P, S // LIST_ROWS], U16, name="offsets")
         wc_raw = sb("wc_raw", [P, PACK, H], F32)
         nc.sync.dma_start(out=wc_raw[:], in_=wc.rearrange("(p j) c -> p j c", j=PACK))
         nc.sync.dma_start(offsets[:], offs)
@@ -62,18 +65,19 @@ def tile_picked_ysubtr_sub_p_kernel(tc, x_words, x_scales, wc, ws, unit, vc, vs,
         nc.sync.dma_start(out=words_all[:], in_=x_words[0].rearrange("p n t -> p (n t)").bitcast(I32))
         unit_planes = sb("unit_planes", [P, PACK], F32)
         nc.sync.dma_start(out=unit_planes[:], in_=unit.rearrange("(p t) o -> p (t o)", t=PACK))
-        u = unit_planes[:]
         ws_raw = []
         for h in range(2):
             raw = sb("ws_raw%d" % h, [P, PACK, WS_COLS], F32)
             nc.sync.dma_start(out=raw[:], in_=ws.rearrange("(p j) c -> p j c", j=PACK)[:, :, h * WS_COLS:(h + 1) * WS_COLS])
             ws_raw.append(raw)
-        v_raw = sb("v_raw", [P, 2, PACK, N], F32)
+        v_raw = []
         for part, v in enumerate((vc, vs)):
-            nc.sync.dma_start(out=v_raw[:, part, :, :], in_=v.rearrange("(p t) m -> p t m", t=PACK))
+            raw = sb("v_raw%d" % part, [P, PACK, N], F32)
+            nc.sync.dma_start(out=raw[:], in_=v.rearrange("(p t) m -> p t m", t=PACK))
+            v_raw.append(raw)
 
         huge = sb("huge", [P, 1], F32)
-        nc.vector.memset(huge[:], 2.0 ** 96)
+        nc.vector.memset(huge[:], 2.0 ** 80)
         guard = sb("guard", [P, 1], F32)
         nc.scalar.activation(guard[:], huge[:], ACT.Abs_reciprocal_sqrt)
 
@@ -81,37 +85,42 @@ def tile_picked_ysubtr_sub_p_kernel(tc, x_words, x_scales, wc, ws, unit, vc, vs,
         make_identity(nc, identity[:])
 
         def round_and_deal(copy, raw, grouped):
-            copy(grouped.rearrange("p t m j -> p m j t"), raw.rearrange("p j (m t) -> p m j t", t=PACK))
+            copy(grouped.rearrange("p t m j -> p m j t"), raw.rearrange("p j m t -> p m j t"))
+
+        def by_slots(raw):
+            return raw.rearrange("p j (m t) -> p j m t", t=PACK)
 
         wc_bf = sb("wc_bf", [P, PACK, P, PACK], BF16)
-        round_and_deal(nc.scalar.copy, wc_raw[:, :, 0:PACK * SCALAR_ROWS], wc_bf[:, :, 0:SCALAR_ROWS, :])
+        round_and_deal(nc.scalar.copy, by_slots(wc_raw[:])[:, :, 0:SCALAR_ROWS, :], wc_bf[:, :, 0:SCALAR_ROWS, :])
         x_bytes = sb("x_bytes", [P, S], U8)
         nc.vector.tensor_copy(x_bytes[:], bytes_all[:].indirect(offsets[:]))
-        round_and_deal(nc.vector.tensor_copy, wc_raw[:, :, PACK * SCALAR_ROWS:H], wc_bf[:, :, SCALAR_ROWS:P, :])
+        round_and_deal(nc.vector.tensor_copy, by_slots(wc_raw[:])[:, :, SCALAR_ROWS:P, :], wc_bf[:, :, SCALAR_ROWS:P, :])
         wc_codes = sb("wc_codes", [P, H], U32, tag="bytes_all")
         wc_scales = sb("wc_scales", [P, H], U8)
         nc.vector.quantize_mx(out=wc_codes[:].bitcast(FP8X4), scales=wc_scales[:], in_=wc_bf[:].rearrange("p t m j -> p (t m j)"))
 
         u2 = sb("u2", [P, PACK], F32)
-        nc.scalar.activation(u2[:], u, ACT.Square)
+        nc.scalar.activation(u2[:], unit_planes[:], ACT.Square)
         u_sign = sb("u_sign", [P, PACK], F32)
-        nc.scalar.activation(u_sign[:], u, ACT.Sign)
-        u2_top = sb("u2_top", [P, PACK], F32)
-        nc.scalar.activation(u2_top[:], u2[:], ACT.Copy, scale=1.02)
-        u2_neg = sb("u2_neg", [P, PACK], F32)
-        nc.scalar.activation(u2_neg[:], u2[:], ACT.Copy, scale=-1.0)
-        u2_floor = sb("u2_floor", [P, PACK], F32)
-        nc.scalar.activation(u2_floor[:], u2[:], ACT.Copy, scale=GAIN_FLOOR)
+        nc.scalar.activation(u_sign[:], unit_planes[:], ACT.Sign)
+        u_root = sb("u_root", [P, PACK], F32)
+        nc.scalar.activation(u_root[:], u2[:], ACT.Abs_reciprocal_sqrt, scale=TOP, bias=TINY)
+        u_inv = sb("u_inv", [P, PACK], F32)
+        nc.scalar.activation(u_inv[:], u_root[:], ACT.Square)
 
         x_codes = []
-        for h in range(2):
-            picked = sb("x_codes%d" % h, [P, HALF], U32)
-            nc.vector.tensor_copy(picked[:], words_all[:].bitcast(U32).indirect(offsets[:, h * HALF // 16:(h + 1) * HALF // 16]))
-            x_codes.append(picked)
+        for first, count in ((0, 1), (1, 1), (2, 2)):
+            picked = sb("x_codes%d" % first, [P, count * CHUNK], U32)
+            cols = slice(first * CHUNK // LIST_ROWS, (first + count) * CHUNK // LIST_ROWS)
+            nc.vector.tensor_copy(picked[:], words_all[:].bitcast(U32).indirect(offsets[:, cols]))
+            x_codes.extend(picked[:, i * CHUNK:(i + 1) * CHUNK].bitcast(FP8X4) for i in range(count))
 
-        def turned_square(name, codes, scales, c):
+        def frames(c):
+            return slice(c * CHUNK, (c + 1) * CHUNK)
+
+        def turned_product(name, codes, scales, c):
             bank = psum.tile([P, H], F32, name="%s_turned" % name, tag="%s%d" % (name, c))
-            nc.tensor.matmul_mx(out=bank[:], lhsT=x_codes[c // PER_HALF][:, in_half(c)].bitcast(FP8X4), lhsT_scale=x_bytes[:, c * CHUNK:(c + 1) * CHUNK],
+            nc.tensor.matmul_mx(out=bank[:], lhsT=x_codes[c], lhsT_scale=x_bytes[:, frames(c)],
                                 rhs=codes[:].bitcast(FP8X4), rhs_scale=scales[:], start=True, stop=True)
             return bank
 
@@ -120,171 +129,199 @@ def tile_picked_ysubtr_sub_p_kernel(tc, x_words, x_scales, wc, ws, unit, vc, vs,
             for t in range(PACK):
                 plane = slice(t * P, (t + 1) * P)
                 nc.tensor.matmul_mx(out=bank[:, t, :], lhsT=codes[:, plane].bitcast(FP8X4), lhsT_scale=scales[:, plane],
-                                    rhs=x_codes[c // PER_HALF][:, in_half(c)].bitcast(FP8X4), rhs_scale=x_bytes[:, c * CHUNK:(c + 1) * CHUNK],
-                                    start=True, stop=True)
+                                    rhs=x_codes[c], rhs_scale=x_bytes[:, frames(c)], start=True, stop=True)
             return bank
 
         last = CHUNKS - 1
-        re = [first_product("re", wc_codes, wc_scales, c) for c in range(last)]
-        re_turned = turned_square("re", wc_codes, wc_scales, last)
-        re_sq = []
-        for c in range(last):
-            sq = sb("re_sq%d" % c, [P, PACK, CHUNK], F32)
-            nc.scalar.activation(sq[:], re[c][:], ACT.Square)
-            re_sq.append(sq)
+        turned = TURNED
+        plain = [c for c in range(CHUNKS) if c != turned]
+        re = {c: first_product("re", wc_codes, wc_scales, c) for c in plain}
+        re_turned = turned_product("re", wc_codes, wc_scales, turned)
+        re_sq = {c: planes_tile("re_sq%d" % c) for c in plain}
+        for c in plain:
+            nc.scalar.activation(re_sq[c][:], re[c][:], ACT.Square)
         turned_sq = [sb("turned_sq%d" % part, [P, H], F32) for part in range(2)]
         nc.scalar.activation(turned_sq[0][:], re_turned[:], ACT.Square)
 
         ws_codes = sb("ws_codes", [P, H], U32)
         ws_scales = sb("ws_scales", [P, H], U8)
-        ws_bf = sb("ws_bf", [P, PACK, P, PACK], BF16)
-        round_and_deal(nc.vector.tensor_copy, ws_raw[0][:], ws_bf[:, :, 0:WS_ROWS, :])
-        for t in range(0, PACK, 2):
-            nc.vector.tensor_copy(ws_bf[:, t:t + 2, WS_ROWS:P, :].rearrange("p t m j -> p m j t"),
-                                  ws_raw[1][:].rearrange("p j (m t) -> p m j t", t=PACK)[:, :, :, t:t + 2])
-        for t in range(0, PACK, 2):
-            cols = slice(t * P, (t + 2) * P)
-            nc.vector.quantize_mx(out=ws_codes[:, cols].bitcast(FP8X4), scales=ws_scales[:, cols], in_=ws_bf[:, t:t + 2, :, :].rearrange("p t m j -> p (t m j)"))
+        ws_bf = [sb("ws_bf%d" % h, [P, PACK, WS_ROWS, PACK], BF16) for h in range(2)]
 
-        im = [first_product("im", ws_codes, ws_scales, c) for c in range(last)]
-        im_turned = turned_square("im", ws_codes, ws_scales, last)
-        im.append(first_product("im", ws_codes, ws_scales, last, tag="re%d" % last))
+        def quantize_ws(h, t):
+            cols = slice(t * P + h * WS_ROWS, t * P + (h + 1) * WS_ROWS)
+            nc.vector.quantize_mx(out=ws_codes[:, cols].bitcast(FP8X4), scales=ws_scales[:, cols], in_=ws_bf[h][:, t, :, :].rearrange("p m j -> p (m j)"))
+
+        for h in range(2):
+            for planes in plane_pairs:
+                round_and_deal(nc.vector.tensor_copy, by_slots(ws_raw[h][:])[:, :, :, planes], ws_bf[h][:, planes, :, :])
+            for t in range(PACK):
+                quantize_ws(h, t)
+
+        im = {c: first_product("im", ws_codes, ws_scales, c) for c in range(turned)}
+        im_turned = turned_product("im", ws_codes, ws_scales, turned)
+        im[last] = first_product("im", ws_codes, ws_scales, last)
+        im[turned] = first_product("im", ws_codes, ws_scales, turned, tag="re%d" % turned)
 
         v_codes, v_scales = [], []
 
         def sign_and_round(engine, part, tag):
             v_bf = sb("v_bf%d" % part, [P, N, PACK], BF16, tag=tag)
-            engine.tensor_tensor(v_bf[:].rearrange("p (b i) t -> p b t i", i=PACK), v_raw[:, part, :, :].rearrange("p t (b i) -> p b t i", i=PACK),
+            engine.tensor_tensor(v_bf[:].rearrange("p (b i) t -> p b t i", i=PACK), v_raw[part][:].rearrange("p t (b i) -> p b t i", i=PACK),
                                  u_sign[:].unsqueeze(1).unsqueeze(3).to_broadcast([P, N // PACK, PACK, PACK]), ALU.mult)
             return v_bf
 
-        def quantize_v(part, v_bf, tag=None):
-            v_codes.append(sb("v_codes%d" % part, [P, N], U32, tag=tag))
+        def quantize_v(part, v_bf):
+            v_codes.append(sb("v_codes%d" % part, [P, N], U32))
             v_scales.append(sb("v_scales%d" % part, [P, N], U8))
             nc.vector.quantize_mx(out=v_codes[part][:].bitcast(FP8X4), scales=v_scales[part][:], in_=v_bf[:].rearrange("p m t -> p (m t)"))
 
-        vc_bf = sign_and_round(nc.vector, 0, tag="ws_bf")
+        vc_bf = sign_and_round(nc.vector, 0, tag="ws_bf1")
         vs_bf = sign_and_round(nc.vector, 1, tag="ws_raw1")
-        quantize_v(0, vc_bf)
 
-        power = [sb("power0", [P, PACK, HALF], F32), sb("power1", [P, PACK, CHUNK], F32)]
-        for c in range(last):
-            sq = sb("im_sq%d" % c, [P, PACK, CHUNK], F32)
-            nc.scalar.activation(sq[:], im[c][:], ACT.Square)
-            nc.vector.tensor_tensor(power[c // PER_HALF][:, :, in_half(c)], re_sq[c][:], sq[:], ALU.add)
-            if c == 0:
-                quantize_v(1, vs_bf)
-
-        nc.scalar.activation(turned_sq[1][:], im_turned[:], ACT.Square)
-        last_power = psum.tile([P, PACK, CHUNK], F32, name="last_power", tag="im%d" % last)
-        for part in range(2):
-            for t in range(PACK):
-                nc.tensor.matmul(last_power[:, t, :], turned_sq[part][:, t * P:(t + 1) * P], identity[:], is_transpose=True,
-                                 start=(part, t) == (0, 0), stop=(part, t) == (1, PACK - 1))
-        late_power = (power[1], last_power)
-
-        inv_root = [sb("inv_root%d" % h, [P, PACK, HALF], F32) for h in range(2)]
-        least = [sb("least%d" % h, [P, PACK, GROUPS], F32) for h in range(2)]
-
-        runs = CHUNK // D
-
-        inv_power = sb("inv_power", [P, PACK, HALF], F32)
-        plane_pairs = (slice(0, PAIR), slice(PAIR, PACK))
-        for planes in plane_pairs:
-            nc.scalar.activation(inv_root[0][:, planes, :], power[0][:, planes, :], ACT.Abs_reciprocal_sqrt, bias=POWER_OFFSET)
-        for planes in plane_pairs:
-            nc.scalar.activation(inv_power[:, planes, :], inv_root[0][:, planes, :], ACT.Square)
-        nc.vector.tensor_reduce(least[0][:], by_runs(power[0][:]), AX.X, ALU.min)
-        nc.vector.tensor_reduce(least[1][:, :, 0:runs], by_runs(late_power[0][:]), AX.X, ALU.min)
-        noise_u2 = sb("noise_u2", [P, PACK, GROUPS], F32)
-        nc.vector.scalar_tensor_tensor(noise_u2[:], least[0][:], NOISE_FACTOR, u2[:].unsqueeze(2).to_broadcast([P, PACK, GROUPS]), ALU.mult, ALU.mult)
-        nc.vector.tensor_reduce(least[1][:, :, runs:], by_runs(late_power[1][:]), AX.X, ALU.min)
-        for c in range(PER_HALF):
-            nc.scalar.activation(inv_root[1][:, :, in_half(c)], late_power[c][:], ACT.Abs_reciprocal_sqrt, bias=POWER_OFFSET)
-        re.append(first_product("re", wc_codes, wc_scales, last, tag="im%d" % last))
-        noise_inv_root = sb("noise_inv_root", [P, PACK, GROUPS], F32)
-        nc.scalar.activation(noise_inv_root[:], least[1][:], ACT.Abs_reciprocal_sqrt, scale=NOISE_FACTOR, bias=guard[:])
-
-        ratio_u2 = sb("ratio_u2", [P, PACK, HALF], F32)
-        for t in range(0, PACK, 2):
-            nc.vector.tensor_tensor(by_runs(ratio_u2[:, t:t + 2, :]), by_runs(inv_power[:, t:t + 2, :]),
-                                    noise_u2[:, t:t + 2, :].unsqueeze(3).to_broadcast([P, 2, GROUPS, D]), ALU.mult)
-        noise_root = sb("noise_root", [P, PACK, GROUPS], F32)
-        nc.vector.scalar_tensor_tensor(noise_root[:], least[1][:], NOISE_FACTOR, noise_inv_root[:], ALU.mult, ALU.mult)
-        neg_gain2 = sb("neg_gain2", [P, PACK, HALF], F32)
-        for t in range(PACK):
-            nc.vector.tensor_scalar(neg_gain2[:, t, :], ratio_u2[:, t, :], u2[:, t:t + 1], u2_top[:, t:t + 1], ALU.min, ALU.subtract)
-
-        def root_ratio(engine, w, c):
-            engine.tensor_tensor(by_runs(w[:]), by_runs(inv_root[1][:, :, in_half(c)]),
-                                 noise_root[:, :, c * runs:(c + 1) * runs].unsqueeze(3).to_broadcast([P, PACK, runs, D]), ALU.mult)
-
-        third = sb("third", [P, PACK, CHUNK], F32)
-        root_ratio(nc.vector, third, 0)
-        clipped = sb("clipped", [P, PACK, CHUNK], F32)
-        nc.gpsimd.tensor_scalar(clipped[:], third[:], 1.0, 0.0, ALU.min, ALU.max)
-        fourth = sb("fourth", [P, PACK, CHUNK], F32, tag="third")
-        root_ratio(nc.gpsimd, fourth, 1)
-        by_gpsimd, by_scalar = plane_pairs
-        clipped_last = sb("clipped_last", [P, PAIR, CHUNK], F32)
-        nc.gpsimd.tensor_scalar(clipped_last[:], fourth[:, by_gpsimd, :], 1.0, 0.0, ALU.min, ALU.max)
-
-        gain = [sb("gain%d" % c, [P, PACK * CHUNK], F32) for c in range(CHUNKS)]
-
-        def early_gain(c, first, count):
-            nc.scalar.activation(gain[c][:].rearrange("p (t n) -> p t n", t=PACK)[:, :, first:first + count],
-                                 neg_gain2[:, :, c * CHUNK + first:c * CHUNK + first + count], ACT.Sqrt, scale=-1.0)
-
-        def root_by_planes(c, source, scale, bias, planes):
-            for t in range(planes.start, planes.stop):
-                nc.scalar.activation(gain[c][:, t * CHUNK:(t + 1) * CHUNK], source[:, t, :], ACT.Sqrt, scale=scale[:, t:t + 1], bias=bias[:, t:t + 1])
-
-        early_gain(0, 0, FIRST_FRAMES)
-        early_gain(0, FIRST_FRAMES, CHUNK - FIRST_FRAMES)
-        early_gain(1, 0, CHUNK)
-        third_sq = sb("third_sq", [P, PACK, CHUNK], F32)
-        for planes in (slice(0, PAIR), slice(PAIR, PACK)):
-            nc.scalar.activation(third_sq[:, planes, :], clipped[:, planes, :], ACT.Square)
-        root_by_planes(2, third_sq, u2_neg, u2_top, slice(0, PACK))
-        fourth_sq = sb("fourth_sq", [P, PACK, CHUNK], F32)
-        kept = sb("kept", [P, PACK, CHUNK], F32)
-        nc.scalar.activation(fourth_sq[:, by_scalar, :], fourth[:, by_scalar, :], ACT.Square)
-        nc.scalar.activation(fourth_sq[:, by_gpsimd, :], clipped_last[:], ACT.Square)
-        nc.scalar.activation(kept[:, by_scalar, :], fourth_sq[:, by_scalar, :], ACT.Relu, scale=-1.0, bias=1.0)
-        root_by_planes(3, fourth_sq, u2_neg, u2_top, by_gpsimd)
-        root_by_planes(3, kept, u2, u2_floor, by_scalar)
-
+        im_sq = {c: planes_tile("im_sq%d" % c) for c in plain}
+        power = {c: planes_tile("power%d" % c) for c in plain}
+        least = [sb("least%d" % c, [P, PACK * RUNS], F32) for c in range(CHUNKS)]
+        noise_root = [sb("noise_root%d" % c, [P, PACK * RUNS], F32) for c in range(CHUNKS)]
+        noise_inv = [sb("noise_inv%d" % c, [P, PACK * RUNS], F32) for c in range(CHUNKS)]
+        ratio = [planes_tile("ratio%d" % c) for c in range(CHUNKS)]
+        excess = [planes_tile("excess%d" % c) for c in range(CHUNKS)]
+        root = [planes_tile("root%d" % c) for c in range(CHUNKS)]
+        inverse = [planes_tile("inverse%d" % c) for c in range(CHUNKS)]
+        gain = [planes_tile("gain%d" % c) for c in range(CHUNKS)]
         z = sb("z", [P, 2 * CHUNKS, CHUNK, PACK], BF16)
         z_codes = sb("z_codes", [P, 2 * S], U32)
         z_scales = sb("z_scales", [P, 2 * S], U8)
 
-        def weigh(c):
-            for part, bank in enumerate((re[c], im[c])):
-                strip = z[:, 2 * c + part, :, :]
-                cuts = (0, FIRST_FRAMES, CHUNK) if (c, part) == (0, 0) else (0, CHUNK)
-                for first, end in zip(cuts, cuts[1:]):
-                    nc.vector.tensor_tensor(strip[:, first:end, :].rearrange("p (b e) t -> p b t e", e=PAIR),
-                                            bank[:, :, first:end].rearrange("p t (b e) -> p b t e", e=PAIR),
-                                            gain[c][:].rearrange("p (t n) -> p t n", t=PACK)[:, :, first:end].rearrange("p t (b e) -> p b t e", e=PAIR), ALU.mult)
+        every_plane = slice(0, PACK)
 
-        def quantize_strips(first, last):
-            cols = slice(first * CHUNK, last * CHUNK)
-            nc.vector.quantize_mx(out=z_codes[:, cols].bitcast(FP8X4), scales=z_scales[:, cols], in_=z[:, first:last, :, :].rearrange("p s n t -> p (s n t)"))
+        def runs_of(planes):
+            return slice(planes.start * RUNS, planes.stop * RUNS)
 
-        for c in range(last):
-            weigh(c)
-        quantize_strips(0, 2 * PER_HALF)
-        quantize_strips(2 * PER_HALF, 2 * last)
-        weigh(last)
-        quantize_strips(2 * last, 2 * last + 1)
-        quantize_strips(2 * last + 1, 2 * last + 2)
+        def square_im(c, planes=every_plane):
+            nc.scalar.activation(im_sq[c][:, planes, :], im[c][:, planes, :], ACT.Square)
 
-        result = sb("result", [P, CHUNKS, CHUNK], F32, tag="kept")
-        for c in range(CHUNKS):
-            acc = psum.tile([P, CHUNK], F32, name="acc%d" % c, tag="re%d" % c)
+        def add(c, planes=every_plane):
+            nc.vector.tensor_tensor(power[c][:, planes, :], re_sq[c][:, planes, :], im_sq[c][:, planes, :], ALU.add)
+
+        def find_least(c, planes=every_plane):
+            nc.vector.tensor_reduce(least[c][:, runs_of(planes)], by_runs(power[c][:, planes, :]), AX.X, ALU.min)
+
+        def noise_first(c):
+            nc.scalar.activation(noise_root[c][:], least[c][:], ACT.Abs_reciprocal_sqrt, scale=NOISE_FACTOR / TOP, bias=guard[:])
+
+        def noise_second(c):
+            nc.scalar.activation(noise_inv[c][:], noise_root[c][:], ACT.Square)
+
+        def spread_noise(c, planes):
+            return noise_inv[c][:, runs_of(planes)].unsqueeze(2).to_broadcast([P, (planes.stop - planes.start) * RUNS, D])
+
+        def form_ratio(c, planes=every_plane):
+            nc.vector.scalar_tensor_tensor(by_runs(ratio[c][:, planes, :]), by_runs(power[c][:, planes, :]), POWER_OFFSET, spread_noise(c, planes), ALU.add, ALU.mult)
+
+        def clip(engine, c):
+            engine.tensor_scalar(excess[c][:], ratio[c][:], CEILING, TOP, ALU.min, ALU.max)
+
+        def clip_on_scalar(c):
+            for planes in plane_pairs:
+                nc.scalar.activation(excess[c][:, planes, :], ratio[c][:, planes, :], ACT.Relu, bias=-TOP)
+
+        def form_gain(c, shift=-1.0):
+            for planes in plane_pairs:
+                nc.scalar.activation(root[c][:, planes, :], excess[c][:, planes, :], ACT.Abs_reciprocal_sqrt, bias=shift)
+            for planes in plane_pairs:
+                nc.scalar.activation(inverse[c][:, planes, :], root[c][:, planes, :], ACT.Square)
+            for t in range(PACK):
+                nc.scalar.activation(gain[c][:, t, :], inverse[c][:, t, :], ACT.Abs_reciprocal_sqrt, scale=u_inv[:, t:t + 1], bias=u_inv[:, t:t + 1])
+
+        def weigh(c, part, cols=slice(0, CHUNK)):
+            bank = (re, im)[part][c]
+            nc.vector.tensor_tensor(z[:, 2 * c + part, cols, :].rearrange("p (b e) t -> p b t e", e=PAIR), bank[:, :, cols].rearrange("p t (b e) -> p b t e", e=PAIR),
+                                    gain[c][:, :, cols].rearrange("p t (b e) -> p b t e", e=PAIR), ALU.mult)
+
+        def form_gain_halves(c):
+            halves = (slice(0, CHUNK // 2), slice(CHUNK // 2, CHUNK))
+            for cols in halves:
+                nc.scalar.activation(root[c][:, :, cols], excess[c][:, :, cols], ACT.Abs_reciprocal_sqrt, bias=-1.0)
+            for cols in halves:
+                nc.scalar.activation(inverse[c][:, :, cols], root[c][:, :, cols], ACT.Square)
+            for cols in halves:
+                for t in range(PACK):
+                    nc.scalar.activation(gain[c][:, t, cols], inverse[c][:, t, cols], ACT.Abs_reciprocal_sqrt, scale=u_inv[:, t:t + 1], bias=u_inv[:, t:t + 1])
+
+        def quantize_strips(first, end):
+            cols = slice(first * CHUNK, end * CHUNK)
+            nc.vector.quantize_mx(out=z_codes[:, cols].bitcast(FP8X4), scales=z_scales[:, cols], in_=z[:, first:end, :, :].rearrange("p s n t -> p (s n t)"))
+
+        result = sb("result", [P, CHUNKS, CHUNK], F32)
+
+        def second_product(c):
+            acc = psum.tile([P, CHUNK], F32, name="acc%d" % c, tag=("re0", "re1", "im0", "im1")[c])
             for part in range(2):
                 cols = slice((2 * c + part) * CHUNK, (2 * c + part + 1) * CHUNK)
                 nc.tensor.matmul_mx(out=acc[:], lhsT=v_codes[part][:].bitcast(FP8X4), lhsT_scale=v_scales[part][:],
                                     rhs=z_codes[:, cols].bitcast(FP8X4), rhs_scale=z_scales[:, cols], start=(part == 0), stop=(part == 1))
             nc.scalar.copy(result[:, c, :], acc[:])
-            nc.sync.dma_start(out=out[:, c * CHUNK:(c + 1) * CHUNK], in_=result[:, c, :])
+            nc.sync.dma_start(out=out[:, frames(c)], in_=result[:, c, :])
+
+        for planes in plane_pairs:
+            square_im(0, planes)
+        for planes in plane_pairs:
+            add(0, planes)
+        for planes in plane_pairs:
+            find_least(0, planes)
+        square_im(1)
+        nc.scalar.activation(turned_sq[1][:], im_turned[:], ACT.Square)
+        noise_first(0)
+        square_im(last, plane_pairs[0])
+        noise_second(0)
+        square_im(last, plane_pairs[1])
+        add(1)
+        quantize_v(0, vc_bf)
+        quantize_v(1, vs_bf)
+        find_least(1)
+        power[turned] = psum.tile([P, PACK, CHUNK], F32, name="turned_power", tag="im%d" % turned)
+        for part in range(2):
+            for t in range(PACK):
+                nc.tensor.matmul(power[turned][:, t, :], turned_sq[part][:, t * P:(t + 1) * P], identity[:], is_transpose=True,
+                                 start=(part, t) == (0, 0), stop=(part, t) == (1, PACK - 1))
+        for planes in plane_pairs:
+            form_ratio(0, planes)
+        noise_first(1)
+        noise_second(1)
+        clip_on_scalar(0)
+        find_least(turned)
+        add(last)
+        noise_first(turned)
+        noise_second(turned)
+        form_ratio(1)
+        find_least(last)
+        clip(nc.vector, 1)
+        noise_first(last)
+        noise_second(last)
+        form_gain(0, GAIN_FLOOR)
+        form_ratio(turned)
+        re[turned] = first_product("re", wc_codes, wc_scales, turned, tag="im%d" % turned)
+        clip(nc.gpsimd, turned)
+        form_gain(1)
+        weigh(0, 0)
+        weigh(0, 1)
+        form_ratio(last)
+        clip(nc.gpsimd, last)
+        form_gain(2)
+        quantize_strips(0, 2)
+        weigh(1, 0)
+        weigh(1, 1)
+        form_gain_halves(3)
+        quantize_strips(2, 4)
+        weigh(2, 0)
+        weigh(2, 1)
+        quantize_strips(4, 6)
+        for cols in (slice(0, CHUNK // 2), slice(CHUNK // 2, CHUNK)):
+            weigh(3, 0, cols)
+            weigh(3, 1, cols)
+        second_product(0)
+        second_product(1)
+        second_product(2)
+        quantize_strips(6, 7)
+        quantize_strips(7, 8)
+        second_product(3)

@@ -177,151 +177,167 @@ def tile_picked_ysubtr_sub_p_kernel(tc, x_words, x_scales, wc, ws, unit, vc, vs,
 
         vc_bf = sign_and_round(nc.vector, 0, tag="ws_bf1")
         vs_bf = sign_and_round(nc.vector, 1, tag="ws_raw1")
+        quantize_v(0, vc_bf)
 
-        im_sq = {c: planes_tile("im_sq%d" % c) for c in plain}
-        power = {c: planes_tile("power%d" % c) for c in plain}
-        least = [sb("least%d" % c, [P, PACK * RUNS], F32) for c in range(CHUNKS)]
-        noise_root = [sb("noise_root%d" % c, [P, PACK * RUNS], F32) for c in range(CHUNKS)]
-        noise_inv = [sb("noise_inv%d" % c, [P, PACK * RUNS], F32) for c in range(CHUNKS)]
-        ratio = [planes_tile("ratio%d" % c) for c in range(CHUNKS)]
-        excess = [planes_tile("excess%d" % c) for c in range(CHUNKS)]
-        root = [planes_tile("root%d" % c) for c in range(CHUNKS)]
-        inverse = [planes_tile("inverse%d" % c) for c in range(CHUNKS)]
-        gain = [planes_tile("gain%d" % c) for c in range(CHUNKS)]
-        z = sb("z", [P, 2 * CHUNKS, CHUNK, PACK], BF16)
-        z_codes = sb("z_codes", [P, 2 * S], U32)
-        z_scales = sb("z_scales", [P, 2 * S], U8)
-
+        low, high = plane_pairs
         every_plane = slice(0, PACK)
+        every_frame = slice(0, CHUNK)
+        early, late = slice(0, CHUNK // 2), slice(CHUNK // 2, CHUNK)
 
-        def runs_of(planes):
-            return slice(planes.start * RUNS, planes.stop * RUNS)
+        im_sq, power, least, noise_root, noise_inv = {}, {}, {}, {}, {}
+        ratio = {}
+        excess = [planes_tile("excess%d" % c) for c in range(CHUNKS)]
+        root = {}
+        gain = [planes_tile("gain%d" % c) for c in range(CHUNKS)]
+        inverse = {}
+        z = sb("z", [P, 2 * CHUNKS, CHUNK, PACK], BF16)
+        z_codes, z_scales = {}, {}
 
-        def square_im(c, planes=every_plane):
-            nc.scalar.activation(im_sq[c][:, planes, :], im[c][:, planes, :], ACT.Square)
+        def width(planes):
+            return planes.stop - planes.start
 
-        def add(c, planes=every_plane):
-            nc.vector.tensor_tensor(power[c][:, planes, :], re_sq[c][:, planes, :], im_sq[c][:, planes, :], ALU.add)
+        def piece(store, name, c, planes, columns, tag):
+            store[c, planes.start] = sb("%s%d_%d" % (name, c, planes.start), [P, width(planes), columns], F32, tag=tag)
+            return store[c, planes.start]
 
-        def find_least(c, planes=every_plane):
-            nc.vector.tensor_reduce(least[c][:, runs_of(planes)], by_runs(power[c][:, planes, :]), AX.X, ALU.min)
+        def square_im(c, planes=every_plane, tag=None):
+            nc.scalar.activation(piece(im_sq, "im_sq", c, planes, CHUNK, tag)[:], im[c][:, planes, :], ACT.Square)
 
-        def noise_first(c):
-            nc.scalar.activation(noise_root[c][:], least[c][:], ACT.Abs_reciprocal_sqrt, scale=NOISE_FACTOR / TOP, bias=guard[:])
+        def add(c, planes=every_plane, tag=None):
+            nc.vector.tensor_tensor(piece(power, "power", c, planes, CHUNK, tag)[:], re_sq[c][:, planes, :], im_sq[c, planes.start][:], ALU.add)
 
-        def noise_second(c):
-            nc.scalar.activation(noise_inv[c][:], noise_root[c][:], ACT.Square)
+        def find_least(c, planes=every_plane, tag=None):
+            nc.vector.tensor_reduce(piece(least, "least", c, planes, RUNS, tag)[:].rearrange("p t v -> p (t v)"), by_runs(power[c, planes.start][:]), AX.X, ALU.min)
 
-        def spread_noise(c, planes):
-            return noise_inv[c][:, runs_of(planes)].unsqueeze(2).to_broadcast([P, (planes.stop - planes.start) * RUNS, D])
+        def noise_first(c, planes=every_plane, tag=None):
+            nc.scalar.activation(piece(noise_root, "noise_root", c, planes, RUNS, tag)[:], least[c, planes.start][:], ACT.Abs_reciprocal_sqrt,
+                                 scale=NOISE_FACTOR / TOP, bias=guard[:])
 
-        def form_ratio(c, planes=every_plane):
-            nc.vector.scalar_tensor_tensor(by_runs(ratio[c][:, planes, :]), by_runs(power[c][:, planes, :]), POWER_OFFSET, spread_noise(c, planes), ALU.add, ALU.mult)
+        def noise_second(c, planes=every_plane):
+            nc.scalar.activation(piece(noise_inv, "noise_inv", c, planes, RUNS, None)[:], noise_root[c, planes.start][:], ACT.Square)
 
-        def clip(engine, c):
-            engine.tensor_scalar(excess[c][:], ratio[c][:], CEILING, TOP, ALU.min, ALU.max)
+        def form_ratio(c, planes=every_plane, whole=False):
+            source, factor = (power[c, 0][:, planes, :], noise_inv[c, 0][:, planes, :]) if whole else (power[c, planes.start][:], noise_inv[c, planes.start][:])
+            nc.vector.scalar_tensor_tensor(by_runs(piece(ratio, "ratio", c, planes, CHUNK, None)[:]), by_runs(source), POWER_OFFSET,
+                                           factor.rearrange("p t v -> p (t v)").unsqueeze(2).to_broadcast([P, width(planes) * RUNS, D]), ALU.add, ALU.mult)
 
-        def clip_on_scalar(c):
-            for planes in plane_pairs:
-                nc.scalar.activation(excess[c][:, planes, :], ratio[c][:, planes, :], ACT.Relu, bias=-TOP)
+        def clip(engine, c, planes=every_plane):
+            engine.tensor_scalar(excess[c][:, planes, :], ratio[c, planes.start][:], CEILING, TOP, ALU.min, ALU.max)
 
-        def form_gain(c, shift=-1.0):
-            for planes in plane_pairs:
-                nc.scalar.activation(root[c][:, planes, :], excess[c][:, planes, :], ACT.Abs_reciprocal_sqrt, bias=shift)
-            for planes in plane_pairs:
-                nc.scalar.activation(inverse[c][:, planes, :], root[c][:, planes, :], ACT.Square)
-            for t in range(PACK):
-                nc.scalar.activation(gain[c][:, t, :], inverse[c][:, t, :], ACT.Abs_reciprocal_sqrt, scale=u_inv[:, t:t + 1], bias=u_inv[:, t:t + 1])
+        def clip_on_scalar(c, planes):
+            nc.scalar.activation(excess[c][:, planes, :], ratio[c, planes.start][:], ACT.Relu, bias=-TOP)
+
+        def take_root(c, planes, cols=every_frame, shift=-1.0, tag=None):
+            key = c, planes.start, cols.start
+            root[key] = sb("root%d_%d_%d" % key, [P, width(planes), width(cols)], F32, tag=tag)
+            nc.scalar.activation(root[key][:], excess[c][:, planes, cols], ACT.Abs_reciprocal_sqrt, bias=shift)
+
+        def invert(c, planes, cols=every_frame):
+            key = c, planes.start, cols.start
+            inverse[key] = sb("inverse%d_%d_%d" % key, [P, width(planes), width(cols)], F32)
+            nc.scalar.activation(inverse[key][:], root[key][:], ACT.Square)
+
+        def form_gain(c, planes, cols=every_frame):
+            for t in range(planes.start, planes.stop):
+                nc.scalar.activation(gain[c][:, t, cols], inverse[c, planes.start, cols.start][:, t - planes.start, :], ACT.Abs_reciprocal_sqrt,
+                                     scale=u_inv[:, t:t + 1], bias=u_inv[:, t:t + 1])
 
         def weigh(c, part, cols=slice(0, CHUNK)):
             bank = (re, im)[part][c]
             nc.vector.tensor_tensor(z[:, 2 * c + part, cols, :].rearrange("p (b e) t -> p b t e", e=PAIR), bank[:, :, cols].rearrange("p t (b e) -> p b t e", e=PAIR),
                                     gain[c][:, :, cols].rearrange("p t (b e) -> p b t e", e=PAIR), ALU.mult)
 
-        def form_gain_halves(c):
-            halves = (slice(0, CHUNK // 2), slice(CHUNK // 2, CHUNK))
-            for cols in halves:
-                nc.scalar.activation(root[c][:, :, cols], excess[c][:, :, cols], ACT.Abs_reciprocal_sqrt, bias=-1.0)
-            for cols in halves:
-                nc.scalar.activation(inverse[c][:, :, cols], root[c][:, :, cols], ACT.Square)
-            for cols in halves:
-                for t in range(PACK):
-                    nc.scalar.activation(gain[c][:, t, cols], inverse[c][:, t, cols], ACT.Abs_reciprocal_sqrt, scale=u_inv[:, t:t + 1], bias=u_inv[:, t:t + 1])
-
-        def quantize_strips(first, end):
-            cols = slice(first * CHUNK, end * CHUNK)
-            nc.vector.quantize_mx(out=z_codes[:, cols].bitcast(FP8X4), scales=z_scales[:, cols], in_=z[:, first:end, :, :].rearrange("p s n t -> p (s n t)"))
+        def quantize_z(c, first=0, end=2 * CHUNK, tag=None):
+            if c not in z_codes:
+                z_codes[c] = sb("z_codes%d" % c, [P, 2 * CHUNK], U32, tag=tag)
+                z_scales[c] = sb("z_scales%d" % c, [P, 2 * CHUNK], U8)
+            nc.vector.quantize_mx(out=z_codes[c][:, first:end].bitcast(FP8X4), scales=z_scales[c][:, first:end],
+                                  in_=z[:, 2 * c:2 * c + 2, :, :].rearrange("p s n t -> p (s n t)")[:, PACK * first:PACK * end])
 
         result = sb("result", [P, CHUNKS, CHUNK], F32)
 
         def second_product(c):
             acc = psum.tile([P, CHUNK], F32, name="acc%d" % c, tag=("re0", "re1", "im0", "im1")[c])
             for part in range(2):
-                cols = slice((2 * c + part) * CHUNK, (2 * c + part + 1) * CHUNK)
+                cols = frames(part)
                 nc.tensor.matmul_mx(out=acc[:], lhsT=v_codes[part][:].bitcast(FP8X4), lhsT_scale=v_scales[part][:],
-                                    rhs=z_codes[:, cols].bitcast(FP8X4), rhs_scale=z_scales[:, cols], start=(part == 0), stop=(part == 1))
+                                    rhs=z_codes[c][:, cols].bitcast(FP8X4), rhs_scale=z_scales[c][:, cols], start=(part == 0), stop=(part == 1))
             nc.scalar.copy(result[:, c, :], acc[:])
             nc.sync.dma_start(out=out[:, frames(c)], in_=result[:, c, :])
 
-        for planes in plane_pairs:
-            square_im(0, planes)
-        for planes in plane_pairs:
-            add(0, planes)
-        for planes in plane_pairs:
-            find_least(0, planes)
+        for step in (square_im, add, find_least):
+            for planes in plane_pairs:
+                step(0, planes)
         square_im(1)
         nc.scalar.activation(turned_sq[1][:], im_turned[:], ACT.Square)
-        noise_first(0)
-        square_im(last, plane_pairs[0])
-        noise_second(0)
-        square_im(last, plane_pairs[1])
+        for step in (noise_first, noise_second):
+            for planes in plane_pairs:
+                step(0, planes)
+        im_sq[last, 0] = planes_tile("im_sq_last", tag="least0_0")
+        for planes in plane_pairs:
+            nc.scalar.activation(im_sq[last, 0][:, planes, :], im[last][:, planes, :], ACT.Square)
         add(1)
-        quantize_v(0, vc_bf)
         quantize_v(1, vs_bf)
         find_least(1)
-        power[turned] = psum.tile([P, PACK, CHUNK], F32, name="turned_power", tag="im%d" % turned)
+        power[turned, 0] = psum.tile([P, PACK, CHUNK], F32, name="turned_power", tag="im%d" % turned)
         for part in range(2):
             for t in range(PACK):
-                nc.tensor.matmul(power[turned][:, t, :], turned_sq[part][:, t * P:(t + 1) * P], identity[:], is_transpose=True,
+                nc.tensor.matmul(power[turned, 0][:, t, :], turned_sq[part][:, t * P:(t + 1) * P], identity[:], is_transpose=True,
                                  start=(part, t) == (0, 0), stop=(part, t) == (1, PACK - 1))
-        for planes in plane_pairs:
-            form_ratio(0, planes)
+        for step in (form_ratio, clip_on_scalar):
+            for planes in plane_pairs:
+                step(0, planes)
+        find_least(turned, tag="noise_inv0_0")
+        power[last, 0] = planes_tile("power_last", tag="power0_0")
+        nc.gpsimd.tensor_tensor(power[last, 0][:, low, :], re_sq[last][:, low, :], im_sq[last, 0][:, low, :], ALU.add)
+        nc.vector.tensor_tensor(power[last, 0][:, high, :], re_sq[last][:, high, :], im_sq[last, 0][:, high, :], ALU.add)
         noise_first(1)
         noise_second(1)
-        clip_on_scalar(0)
-        find_least(turned)
-        add(last)
+        take_root(0, low, shift=GAIN_FLOOR, tag="noise_inv0_2")
+        take_root(0, high, shift=GAIN_FLOOR)
         noise_first(turned)
+        invert(0, low)
         noise_second(turned)
+        invert(0, high)
         form_ratio(1)
         find_least(last)
         clip(nc.vector, 1)
-        noise_first(last)
-        noise_second(last)
-        form_gain(0, GAIN_FLOOR)
+        for planes in plane_pairs:
+            form_gain(0, planes)
         form_ratio(turned)
         re[turned] = first_product("re", wc_codes, wc_scales, turned, tag="im%d" % turned)
         clip(nc.gpsimd, turned)
-        form_gain(1)
+        take_root(1, low)
+        take_root(1, high)
+        noise_first(last)
+        invert(1, low)
+        noise_second(last)
+        invert(1, high)
         weigh(0, 0)
         weigh(0, 1)
+        for planes in plane_pairs:
+            form_gain(1, planes)
         form_ratio(last)
         clip(nc.gpsimd, last)
-        form_gain(2)
-        quantize_strips(0, 2)
+        for step in (take_root, invert, form_gain):
+            for planes in plane_pairs:
+                step(turned, planes)
+        quantize_z(0)
         weigh(1, 0)
         weigh(1, 1)
-        form_gain_halves(3)
-        quantize_strips(2, 4)
-        weigh(2, 0)
-        weigh(2, 1)
-        quantize_strips(4, 6)
-        for cols in (slice(0, CHUNK // 2), slice(CHUNK // 2, CHUNK)):
-            weigh(3, 0, cols)
-            weigh(3, 1, cols)
+        for step in (take_root, invert, form_gain):
+            for cols in (early, late):
+                step(last, every_plane, cols)
+        for c in (1, turned):
+            quantize_z(c, 0, CHUNK)
+            quantize_z(c, CHUNK, 2 * CHUNK)
+            for cols in ((every_frame,) if c == 1 else (early, late)):
+                weigh(c + 1, 0, cols)
+                weigh(c + 1, 1, cols)
         second_product(0)
         second_product(1)
         second_product(2)
-        quantize_strips(6, 7)
-        quantize_strips(7, 8)
+        quantize_z(last, 0, CHUNK)
+        quantize_z(last, CHUNK, CHUNK + CHUNK // 2)
+        quantize_z(last, CHUNK + CHUNK // 2, 2 * CHUNK)
         second_product(3)

@@ -164,20 +164,24 @@ def tile_picked_ysubtr_sub_p_kernel(tc, x_words, x_scales, wc, ws, unit, vc, vs,
 
         v_codes, v_scales = [], []
 
-        def sign_and_round(engine, part, tag):
-            v_bf = sb("v_bf%d" % part, [P, N, PACK], BF16, tag=tag)
-            engine.tensor_tensor(v_bf[:].rearrange("p (b i) t -> p b t i", i=PACK), v_raw[part][:].rearrange("p t (b i) -> p b t i", i=PACK),
-                                 u_sign[:].unsqueeze(1).unsqueeze(3).to_broadcast([P, N // PACK, PACK, PACK]), ALU.mult)
+        def sign_and_round(engine, part, tag, cols=slice(0, N)):
+            count = cols.stop - cols.start
+            v_bf = sb("v_bf%d_%d" % (part, cols.start), [P, count, PACK], BF16, tag=tag)
+            engine.tensor_tensor(v_bf[:].rearrange("p (b i) t -> p b t i", i=PACK), v_raw[part][:, :, cols].rearrange("p t (b i) -> p b t i", i=PACK),
+                                 u_sign[:].unsqueeze(1).unsqueeze(3).to_broadcast([P, count // PACK, PACK, PACK]), ALU.mult)
             return v_bf
 
-        def quantize_v(part, v_bf):
+        for part in range(2):
             v_codes.append(sb("v_codes%d" % part, [P, N], U32))
             v_scales.append(sb("v_scales%d" % part, [P, N], U8))
-            nc.vector.quantize_mx(out=v_codes[part][:].bitcast(FP8X4), scales=v_scales[part][:], in_=v_bf[:].rearrange("p m t -> p (m t)"))
+
+        def quantize_v(part, v_bf, cols=slice(0, N)):
+            nc.vector.quantize_mx(out=v_codes[part][:, cols].bitcast(FP8X4), scales=v_scales[part][:, cols], in_=v_bf[:].rearrange("p m t -> p (m t)"))
 
         vc_bf = sign_and_round(nc.vector, 0, tag="ws_bf1")
-        vs_bf = sign_and_round(nc.vector, 1, tag="ws_raw1")
         quantize_v(0, vc_bf)
+        v_halves = (slice(0, N // 2), slice(N // 2, N))
+        vs_first = sign_and_round(nc.vector, 1, "ws_raw1", v_halves[0])
 
         low, high = plane_pairs
         every_plane = slice(0, PACK)
@@ -190,7 +194,7 @@ def tile_picked_ysubtr_sub_p_kernel(tc, x_words, x_scales, wc, ws, unit, vc, vs,
         root = {}
         gain = [planes_tile("gain%d" % c) for c in range(CHUNKS)]
         inverse = {}
-        z = sb("z", [P, 2 * CHUNKS, CHUNK, PACK], BF16)
+        z = [sb("z%d" % c, [P, 2, CHUNK, PACK], BF16) for c in range(CHUNKS)]
         z_codes, z_scales = {}, {}
 
         def width(planes):
@@ -244,7 +248,7 @@ def tile_picked_ysubtr_sub_p_kernel(tc, x_words, x_scales, wc, ws, unit, vc, vs,
 
         def weigh(c, part, cols=slice(0, CHUNK)):
             bank = (re, im)[part][c]
-            nc.vector.tensor_tensor(z[:, 2 * c + part, cols, :].rearrange("p (b e) t -> p b t e", e=PAIR), bank[:, :, cols].rearrange("p t (b e) -> p b t e", e=PAIR),
+            nc.vector.tensor_tensor(z[c][:, part, cols, :].rearrange("p (b e) t -> p b t e", e=PAIR), bank[:, :, cols].rearrange("p t (b e) -> p b t e", e=PAIR),
                                     gain[c][:, :, cols].rearrange("p t (b e) -> p b t e", e=PAIR), ALU.mult)
 
         def quantize_z(c, first=0, end=2 * CHUNK, tag=None):
@@ -252,17 +256,21 @@ def tile_picked_ysubtr_sub_p_kernel(tc, x_words, x_scales, wc, ws, unit, vc, vs,
                 z_codes[c] = sb("z_codes%d" % c, [P, 2 * CHUNK], U32, tag=tag)
                 z_scales[c] = sb("z_scales%d" % c, [P, 2 * CHUNK], U8)
             nc.vector.quantize_mx(out=z_codes[c][:, first:end].bitcast(FP8X4), scales=z_scales[c][:, first:end],
-                                  in_=z[:, 2 * c:2 * c + 2, :, :].rearrange("p s n t -> p (s n t)")[:, PACK * first:PACK * end])
+                                  in_=z[c][:].rearrange("p s n t -> p (s n t)")[:, PACK * first:PACK * end])
 
         result = sb("result", [P, CHUNKS, CHUNK], F32)
 
-        def second_product(c):
-            acc = psum.tile([P, CHUNK], F32, name="acc%d" % c, tag=("re0", "re1", "im0", "im1")[c])
-            for part in range(2):
-                cols = frames(part)
-                nc.tensor.matmul_mx(out=acc[:], lhsT=v_codes[part][:].bitcast(FP8X4), lhsT_scale=v_scales[part][:],
-                                    rhs=z_codes[c][:, cols].bitcast(FP8X4), rhs_scale=z_scales[c][:, cols], start=(part == 0), stop=(part == 1))
-            nc.scalar.copy(result[:, c, :], acc[:])
+        acc = {}
+
+        def second_product(c, part):
+            if part == 0:
+                acc[c] = psum.tile([P, CHUNK], F32, name="acc%d" % c, tag=("re0", "re1", "im0", "im1")[c])
+            cols = frames(part)
+            nc.tensor.matmul_mx(out=acc[c][:], lhsT=v_codes[part][:].bitcast(FP8X4), lhsT_scale=v_scales[part][:],
+                                rhs=z_codes[c][:, cols].bitcast(FP8X4), rhs_scale=z_scales[c][:, cols], start=(part == 0), stop=(part == 1))
+
+        def store(c):
+            nc.scalar.copy(result[:, c, :], acc[c][:])
             nc.sync.dma_start(out=out[:, frames(c)], in_=result[:, c, :])
 
         for step in (square_im, add, find_least):
@@ -277,7 +285,7 @@ def tile_picked_ysubtr_sub_p_kernel(tc, x_words, x_scales, wc, ws, unit, vc, vs,
         for planes in plane_pairs:
             nc.scalar.activation(im_sq[last, 0][:, planes, :], im[last][:, planes, :], ACT.Square)
         add(1)
-        quantize_v(1, vs_bf)
+        quantize_v(1, vs_first, v_halves[0])
         find_least(1)
         power[turned, 0] = psum.tile([P, PACK, CHUNK], F32, name="turned_power", tag="im%d" % turned)
         for part in range(2):
@@ -328,16 +336,26 @@ def tile_picked_ysubtr_sub_p_kernel(tc, x_words, x_scales, wc, ws, unit, vc, vs,
         for step in (take_root, invert, form_gain):
             for cols in (early, late):
                 step(last, every_plane, cols)
-        for c in (1, turned):
-            quantize_z(c, 0, CHUNK)
-            quantize_z(c, CHUNK, 2 * CHUNK)
-            for cols in ((every_frame,) if c == 1 else (early, late)):
-                weigh(c + 1, 0, cols)
-                weigh(c + 1, 1, cols)
-        second_product(0)
-        second_product(1)
-        second_product(2)
+        quantize_z(1, 0, CHUNK)
+        quantize_z(1, CHUNK, 2 * CHUNK)
+        vs_second = sign_and_round(nc.gpsimd, 1, "z1", v_halves[1])
+        weigh(turned, 0)
+        weigh(turned, 1)
+        quantize_z(turned, 0, CHUNK)
+        quantize_z(turned, CHUNK, 2 * CHUNK)
+        quantize_v(1, vs_second, v_halves[1])
+        for part in range(2):
+            for c in range(last):
+                second_product(c, part)
+        weigh(last, 0, early)
+        weigh(last, 1, early)
+        weigh(last, 0, late)
+        weigh(last, 1, late)
         quantize_z(last, 0, CHUNK)
         quantize_z(last, CHUNK, CHUNK + CHUNK // 2)
         quantize_z(last, CHUNK + CHUNK // 2, 2 * CHUNK)
-        second_product(3)
+        for c in range(last):
+            store(c)
+        second_product(last, 0)
+        second_product(last, 1)
+        store(last)

@@ -145,17 +145,23 @@ def tile_picked_ysubtr_sub_p_kernel(tc, x_words, x_scales, wc, ws, unit, vc, vs,
 
         ws_codes = sb("ws_codes", [P, H], U32)
         ws_scales = sb("ws_scales", [P, H], U8)
-        ws_bf = [sb("ws_bf%d" % h, [P, PACK, WS_ROWS, PACK], BF16) for h in range(2)]
+        ws_bf = sb("ws_bf1", [P, PACK, P, PACK], BF16)
 
-        def quantize_ws(h, t):
-            cols = slice(t * P + h * WS_ROWS, t * P + (h + 1) * WS_ROWS)
-            nc.vector.quantize_mx(out=ws_codes[:, cols].bitcast(FP8X4), scales=ws_scales[:, cols], in_=ws_bf[h][:, t, :, :].rearrange("p m j -> p (m j)"))
+        def quantize_ws(t, rows):
+            cols = slice(t * P + rows.start, t * P + rows.stop)
+            nc.vector.quantize_mx(out=ws_codes[:, cols].bitcast(FP8X4), scales=ws_scales[:, cols], in_=ws_bf[:, t, rows, :].rearrange("p m j -> p (m j)"))
 
-        for h in range(2):
-            for planes in plane_pairs:
-                round_and_deal(nc.vector.tensor_copy, by_slots(ws_raw[h][:])[:, :, :, planes], ws_bf[h][:, planes, :, :])
-            for t in range(PACK):
-                quantize_ws(h, t)
+        row_halves = (slice(0, WS_ROWS), slice(WS_ROWS, P))
+        for planes in reversed(plane_pairs):
+            round_and_deal(nc.vector.tensor_copy, by_slots(ws_raw[0][:])[:, :, :, planes], ws_bf[:, planes, row_halves[0], :])
+        for t in range(PAIR, PACK):
+            quantize_ws(t, row_halves[0])
+        for planes in plane_pairs:
+            round_and_deal(nc.vector.tensor_copy, by_slots(ws_raw[1][:])[:, :, :, planes], ws_bf[:, planes, row_halves[1], :])
+        for t in range(PAIR):
+            quantize_ws(t, slice(0, P))
+        for t in range(PAIR, PACK):
+            quantize_ws(t, row_halves[1])
 
         im = {c: first_product("im", ws_codes, ws_scales, c) for c in range(turned)}
         im_turned = turned_product("im", ws_codes, ws_scales, turned)

from contextlib import ExitStack

import concourse.mybir as mybir
from concourse.masks import make_identity

F32 = mybir.dt.float32
BF16 = mybir.dt.bfloat16
I32 = mybir.dt.int32
U32 = mybir.dt.uint32
U16 = mybir.dt.uint16
U8 = mybir.dt.uint8
FP8X4 = mybir.dt.float8_e4m3fn_x4
ALU = mybir.AluOpType
ACT = mybir.ActivationFunctionType
AX = mybir.AxisListType

K, T, S, D, H, N = 512, 2048, 512, 8, 512, 128
FLOPS = 2 * (2 * K * H * S + 2 * H * N * S)

P = 128
PACK = 4
PAIR = 2
QUADRANT = 32
CHUNK = 128
CHUNKS = S // CHUNK
RUNS = CHUNK // D
LIST_ROWS = 16
WS_COLS = H // 2
WS_ROWS = P // 2
SCALAR_ROWS = 80

POWER_OFFSET, NOISE_FACTOR, GAIN_FLOOR = 0.05, 1.5, 0.02
TOP = 1.02
CEILING = 2.0 ** 90
TURNED = 2
TINY = 2.0 ** -80


def tile_picked_ysubtr_sub_p_kernel(tc, x_words, x_scales, wc, ws, unit, vc, vs, offs, out):
    nc = tc.nc
    with ExitStack() as ctx:
        keep = ctx.enter_context(tc.tile_pool(name="keep", bufs=1))
        psum = ctx.enter_context(tc.psum_pool(name="psum", bufs=1))

        def sb(name, shape, dtype, tag=None):
            return keep.tile(shape, dtype, name=name, tag=tag or name, align_bytes=64)

        def planes_tile(name, tag=None):
            return sb(name, [P, PACK, CHUNK], F32, tag=tag)

        def by_runs(ap):
            return ap.rearrange("p t (v d) -> p (t v) d", d=D)

        plane_pairs = (slice(0, PAIR), slice(PAIR, PACK))

        offsets = keep.tile([P, S // LIST_ROWS], U16, name="offsets")
        wc_raw = sb("wc_raw", [P, PACK, H], F32)
        nc.sync.dma_start(out=wc_raw[:], in_=wc.rearrange("(p j) c -> p j c", j=PACK))
        nc.sync.dma_start(offsets[:], offs)
        bytes_all = sb("bytes_all", [P, T], U8)
        nc.vector.memset(bytes_all[:].bitcast(I32), 0)
        for r in range(PACK):
            nc.sync.dma_start(out=bytes_all[r:P:QUADRANT, :].bitcast(I32), in_=x_scales[0, r:K // 32:PACK, :].bitcast(I32))
        words_all = sb("words_all", [P, T], I32)
        nc.sync.dma_start(out=words_all[:], in_=x_words[0].rearrange("p n t -> p (n t)").bitcast(I32))
        unit_planes = sb("unit_planes", [P, PACK], F32)
        nc.sync.dma_start(out=unit_planes[:], in_=unit.rearrange("(p t) o -> p (t o)", t=PACK))
        ws_raw = []
        for h in range(2):
            raw = sb("ws_raw%d" % h, [P, PACK, WS_COLS], F32)
            nc.sync.dma_start(out=raw[:], in_=ws.rearrange("(p j) c -> p j c", j=PACK)[:, :, h * WS_COLS:(h + 1) * WS_COLS])
            ws_raw.append(raw)
        v_raw = []
        for part, v in enumerate((vc, vs)):
            raw = sb("v_raw%d" % part, [P, PACK, N], F32)
            nc.sync.dma_start(out=raw[:], in_=v.rearrange("(p t) m -> p t m", t=PACK))
            v_raw.append(raw)

        huge = sb("huge", [P, 1], F32)
        nc.vector.memset(huge[:], 2.0 ** 80)
        guard = sb("guard", [P, 1], F32)
        nc.scalar.activation(guard[:], huge[:], ACT.Abs_reciprocal_sqrt)

        identity = sb("identity", [P, P], F32)
        make_identity(nc, identity[:])

        def round_and_deal(copy, raw, grouped):
            copy(grouped.rearrange("p t m j -> p m j t"), raw.rearrange("p j m t -> p m j t"))

        def by_slots(raw):
            return raw.rearrange("p j (m t) -> p j m t", t=PACK)

        wc_bf = sb("wc_bf", [P, PACK, P, PACK], BF16)
        round_and_deal(nc.scalar.copy, by_slots(wc_raw[:])[:, :, 0:SCALAR_ROWS, :], wc_bf[:, :, 0:SCALAR_ROWS, :])
        x_bytes = sb("x_bytes", [P, S], U8)
        nc.vector.tensor_copy(x_bytes[:], bytes_all[:].indirect(offsets[:]))
        round_and_deal(nc.vector.tensor_copy, by_slots(wc_raw[:])[:, :, SCALAR_ROWS:P, :], wc_bf[:, :, SCALAR_ROWS:P, :])
        wc_codes = sb("wc_codes", [P, H], U32, tag="bytes_all")
        wc_scales = sb("wc_scales", [P, H], U8)
        nc.vector.quantize_mx(out=wc_codes[:].bitcast(FP8X4), scales=wc_scales[:], in_=wc_bf[:].rearrange("p t m j -> p (t m j)"))

        u2 = sb("u2", [P, PACK], F32)
        nc.scalar.activation(u2[:], unit_planes[:], ACT.Square)
        u_sign = sb("u_sign", [P, PACK], F32)
        nc.scalar.activation(u_sign[:], unit_planes[:], ACT.Sign)
        u_root = sb("u_root", [P, PACK], F32)
        nc.scalar.activation(u_root[:], u2[:], ACT.Abs_reciprocal_sqrt, scale=TOP, bias=TINY)
        u_inv = sb("u_inv", [P, PACK], F32)
        nc.scalar.activation(u_inv[:], u_root[:], ACT.Square)

        x_codes = []
        for first, count in ((0, 1), (1, 1), (2, 2)):
            picked = sb("x_codes%d" % first, [P, count * CHUNK], U32)
            cols = slice(first * CHUNK // LIST_ROWS, (first + count) * CHUNK // LIST_ROWS)
            nc.vector.tensor_copy(picked[:], words_all[:].bitcast(U32).indirect(offsets[:, cols]))
            x_codes.extend(picked[:, i * CHUNK:(i + 1) * CHUNK].bitcast(FP8X4) for i in range(count))

        def frames(c):
            return slice(c * CHUNK, (c + 1) * CHUNK)

        def turned_product(name, codes, scales, c):
            bank = psum.tile([P, H], F32, name="%s_turned" % name, tag="%s%d" % (name, c))
            nc.tensor.matmul_mx(out=bank[:], lhsT=x_codes[c], lhsT_scale=x_bytes[:, frames(c)],
                                rhs=codes[:].bitcast(FP8X4), rhs_scale=scales[:], start=True, stop=True)
            return bank

        def first_product(name, codes, scales, c, tag=None):
            bank = psum.tile([P, PACK, CHUNK], F32, name="%s%d" % (name, c), tag=tag or "%s%d" % (name, c))
            for t in range(PACK):
                plane = slice(t * P, (t + 1) * P)
                nc.tensor.matmul_mx(out=bank[:, t, :], lhsT=codes[:, plane].bitcast(FP8X4), lhsT_scale=scales[:, plane],
                                    rhs=x_codes[c], rhs_scale=x_bytes[:, frames(c)], start=True, stop=True)
            return bank

        last = CHUNKS - 1
        turned = TURNED
        plain = [c for c in range(CHUNKS) if c != turned]
        re = {c: first_product("re", wc_codes, wc_scales, c) for c in plain}
        re_turned = turned_product("re", wc_codes, wc_scales, turned)
        re_sq = {c: planes_tile("re_sq%d" % c) for c in plain}
        for c in plain:
            nc.scalar.activation(re_sq[c][:], re[c][:], ACT.Square)
        turned_sq = [sb("turned_sq%d" % part, [P, H], F32) for part in range(2)]
        nc.scalar.activation(turned_sq[0][:], re_turned[:], ACT.Square)

        ws_codes = sb("ws_codes", [P, H], U32)
        ws_scales = sb("ws_scales", [P, H], U8)
        ws_bf = sb("ws_bf1", [P, PACK, P, PACK], BF16)

        def quantize_ws(t, rows):
            cols = slice(t * P + rows.start, t * P + rows.stop)
            nc.vector.quantize_mx(out=ws_codes[:, cols].bitcast(FP8X4), scales=ws_scales[:, cols], in_=ws_bf[:, t, rows, :].rearrange("p m j -> p (m j)"))

        row_halves = (slice(0, WS_ROWS), slice(WS_ROWS, P))
        for planes in reversed(plane_pairs):
            round_and_deal(nc.vector.tensor_copy, by_slots(ws_raw[0][:])[:, :, :, planes], ws_bf[:, planes, row_halves[0], :])
        for t in range(PAIR, PACK):
            quantize_ws(t, row_halves[0])
        for planes in plane_pairs:
            round_and_deal(nc.vector.tensor_copy, by_slots(ws_raw[1][:])[:, :, :, planes], ws_bf[:, planes, row_halves[1], :])
        for t in range(PAIR):
            quantize_ws(t, slice(0, P))
        for t in range(PAIR, PACK):
            quantize_ws(t, row_halves[1])

        im = {c: first_product("im", ws_codes, ws_scales, c) for c in range(turned)}
        im_turned = turned_product("im", ws_codes, ws_scales, turned)
        im[last] = first_product("im", ws_codes, ws_scales, last)
        im[turned] = first_product("im", ws_codes, ws_scales, turned, tag="re%d" % turned)

        v_codes, v_scales = [], []

        def sign_and_round(engine, part, tag, cols=slice(0, N)):
            count = cols.stop - cols.start
            v_bf = sb("v_bf%d_%d" % (part, cols.start), [P, count, PACK], BF16, tag=tag)
            engine.tensor_tensor(v_bf[:].rearrange("p (b i) t -> p b t i", i=PACK), v_raw[part][:, :, cols].rearrange("p t (b i) -> p b t i", i=PACK),
                                 u_sign[:].unsqueeze(1).unsqueeze(3).to_broadcast([P, count // PACK, PACK, PACK]), ALU.mult)
            return v_bf

        for part in range(2):
            v_codes.append(sb("v_codes%d" % part, [P, N], U32))
            v_scales.append(sb("v_scales%d" % part, [P, N], U8))

        def quantize_v(part, v_bf, cols=slice(0, N)):
            nc.vector.quantize_mx(out=v_codes[part][:, cols].bitcast(FP8X4), scales=v_scales[part][:, cols], in_=v_bf[:].rearrange("p m t -> p (m t)"))

        vc_bf = sign_and_round(nc.vector, 0, tag="ws_bf1")
        quantize_v(0, vc_bf)
        v_halves = (slice(0, N // 2), slice(N // 2, N))
        vs_first = sign_and_round(nc.vector, 1, "ws_raw1", v_halves[0])

        low, high = plane_pairs
        every_plane = slice(0, PACK)
        every_frame = slice(0, CHUNK)
        early, late = slice(0, CHUNK // 2), slice(CHUNK // 2, CHUNK)

        im_sq, power, least, noise_root, noise_inv = {}, {}, {}, {}, {}
        ratio = {}
        excess = [planes_tile("excess%d" % c) for c in range(CHUNKS)]
        root = {}
        gain = [planes_tile("gain%d" % c) for c in range(CHUNKS)]
        inverse = {}
        z = [sb("z%d" % c, [P, 2, CHUNK, PACK], BF16) for c in range(CHUNKS)]
        z_codes, z_scales = {}, {}

        def width(planes):
            return planes.stop - planes.start

        def piece(store, name, c, planes, columns, tag):
            store[c, planes.start] = sb("%s%d_%d" % (name, c, planes.start), [P, width(planes), columns], F32, tag=tag)
            return store[c, planes.start]

        def square_im(c, planes=every_plane, tag=None):
            nc.scalar.activation(piece(im_sq, "im_sq", c, planes, CHUNK, tag)[:], im[c][:, planes, :], ACT.Square)

        def add(c, planes=every_plane, tag=None):
            nc.vector.tensor_tensor(piece(power, "power", c, planes, CHUNK, tag)[:], re_sq[c][:, planes, :], im_sq[c, planes.start][:], ALU.add)

        def find_least(c, planes=every_plane, tag=None):
            nc.vector.tensor_reduce(piece(least, "least", c, planes, RUNS, tag)[:].rearrange("p t v -> p (t v)"), by_runs(power[c, planes.start][:]), AX.X, ALU.min)

        def noise_first(c, planes=every_plane, tag=None):
            nc.scalar.activation(piece(noise_root, "noise_root", c, planes, RUNS, tag)[:], least[c, planes.start][:], ACT.Abs_reciprocal_sqrt,
                                 scale=NOISE_FACTOR / TOP, bias=guard[:])

        def noise_second(c, planes=every_plane):
            nc.scalar.activation(piece(noise_inv, "noise_inv", c, planes, RUNS, None)[:], noise_root[c, planes.start][:], ACT.Square)

        def form_ratio(c, planes=every_plane, whole=False):
            source, factor = (power[c, 0][:, planes, :], noise_inv[c, 0][:, planes, :]) if whole else (power[c, planes.start][:], noise_inv[c, planes.start][:])
            nc.vector.scalar_tensor_tensor(by_runs(piece(ratio, "ratio", c, planes, CHUNK, None)[:]), by_runs(source), POWER_OFFSET,
                                           factor.rearrange("p t v -> p (t v)").unsqueeze(2).to_broadcast([P, width(planes) * RUNS, D]), ALU.add, ALU.mult)

        def clip(engine, c, planes=every_plane):
            engine.tensor_scalar(excess[c][:, planes, :], ratio[c, planes.start][:], CEILING, TOP, ALU.min, ALU.max)

        def clip_on_scalar(c, planes):
            nc.scalar.activation(excess[c][:, planes, :], ratio[c, planes.start][:], ACT.Relu, bias=-TOP)

        def take_root(c, planes, cols=every_frame, shift=-1.0, tag=None):
            key = c, planes.start, cols.start
            root[key] = sb("root%d_%d_%d" % key, [P, width(planes), width(cols)], F32, tag=tag)
            nc.scalar.activation(root[key][:], excess[c][:, planes, cols], ACT.Abs_reciprocal_sqrt, bias=shift)

        def invert(c, planes, cols=every_frame):
            key = c, planes.start, cols.start
            inverse[key] = sb("inverse%d_%d_%d" % key, [P, width(planes), width(cols)], F32)
            nc.scalar.activation(inverse[key][:], root[key][:], ACT.Square)

        def form_gain(c, planes, cols=every_frame):
            for t in range(planes.start, planes.stop):
                nc.scalar.activation(gain[c][:, t, cols], inverse[c, planes.start, cols.start][:, t - planes.start, :], ACT.Abs_reciprocal_sqrt,
                                     scale=u_inv[:, t:t + 1], bias=u_inv[:, t:t + 1])

        def weigh(c, part, cols=slice(0, CHUNK)):
            bank = (re, im)[part][c]
            nc.vector.tensor_tensor(z[c][:, part, cols, :].rearrange("p (b e) t -> p b t e", e=PAIR), bank[:, :, cols].rearrange("p t (b e) -> p b t e", e=PAIR),
                                    gain[c][:, :, cols].rearrange("p t (b e) -> p b t e", e=PAIR), ALU.mult)

        def quantize_z(c, first=0, end=2 * CHUNK, tag=None):
            if c not in z_codes:
                z_codes[c] = sb("z_codes%d" % c, [P, 2 * CHUNK], U32, tag=tag)
                z_scales[c] = sb("z_scales%d" % c, [P, 2 * CHUNK], U8)
            nc.vector.quantize_mx(out=z_codes[c][:, first:end].bitcast(FP8X4), scales=z_scales[c][:, first:end],
                                  in_=z[c][:].rearrange("p s n t -> p (s n t)")[:, PACK * first:PACK * end])

        result = sb("result", [P, CHUNKS, CHUNK], F32)

        acc = {}

        def second_product(c, part):
            if part == 0:
                acc[c] = psum.tile([P, CHUNK], F32, name="acc%d" % c, tag=("re0", "re1", "im0", "im1")[c])
            cols = frames(part)
            nc.tensor.matmul_mx(out=acc[c][:], lhsT=v_codes[part][:].bitcast(FP8X4), lhsT_scale=v_scales[part][:],
                                rhs=z_codes[c][:, cols].bitcast(FP8X4), rhs_scale=z_scales[c][:, cols], start=(part == 0), stop=(part == 1))

        def store(c):
            nc.scalar.copy(result[:, c, :], acc[c][:])
            nc.sync.dma_start(out=out[:, frames(c)], in_=result[:, c, :])

        for step in (square_im, add, find_least):
            for planes in plane_pairs:
                step(0, planes)
        square_im(1)
        nc.scalar.activation(turned_sq[1][:], im_turned[:], ACT.Square)
        for step in (noise_first, noise_second):
            for planes in plane_pairs:
                step(0, planes)
        im_sq[last, 0] = planes_tile("im_sq_last", tag="least0_0")
        for planes in plane_pairs:
            nc.scalar.activation(im_sq[last, 0][:, planes, :], im[last][:, planes, :], ACT.Square)
        add(1)
        quantize_v(1, vs_first, v_halves[0])
        find_least(1)
        power[turned, 0] = psum.tile([P, PACK, CHUNK], F32, name="turned_power", tag="im%d" % turned)
        for part in range(2):
            for t in range(PACK):
                nc.tensor.matmul(power[turned, 0][:, t, :], turned_sq[part][:, t * P:(t + 1) * P], identity[:], is_transpose=True,
                                 start=(part, t) == (0, 0), stop=(part, t) == (1, PACK - 1))
        for step in (form_ratio, clip_on_scalar):
            for planes in plane_pairs:
                step(0, planes)
        find_least(turned, tag="noise_inv0_0")
        power[last, 0] = planes_tile("power_last", tag="power0_0")
        nc.gpsimd.tensor_tensor(power[last, 0][:, low, :], re_sq[last][:, low, :], im_sq[last, 0][:, low, :], ALU.add)
        nc.vector.tensor_tensor(power[last, 0][:, high, :], re_sq[last][:, high, :], im_sq[last, 0][:, high, :], ALU.add)
        noise_first(1)
        noise_second(1)
        take_root(0, low, shift=GAIN_FLOOR, tag="noise_inv0_2")
        take_root(0, high, shift=GAIN_FLOOR)
        noise_first(turned)
        invert(0, low)
        noise_second(turned)
        invert(0, high)
        form_ratio(1)
        find_least(last)
        clip(nc.vector, 1)
        for planes in plane_pairs:
            form_gain(0, planes)
        form_ratio(turned)
        re[turned] = first_product("re", wc_codes, wc_scales, turned, tag="im%d" % turned)
        clip(nc.gpsimd, turned)
        take_root(1, low)
        take_root(1, high)
        noise_first(last)
        invert(1, low)
        noise_second(last)
        invert(1, high)
        weigh(0, 0)
        weigh(0, 1)
        for planes in plane_pairs:
            form_gain(1, planes)
        form_ratio(last)
        clip(nc.gpsimd, last)
        for step in (take_root, invert, form_gain):
            for planes in plane_pairs:
                step(turned, planes)
        quantize_z(0)
        weigh(1, 0)
        weigh(1, 1)
        for step in (take_root, invert, form_gain):
            for cols in (early, late):
                step(last, every_plane, cols)
        quantize_z(1, 0, CHUNK)
        quantize_z(1, CHUNK, 2 * CHUNK)
        vs_second = sign_and_round(nc.gpsimd, 1, "z1", v_halves[1])
        weigh(turned, 0)
        weigh(turned, 1)
        quantize_z(turned, 0, CHUNK)
        quantize_z(turned, CHUNK, 2 * CHUNK)
        quantize_v(1, vs_second, v_halves[1])
        for part in range(2):
            for c in range(last):
                second_product(c, part)
        weigh(last, 0, early)
        weigh(last, 1, early)
        weigh(last, 0, late)
        weigh(last, 1, late)
        quantize_z(last, 0, CHUNK)
        quantize_z(last, CHUNK, CHUNK + CHUNK // 2)
        quantize_z(last, CHUNK + CHUNK // 2, 2 * CHUNK)
        for c in range(last):
            store(c)
        second_product(last, 0)
        second_product(last, 1)
        store(last)
